import numpy as np, ml_dtypes
CORES = [48,51,52,55]
N = 4
BF = ml_dtypes.bfloat16
W, K, I, M, VIS = 4096, 256, 16, 256, 6
def mark(u, a):
    return ((u * u >> 5) + 37 * u + a) & (M - 1)
def parts(rng):
    pop = rng.integers(0, M, (N, 8, 16))
    nm = np.where(rng.random((N, 8, W)) < 0.5, np.take_along_axis(pop, rng.integers(0, 16, (N, 8, W)), 2), rng.integers(0, M, (N, 8, W)))
    vo = rng.integers(0, 256, (N, 8, 16, W)); vn = rng.integers(0, 256, (N, 8, 16, W)); x = rng.integers(0, 256, (N, 8, 16, M))
    c = rng.integers(0, W, (N, 8, K)); s = 2 * rng.integers(0, 512, (N, 8, K)) + 1
    z = np.minimum(rng.integers(0, 160, (N, 8, 1, K)) + rng.integers(0, 64, (N, 8, 16, K)), 255)
    return nm, vo, vn, x, c, s, z
def bf(a):
    return np.ascontiguousarray(a.reshape(N, 128, -1)).astype(np.float32).astype(BF)
def pack(nm, vo, vn, x, c, s, z):
    return {"nm": nm.astype(np.int32), "vo": bf(vo), "vn": bf(vn), "xo": bf(x), "c0": c.astype(np.int32), "s0": s.astype(np.int32), "z0": bf(z)}
def share16(rng, S):
    S = np.asarray(S); b = S >> 4
    v = b[..., None] + (np.arange(16) < (S & 15)[..., None])
    d = (rng.random(S.shape + (8,)) * (np.minimum(b, np.maximum(254 - b, 0))[..., None] + 1)).astype(np.int64)
    v = v + np.concatenate([d, -d], axis=-1)
    return np.take_along_axis(v, np.argsort(rng.random(v.shape), axis=-1), -1)
def sums(rng, lo, hi):
    a = np.arange(lo, hi + 1); h = mark(a, 0); o = np.argsort(h + rng.random(len(a)))
    return a[o[np.minimum(np.searchsorted(h[o], np.arange(M)), len(a) - 1)]]
def setup_inputs(rng):
    return pack(*parts(rng))
def setup_inputs_spread(rng):
    nm, vo, vn, x, c, s, z = parts(rng)
    def sized(n):
        return np.minimum((np.exp2(8 * rng.random((N, 8, 1, n))) * rng.random((N, 8, 16, n))).astype(np.int64), 255)
    nm = np.minimum((M * rng.random((N, 8, W)) ** 3).astype(np.int64), M - 1)
    s = 2 * np.exp2(9 * rng.random((N, 8, K))).astype(np.int64) - 1
    return pack(nm, sized(W), sized(W), sized(M), c, s, sized(K))
def setup_inputs_ends(rng):
    nm, vo, vn, x, c, s, z = parts(rng)
    def ends(n):
        return 255 * np.where(rng.random((N, 8, 1, n)) < 0.5, rng.integers(0, 2, (N, 8, 1, n)), rng.integers(0, 2, (N, 8, 16, n)))
    vo, vn, x, z = ends(W), ends(W), ends(M), ends(K)
    nm = np.where(rng.random(nm.shape) < 0.7, (M - 1) * rng.integers(0, 2, nm.shape), nm)
    c = np.where(rng.random(c.shape) < 0.7, (W - 1) * rng.integers(0, 2, c.shape), c)
    s = np.where(rng.random(s.shape) < 0.7, 1 + 1022 * rng.integers(0, 2, s.shape), s)
    up = rng.integers(0, 2, (N, 8, 1))
    nm[..., W - 1] = M - 1; nm[..., 0] = 0; nm[..., 1:I - 3] = (M - 1) * rng.integers(0, 2, (N, 8, I - 4)); nm[..., I - 3] = 0; nm[..., I - 2] = M - 1
    vo[..., W - 1] = 255 * up; vn[..., I - 2] = 255 * (1 - up); vo[..., 0] = 255 * (1 - up); vn[..., I - 3] = 255 * up
    h = W // 2; vo[..., h:h + I] = 255 * up[..., None]; vn[..., h:h + I] = 255 * up[..., None]
    for k, a in ((0, W - 1), (1, h), (2, h), (K - 1, W - 1)):
        c[..., k] = a; s[..., k] = 1
    z[..., 1] = 0; z[..., 2] = 255; z[..., K - 1] = 255
    return pack(nm, vo, vn, x, c, s, z)
def setup_inputs_corners(rng):
    nm, vo, vn, x, c, s, z = parts(rng); pl = np.arange(W)
    ty = (np.arange(8)[None, :] + 3 * np.arange(N)[:, None] + int(rng.integers(0, 8))) % 8
    first = int(rng.integers(0, N)); ty[(first + 1) % N, int(np.argmin(ty[first]))] = 0
    for q in range(N):
        for g in range(8):
            t = int(ty[q, g])
            if t == 0:
                vo[q, g] = 0; vn[q, g] = rng.integers(0, 4, (16, W)); vn[q, g][:, I - 1::I] = share16(rng, sums(rng, 64, 4080)[rng.permutation(M)]).T
                c[q, g] = I * rng.permutation(np.arange(K) % M); s[q, g] = 1; z[q, g] = 0
            elif t == 1:
                vo[q, g] = vo[q, g] >> 1; vn[q, g] = vn[q, g] >> 1; z[q, g] = 255
            elif t == 2: nm[q, g] = (M - 1) * int(rng.integers(0, 2))
            elif t == 3: nm[q, g] = pl & (M - 1)
            elif t == 4:
                nm[q, g] = np.where(pl % I == I - 1, pl - (I - 1), pl) & (M - 1); c[q, g] = I * rng.integers(0, M, K); s[q, g] = 1
            elif t == 5:
                v = rng.integers(0, 256, (16, 1)); vo[q, g] = v; vn[q, g] = v
                z[q, g] = np.argsort(np.argsort(rng.random((16, K)), axis=0), axis=0) >= rng.choice(np.array([0, 8, 9, 16]), K)
            elif t == 6: x[q, g] = 255 * rng.integers(0, 2, (16, M))
            else:
                c[q, g] = rng.choice(np.array([0, W - 2, W - 1, W - I, W - I + 1]), K); s[q, g] = rng.choice(np.array([1, 3, 1021, 1023]), K)
    return pack(nm, vo, vn, x, c, s, z)
def setup_inputs_crowd(rng):
    nm, vo, vn, x, c, s, z = parts(rng); pl = np.arange(W); vo[:] = 0; z[:] = 0
    for g in range(8):
        for q in range(N):
            if q == 0 or g & 1:
                sm = sums(rng, 960, 3200); pick = sm[2 * rng.integers(0, M // 2, 2) + ((g >> 1) & 1)]
            S = np.full(W, int(pick[0]))
            if g >= 6:
                S = np.where(pl < W // 2, int(pick[0]), int(pick[1])); s[q, g] = 1
            vn[q, g] = share16(rng, S).T
            if g & 3: z[q, g, :, (0, K - 1, int(rng.integers(0, K)))[(g & 3) - 1]] = 255
    v = rng.integers(0, 256, (16, 1)); vo[:, 0] = v; vn[:, 0] = v; nm[:, 0] = np.maximum(nm[:, 0], 1)
    return pack(nm, vo, vn, x, c, s, z)
def setup_inputs_ties(rng):
    nm, vo, vn, x, c, s, z = parts(rng)
    vo[:, ::2] = 85 * rng.integers(0, 4, (N, 4, 16, W)); vn[:, ::2] = 85 * rng.integers(0, 4, (N, 4, 16, W))
    z[:, ::2] = np.minimum(85 * rng.integers(0, 4, (N, 4, 16, K)) + rng.integers(0, 2, (N, 4, 16, K)), 255)
    for q in range(N):
        for g in (1, 3, 5, 7):
            hi = int(rng.integers(1600, 3201)); lo = hi if g > 4 else hi - int(rng.integers(1, 400))
            v1 = share16(rng, hi); v2 = share16(rng, lo); ix = np.argsort(rng.random((16, W)), axis=0)
            vo[q, g] = 0; vn[q, g] = np.where(rng.random(W) < 0.3, v1[ix], v2[ix])
            a = int(np.sort(v1)[7]); b = int(np.sort(v2)[7])
            z[q, g] = rng.choice(np.array([a, a + 1, b, b + 1]), K)
    return pack(nm, vo, vn, x, c, s, z)
def check_inputs(d):
    bad = []
    for k, lo, hi in (("nm", 0, M - 1), ("c0", 0, W - 1), ("s0", 1, 1023), ("vo", 0, 255), ("vn", 0, 255), ("xo", 0, 255), ("z0", 0, 255)):
        v = np.asarray(d[k]).astype(np.float64)
        if not np.all((v >= lo) & (v <= hi)): bad.append("range of " + k)
        elif not np.all(v == np.floor(v)): bad.append("whole numbers in " + k)
    if not np.all((np.asarray(d["s0"]).astype(np.int64) & 1) == 1): bad.append("odd numbers in s0")
    return bad
def reference(nm, vo, vn, xo, c0, s0, z0):
    name = nm.astype(np.int64)
    O = vo.astype(np.float32).astype(np.int32).reshape(N, 8, 16, W); V = vn.astype(np.float32).astype(np.int32).reshape(N, 8, 16, W)
    X = xo.astype(np.float32).astype(np.int32).reshape(N, 8, 16, M); z = z0.astype(np.float32).astype(np.int32).reshape(N, 8, 16, K)
    c = c0.astype(np.int64); s = s0.astype(np.int64); A = np.zeros((N, 8, K), np.int64)
    row = np.arange(I); rule = np.arange(K); obj = np.arange(M); odd = (obj & 1) == 1
    for t in range(VIS):
        e = (c[..., None] + s[..., None] * row) & (W - 1)
        n = np.take_along_axis(name, e.reshape(N, 8, K * I), 2).reshape(N, 8, K, I)
        eq = n[..., :, None] == n[..., None, :]
        head = np.argmax(eq, axis=-1) == row; last = I - 1 - np.argmax(eq[..., ::-1], axis=-1)
        el = np.take_along_axis(e, last, 3)
        D = np.take_along_axis(V, el.reshape(N, 8, 1, K * I), 3) - np.take_along_axis(O, e.reshape(N, 8, 1, K * I), 3)
        D = D.reshape(N, 8, 16, K, I); S = np.add.reduce(np.abs(D), axis=2).astype(np.int64)
        f = np.argmax(np.where(head, S, -1), axis=-1)
        df = np.take_along_axis(D, f[:, :, None, :, None], 4)[..., 0]; B = np.abs(df)
        u = np.take_along_axis(S, f[..., None], 3)[..., 0]
        fire = np.add.reduce((B >= z).astype(np.int64), axis=2) >= 9
        m = mark(u, A)
        low = np.full((N, 8, M), K)
        np.minimum.at(low, (np.arange(N)[:, None, None], np.arange(8)[None, :, None], m), np.where(fire, rule, K))
        act = fire & (np.take_along_axis(low, m, 2) == rule)
        has = low < K; dm = np.take_along_axis(df, np.minimum(low, K - 1)[:, :, None, :], 3)
        has = np.where(odd, np.roll(has, 1, axis=0), has); dm = np.where(odd, np.roll(dm, 1, axis=0), dm)
        hw = has[:, :, None, :]; X2 = np.where(hw, np.clip(X + dm, 0, 255), X); a, b = t * M, (t + 1) * M
        name[..., a:b] = np.where(has, obj, name[..., a:b]); O[..., a:b] = np.where(hw, X, O[..., a:b]); V[..., a:b] = np.where(hw, X2, V[..., a:b])
        X = X2
        c = np.where(act, c + I * s, c + s * (f + 1)) & (W - 1); s = np.where(act, 2 * (u & 511) + 1, s)
        z = np.where(act[:, :, None, :], (z + B) >> 1, np.maximum(z - 1, 0)); A = (fire & ~act).astype(np.int64)
        if t < VIS - 1:
            c, s, z, A = np.roll(c, 1, axis=0), np.roll(s, 1, axis=0), np.roll(z, 1, axis=0), np.roll(A, 1, axis=0)
    L = VIS * M
    return {"yn": name[..., :L].astype(np.float32), "yo": O[..., :L].reshape(N, 128, L).astype(np.float32).astype(BF), "yv": V[..., :L].reshape(N, 128, L).astype(np.float32).astype(BF),
            "yx": X.reshape(N, 128, M).astype(np.float32).astype(BF), "yc": c.astype(np.float32), "ys": s.astype(np.float32), "ya": A.astype(np.float32), "yz": z.reshape(N, 128, K).astype(np.float32).astype(BF)}

@@ -1,0 +1,620 @@
+import math
+from concourse.mybir import AluOpType as A, ActivationFunctionType as F
+
+VIS, NB = 6, 2
+SW, MW = 400, 144
+BF, FP, I3, U2 = "bfloat16", "float32", "int32", "uint16"
+SCRATCH = {}
+for _b in range(NB):
+    for _n, _w, _d in (("WN", 4096, BF), ("WO", 4096, BF), ("WV", 4096, BF), ("NG", 2048, BF), ("OG", 2048, BF),
+                       ("DD", 2048, BF), ("AD", 2048, BF), ("EQ", 1024, BF), ("ST", VIS * SW, FP), ("SO", VIS * SW, FP),
+                       ("EU", VIS * 128, U2), ("EO", VIS * 128, U2), ("ML", VIS * MW, BF), ("MO", VIS * MW, BF),
+                       ("CN", 512, BF), ("CA", 512, BF), ("CB", 512, BF), ("DF", 272, BF), ("LO", 256, BF),
+                       ("TF", 9 * 128, FP), ("TI", 12 * 128, I3), ("TB", 14 * 128, BF), ("TU", 256, U2),
+                       ("SF", 128, FP), ("SI", 128, I3), ("SB", 64, BF), ("ZB", 128, BF), ("CS", 128, I3), ("CF", 128, FP)):
+        SCRATCH["%s%d" % (_n, _b)] = ("sbuf", [128, _w], _d)
+    for _n in "ABCD":
+        SCRATCH["P%s%d" % (_n, _b)] = ("psum", [128, 512], FP)
+for _n, _w, _d in (("NI", 256, I3), ("NH", 256, BF), ("PI", 64, I3), ("PF", 128, FP), ("KB", 50 * 128, BF), ("KF", 9 * 128, FP),
+                   ("KS", 128, BF), ("OI", 80, FP), ("OU", 80, U2)):
+    SCRATCH[_n] = ("sbuf", [128, _w], _d)
+ENG = ("g", "pe", "dve", "act", "sp")
+NDS = 56
+SEMAPHORES = ["c_" + e for e in ENG] + ["d%d" % i for i in range(NDS)] + ["sent"] + \
+    ["r%d_%d_%d" % (m, b, t) for m in range(3) for b in range(NB) for t in range(VIS)]
+LN2 = math.log(2.0)
+TOP = 41.5
+WB = 2 * TOP / 64
+HOP, GC, CY, PC = 0.12, 1.6, 0.001, 0.00045
+NACT = 80
+LOOK = 0.05
+LEAD = 4.0
+VCH = 4
+
+
+class V:
+    pass
+
+
+def R(buf, c0, c1, step=1, p0=0, p1=128, pstep=1):
+    return (buf, c0, c1, step, p0, p1, pstep)
+
+
+def IND(win, off):
+    return ("ind", win, off)
+
+
+def n_of(r):
+    if r[0] == "ind":
+        return 16 * n_of(r[2])
+    return (r[2] - r[1] + r[3] - 1) // r[3]
+
+
+def two(r):
+    return SCRATCH[r[0]][2] in (BF, U2)
+
+
+def psum(r):
+    return r[0] in SCRATCH and SCRATCH[r[0]][0] == "psum"
+
+
+def build():
+    ops = []
+    bias = [0.0, 1000]
+
+    def add(eng, call, reads, writes, dur, **kw):
+        rd = []
+        for r in reads:
+            if isinstance(r, tuple):
+                rd += [r[1], r[2]] if r[0] == "ind" else [r]
+        o = dict(eng=eng, call=call, reads=rd, writes=list(writes), dur=dur, lat=0.0, sem=None, after=None, recv=None)
+        o["bias"], o["kind"] = bias[0], bias[1]
+        bias[1] += 1
+        o.update(kw)
+        ops.append(o)
+        return len(ops) - 1
+
+    def cost(out, ins, mul=1.0):
+        n = n_of(out)
+        if ins[0][0] == "ind":
+            return 0.06 + n * GC * CY
+        if mul == 1.0 and two(out) and all(two(i) for i in ins):
+            mul = 0.5
+        return 0.03 + max(64, n * mul) * CY
+
+    def ts(out, a, s1, o0, s2=None, o1=None):
+        return add("dve", ("ts", out, a, s1, s2, o0, o1), [a, s1, s2], [out], cost(out, [a]))
+
+    def tt(out, a, b, op):
+        m = 1.0 if (a[0] == "ind" or psum(a) or psum(b)) else 2.0
+        return add("dve", ("tt", out, a, b, op), [a, b], [out], cost(out, [a, b], m + 1e-9))
+
+    def cp(out, a, eng="dve"):
+        if eng == "act":
+            return act(out, a, F.Identity)
+        return add("dve", ("cp", out, a), [a], [out], cost(out, [a]))
+
+    def act(out, a, f, bias=0.0, scale=1.0, extra=0.0):
+        return add("act", ("act", out, a, f, bias, scale), [a, bias, scale], [out], 0.04 + extra + cost(out, [a], 1.0 + 1e-9))
+
+    def mm(lst):
+        d, rd, wr = 0.0, [], []
+        for (o, l, r, st, sp) in lst:
+            d += max(min(64, n_of(l)), n_of(r)) * (1 if two(l) else 4) * PC
+            rd += [l, r]
+            wr.append(o)
+        return add("pe", ("mm", lst), rd, wr, 0.03 + d)
+
+    def mset(out, v):
+        return add("dve", ("ms", out, v), [], [out], cost(out, [out]))
+
+    def iota(out, pat, base=0, cm=0):
+        return add("g", ("io", out, pat, base, cm), [], [out], 0.13 + 2 * n_of(out) * CY)
+
+    nds = [0]
+
+    def dma(q, out, a, kb, sem=None):
+        if sem is None:
+            sem = "d%d" % nds[0]
+            nds[0] += 1
+        rd = [a] if a[0] in SCRATCH else []
+        wr = [out] if out[0] in SCRATCH else []
+        return add(q, ("dma", out, a), rd, wr, 0.1 if q != "g" else 0.8, lat=1.8, sem=sem, kb=kb)
+
+    def newsem():
+        nds[0] += 1
+        return "d%d" % (nds[0] - 1)
+
+    def send(dst, src, sem):
+        i = add("g", ("rd", dst, src, sem), [src], [], 0.4, lat=1.6 + n_of(src) * (2 if two(src) else 4) * 0.0006, sem="sent")
+        add("none", None, [], [dst], 0.0, after=i, recv=sem)
+
+    PIc = lambda j, n=1: R("PI", j, j + n)
+    PFc = lambda j, n=1: R("PF", j, j + n)
+    K = lambda j, n=128: R("KB", 128 * j, 128 * j + n)
+    KF = lambda j, n=128: R("KF", 128 * j, 128 * j + n)
+    osem = {q: newsem() for q in ("sp", "act", "g")}
+
+    for b in range(NB):
+        for h in range(2):
+            for j, nme in enumerate(("c0", "s0")):
+                dma("act", R("CS%d" % b, 0, 128, 1, 8 * j + 4 * h, 8 * j + 4 * h + 4),
+                    R(nme, 128 * h, 128 * h + 128, 1, 4 * b, 4 * b + 4), 2)
+    dma("sp", R("NI", 0, 256), R("nm", 0, 4096, 1, 0, 8), 128)
+    seq = [len(ops) - 1]
+    for b in range(NB):
+        for c in range(4):
+            mset(R("WN%d" % b, 1024 * c, 1024 * c + 1024), 0.0)
+    cp(R("NH", 0, 256), R("NI", 0, 256))
+
+    def log(w, nme, b):
+        for h in range(2):
+            seq.append(dma("sp", R("%s%d" % (w, b), 0, 4096, 1, 64 * h, 64 * h + 64), R(nme, 0, 4096, 1, 64 * b, 64 * b + 64), 512))
+
+    log("WO", "vo", 0)
+    for b in range(NB):
+        for h in range(2):
+            seq.append(dma("sp", R("WN%d" % b, 0, 4096, 1, 64 * h, 64 * h + 64, 16), R("NH", 0, 256, 1, 64 * b, 64 * b + 64), 32))
+    for b in range(NB):
+        if b:
+            log("WO", "vo", b)
+        log("WV", "vn", b)
+        for h in range(2):
+            seq.append(dma("sp", R("ZB%d" % b, 0, 128, 1, 64 * h, 64 * h + 64), R("z0", 128 * h, 128 * h + 128, 1, 64 * b, 64 * b + 64), 16))
+            seq.append(dma("sp", R("CA%d" % b, 256, 512, 1, 64 * h, 64 * h + 64), R("xo", 0, 256, 1, 64 * b, 64 * b + 64), 32))
+    for a, e in zip(seq, seq[1:]):
+        ops[e]["behind"] = a
+
+    iota(PIc(0), [[0, 1]], 0, 1)
+    cP, ca, cg8, ch, cg, c64, ca8, ca7, cq, cr = range(10)
+    for j, (sh, mk) in enumerate(((0, 15), (4, 7), (6, 1), (4, 3), (0, 63), (3, 1), (0, 7), (5, 3), (4, 1))):
+        ts(PIc(1 + j), PIc(0), sh, A.arith_shift_right, mk, A.bitwise_and)
+    cp(PFc(0, 10), PIc(0, 10))
+    (cbase, cP15, cz, c16a, ch128, cnh, ctp, cty, cf00, cf01, cf10, cf11, cna8, ct1, ct2, ct3, cown) = range(10, 27)
+    IC, M16, G8, M64, G4 = K(0, 144), K(2), K(3), K(4), K(5)
+    ICn = K(0)
+    iota(M16, [[0, 8], [1, 16]])
+    iota(G8, [[1, 8], [0, 16]])
+    iota(IC, [[1, 144]])
+    RE, RS, I32, PM, D0 = KF(0), KF(1), KF(2), K(40), KF(4)
+    ts(PFc(cna8), PFc(ca8), -1.0, A.mult, 1.0, A.add)
+    ts(RS, G8, PFc(ca7), A.is_equal, PFc(ca8), A.mult)
+    ts(RE, G8, PFc(ca7), A.is_equal, PFc(cna8), A.mult)
+    ts(KF(5), M16, 1.0, A.mult)
+    tt(KF(5), KF(5), RS, A.mult)
+    tt(RE, RE, KF(5), A.add)
+    for b in range(NB):
+        s16 = lambda r: R(r[0], r[1], r[2], 1, 0, 16)
+        cp(s16(R("CF%d" % b, 0, 128)), s16(R("CS%d" % b, 0, 128)))
+        mm([(R("PC%d" % b, 0, 128), s16(RE), s16(R("CF%d" % b, 0, 128)), True, True),
+            (R("PC%d" % b, 128, 256), s16(RS), s16(R("CF%d" % b, 0, 128)), True, True)])
+        cp(R("TI%d" % b, 0, 128), R("PC%d" % b, 0, 128))
+        ts(R("TI%d" % b, 128, 256), R("TI%d" % b, 0, 128), 4095, A.bitwise_and)
+        cp(R("EU%d" % b, 0, 128), R("TI%d" % b, 128, 256))
+        cp(R("ST%d" % b, 136, 264), R("PC%d" % b, 128, 256), "act")
+        cp(R("ST%d" % b, 8, 136), R("ZB%d" % b, 0, 128), "act")
+        mset(R("ST%d" % b, 0, 8), 1792.0)
+        mset(R("DF%d" % b, 256, 272), 0.0)
+        iota(R("CN%d" % b, 256, 512), [[1, 256]])
+    J, I16, MA, RC = K(6, 144), K(8), K(9), K(10)
+    ts(PFc(cP15), PFc(cP), 15.0, A.add)
+    ts(PFc(cz), PFc(ca), 0.0, A.is_equal)
+    ts(J, IC, PFc(cP15), A.is_equal, PFc(cz), A.mult)
+    ts(I16, ICn, PFc(cP), A.is_equal)
+    tt(PFc(cbase), PFc(cP), PFc(ca), A.subtract)
+    tE, tL, inv, dl, wE = PFc(32, 8), PFc(40, 8), PFc(48, 8), PFc(56, 8), R("KS", 0, 8)
+    iota(PIc(16, 8), [[1, 8]], 1, 1)
+    iota(PIc(24, 8), [[-1, 8]], 15, 1)
+    ts(PIc(32, 16), PIc(16, 16), 15, A.bitwise_and)
+    ts(inv, PIc(40, 8), PFc(cbase), A.add)
+    ts(tE, PIc(32, 8), PFc(ca), A.min, PFc(cbase), A.add)
+    ts(tL, PIc(32, 8), PFc(ca), A.max, PFc(cbase), A.add)
+    tt(dl, tL, tE, A.subtract)
+    act(wE, dl, F.Exp, -60 * LN2, 8 * LN2, 1.5)
+    cp(PFc(72, 8), wE)
+    ts(PFc(79), PFc(79), PFc(cna8), A.mult)
+    DM = [K(12 + d) for d in range(8)]
+    WM = [K(20 + d) for d in range(8)]
+    PN = [K(28 + d) for d in range(8)]
+    for d in range(8):
+        ts(DM[d], ICn, PFc(48 + d), A.is_equal)
+        tt(DM[d], DM[d], I16, A.subtract)
+    for d in range(8):
+        ts(WM[d], ICn, PFc(32 + d), A.is_equal, PFc(72 + d), A.mult)
+    for d in range(8):
+        ts(PN[d], ICn, PFc(40 + d), A.is_equal, -131072.0, A.mult)
+    S32, NS1, PS1, NS2, C256, C16 = (R("KS", 16, 24), R("KS", 24, 32), R("KS", 32, 40), R("KS", 40, 48), R("KS", 48, 56), R("KS", 64, 80))
+    for r, v in ((S32, 32.0), (NS1, -1.0), (PS1, 1.0), (NS2, -2.0)):
+        ts(r, K(0, 8), PFc(cg8), A.is_equal, v, A.mult)
+    ts(C256, K(0, 8), 256.0, A.mult)
+    ts(C16, K(0, 16), 16.0, A.mult)
+    ts(D0, M16, 0.0, A.is_equal, -1000001.0, A.mult)
+    ts(D0, D0, 1.0, A.add)
+    ts(MA, M16, PFc(ca), A.is_equal)
+    ts(I32, ICn, PFc(cP), A.is_equal)
+    DC, D16, DK, J128, N4 = KF(6), KF(7), KF(8), K(48, 144), K(39)
+    act(DC, I32, F.Identity, 0.0, 7.5 - 0.000354)
+    act(D16, I32, F.Identity, 0.0, 16.0)
+    ts(PFc(27), PFc(ca), -1.0, A.mult, 16.0, A.add)
+    act(DK, I32, F.Identity, 0.0, PFc(27))
+    act(J128, J, F.Identity, 0.0, 128.0)
+    act(N4, I32, F.Identity, 0.0, 32.0)
+    ts(PFc(c16a), PFc(ca), 16.0, A.mult, 15.0, A.add)
+    ts(PFc(ch128), PFc(ch), 128.0, A.mult)
+    ts(RC, ICn, PFc(ch128), A.add)
+    ts(PFc(cnh), PFc(ch), -1.0, A.mult, 1.0, A.add)
+    O = lambda a, n: R("OI", a, a + n)
+    iota(O(0, 8), [[1, 8]])
+    iota(O(8, 8), [[16, 8]], 15)
+    iota(O(16, 16), [[1, 8], [0, 2]])
+    iota(O(32, 4), [[2, 4]], 8)
+    iota(O(36, 8), [[0, 2], [2, 4]])
+    iota(O(44, 2), [[2, 2]])
+    ts(O(32, 14), O(32, 14), PFc(ca8), A.add)
+    cp(R("OU", 0, 46), O(0, 46))
+    LB, LK, LOH, LU, LF = (R("OU", a, a + n) for a, n in ((0, 8), (8, 8), (16, 16), (32, 4), (36, 10)))
+    IOH, IU = K(36, 256), K(38, 64)
+    iota(IOH, [[0, 8], [1, 2], [2, 16]])
+    iota(IU, [[0, 8], [1, 8]])
+    ts(PFc(cown), PFc(c64), -WB, A.mult, TOP, A.add)
+    ts(PFc(ct1), PFc(ch), -300.0, A.mult)
+    tt(PFc(64), PFc(cown), PFc(ct1), A.add)
+    ts(PFc(65), PFc(c64), -WB, A.mult, PFc(ch), A.mult)
+    ts(PFc(65), PFc(65), TOP, A.add)
+    act(PFc(66, 2), PFc(64, 2), F.Exp)
+    iota(M64, [[0, 2], [1, 64]])
+    iota(G4, [[0, 2], [1, 4], [0, 16]])
+    SEL = [K(41), K(42)]
+    BO = [K(43), K(44)]
+    LY = [[K(45), K(46)], [K(47), K(11)]]
+    for h, fl in ((0, cnh), (1, ch)):
+        ts(SEL[h], M64, PFc(c64), A.is_equal, PFc(fl), A.mult)
+        ts(BO[h], G4, PFc(cg), A.is_equal, PFc(fl), A.mult)
+    ts(PFc(ct2), PFc(cr), 64.0, A.mult, PFc(ca), A.add)
+    ts(PFc(ctp), PFc(cq), 16.0, A.mult, PFc(ct2), A.add)
+    ts(PM, ICn, PFc(ctp), A.is_equal)
+    ts(PFc(ct3), PFc(ca7), 2.0, A.mult, PFc(ch), A.add)
+    ts(PFc(cty), PFc(cg), 16.0, A.mult, PFc(ct3), A.add)
+    for h, fl in ((0, cnh), (1, ch)):
+        for y, fy in ((0, cna8), (1, ca8)):
+            c = cf00 + 2 * h + y
+            ts(PFc(c), PFc(fl), PFc(fy), A.mult, 256.0, A.mult)
+            ts(LY[h][y], M64, PFc(cty), A.is_equal, PFc(c), A.mult)
+    BK = K(5)
+    ts(BK, G8, PFc(cg8), A.is_equal)
+    csem = [[newsem() for _ in range(3)] for _ in range(NB)]
+
+    for t in range(VIS):
+        for b in range(NB):
+            last = t == VIS - 1
+            bias[1] = 200 * b
+            X = lambda nme, a, e, *k: R("%s%d" % (nme, b), a, e, *k)
+            TF = lambda j, n=128: X("TF", 128 * j, 128 * j + n)
+            TI = lambda j, n=128: X("TI", 128 * j, 128 * j + n)
+            TB = lambda j, n=128: X("TB", 128 * j, 128 * j + n)
+            s0 = SW * t
+            Ai, Zi, Si, Sa = X("ST", s0, s0 + 8), X("ST", s0 + 8, s0 + 136), X("ST", s0 + 136, s0 + 264), X("ST", s0 + 264, s0 + 392)
+            bias[0] = LEAD if b == 0 else 0.0
+            e0 = 128 * t
+            CO, CV = ("CA", "CB") if t % 2 == 0 else ("CB", "CA")
+            blk = (256 * t, 256 * t + 256)
+            for j, (c, w) in enumerate((("CN", "WN"), (CO, "WO"), (CV, "WV"))):
+                dma("sp", X(c, 0, 256), X(w, *blk), 64, csem[b]["NAB".index(c[1])])
+            for c in range(2):
+                for a, e, q in ((64 * c, min(64 * c + 64, NACT), "act"), (max(64 * c, NACT), 64 * c + 64, "dve")):
+                    if a < e:
+                        cp(X("NG", 16 * a, 16 * e), IND(X("WN", 0, 4096), X("EU", e0 + a, e0 + e)), q)
+                mm([(X("PC", 64 * c, 64 * c + 64), R("KB", J[1] + 15 - k, J[1] + 143 - k), X("NG", 1024 * c + k, 1024 * c + 1024, 16), k == 0, k == 15)
+                    for k in range(16)])
+            cp(TB(0), X("PC", 0, 128), "act")
+            w = 128 // VCH
+            for c in range(VCH):
+                cp(X("OG", 16 * w * c, 16 * w * (c + 1)), IND(X("WO", 0, 4096), X("EU", e0 + w * c, e0 + w * (c + 1))), "act")
+            act(TF(0), Si, F.Identity, 0.0, 1.0 / (8 * LN2))
+            cp(TF(1), X("EU", e0, e0 + 128))
+            for o, m in ((X("PC", 384, 512), DC), (X("PD", 256, 384), D16), (X("PD", 384, 512), DK)):
+                mm([(o, I32, TF(1), True, False), (o, m, Si, False, True)])
+            for c, bank in enumerate(("PA", "PB")):
+                mm([(X(bank, 128 * d, 128 * d + 128), DM[4 * c + d], TB(0), True, True) for d in range(4)])
+                ts(X("EQ", 512 * c, 512 * c + 512), X(bank, 0, 512), 0.0, A.is_equal)
+            for c in range(2):
+                mm([(X("PC", 128, 256), WM[d], X("EQ", 128 * d, 128 * d + 128), d == 0, d == 7) for d in range(4 * c, 4 * c + 4)])
+            mm([(X("PD", 0, 128), X("EQ", 128 * d, 128 * d + 128), PN[d], d == 0, False) for d in range(8)])
+            act(X("PC", 256, 384), X("PC", 128, 256), F.Ln, 2.0 ** -60, 1.0, 1.5 if t + b == 0 else 0.0)
+            tt(TF(3), X("PC", 256, 384), TF(0), A.mult)
+            tt(TI(0), X("PC", 384, 512), TF(3), A.add)
+            ts(TI(1), TI(0), 4095, A.bitwise_and)
+            cp(X("TU", 0, 128), TI(1))
+            for c in range(VCH):
+                a, e = 16 * w * c, 16 * w * (c + 1)
+                tt(X("DD", a, e), IND(X("WV", 0, 4096), X("TU", w * c, w * (c + 1))), X("OG", a, e), A.subtract)
+                act(X("AD", a, e), X("DD", a, e), F.Abs)
+                if (c + 1) % (VCH // 4) == 0:
+                    hh = c // (VCH // 4)
+                    mm([(X("PD", k, 128, 16, 32 * hh, 32 * hh + 32), X("AD", 512 * hh + k, 512 * hh + 512, 16), S32, False, k == 15)
+                        for k in range(16)])
+            SC = TF(4)
+            add("dve", ("scan", SC, D0, X("PD", 0, 128)), [D0, X("PD", 0, 128)], [SC], 0.03 + 128 * CY)
+            SI = lambda a, n=8: X("SI", a, a + n)
+            SF = lambda a, n=8: X("SF", a, a + n)
+            cp(SI(0), R(SC[0], SC[1] + 15, SC[2], 16))
+            ts(SI(8), SI(0), 15, A.bitwise_and)
+            mm([(X("PA", 0, 8), I16, C256, True, False)])
+            tt(TB(1), IND(SI(8), LB), MA, A.mult)
+            mm([(X("PA", 0, 8), TB(1), NS1, False, True)])
+            FO = X("TU", 128, 136)
+            ts(FO, X("PA", 0, 8), PFc(c16a), A.add)
+            tt(TB(2), IND(X("AD", 0, 2048), FO), Zi, A.is_ge)
+            mm([(X("PA", 8, 16), TB(2), S32, True, True)])
+            NF = X("SB", 0, 8)
+            ts(NF, X("PA", 8, 16), 272.0, A.is_ge)
+            ts(SI(16), R(SC[0], SC[1] + 15, SC[2], 16), 1.0 / 32, A.mult, -3504.24, A.add)
+            tt(SI(24), SI(16), SI(16), A.mult)
+            tt(SI(32), SI(24), Ai, A.add)
+            ts(SI(40), SI(32), 5, A.arith_shift_right, 31, A.bitwise_and)
+            ts(SI(48), SI(32), 10, A.arith_shift_right, 7, A.bitwise_and)
+            ts(SI(56), SI(32), 5, A.arith_shift_right, 255, A.bitwise_and)
+            OH, UU = TB(3, 256), TB(5, 64)
+            UW = lambda j, a, n: X("TB", 1536 + 64 * j + a, 1536 + 64 * j + a + n)
+            tt(OH, IND(SI(40), LOH), IOH, A.is_equal)
+            tt(UU, IND(SI(40, 16), LU), IU, A.is_equal)
+            ts(TB(6, 64), UU, PFc(66), A.mult)
+            act(X("TB", 832, 896), UU, F.Identity, 0.0, PFc(67))
+            act(TB(7, 32), TB(5, 32), F.Identity, 0.0, 2.0 ** 60)
+            tt(TB(12, 160), IND(NF, LF), TB(6, 160), A.mult)
+            lst = []
+            for q in range(4):
+                o = lambda j: X("PA", 32 + 8 * j, 40 + 8 * j, 1, 32 * q, 32 * q + 32)
+                l = lambda h: R(OH[0], OH[1] + 128 * h + 32 * q, OH[1] + 128 * h + 32 * q + 32)
+                lst += [(o(0), l(0), UW(0, 8 * q, 8), True, True), (o(1), l(0), UW(1, 8 * q, 8), True, True)]
+                for j in range(2):
+                    lst += [(o(2 + j), l(0), UW(2, 8 * q, 8), True, False), (o(2 + j), l(1), UW(j, 32 + 8 * q, 8), False, True)]
+            mm(lst)
+            ts(SF(0, 32), X("PA", 32, 64), math.exp(-TOP), A.max, math.exp(TOP), A.min)
+            act(X("SB", 16, 48), SF(0, 32), F.Ln)
+            mm([(X("PA", 64, 72), PM, X("SB", 16 + 8 * q, 24 + 8 * q), q == 0, q == 3) for q in range(4)])
+            LW = X("TU", 136, 144)
+            lv = (-1.0 / WB, A.mult, 128.375, A.add)
+            ts(SI(64), X("PA", 64, 72), *lv)
+            ts(LW, X("PA", 64, 72), *lv)
+            m0 = MW * t
+            HL = X("MO", m0 + 128, m0 + 136)
+            ts(HL, X("PA", 64, 72), -127.5 * WB, A.is_gt)
+            cp(TB(10), IND(X("DD", 0, 2048), FO), "act")
+            mm([(X("PB", 128 + 128 * h, 256 + 128 * h), SEL[h], TB(10), True, True) for h in range(2)])
+            cp(X("DF", 0, 256), X("PB", 128, 384), "act")
+            GG = X("MO", m0, m0 + 128)
+            cp(GG, IND(X("DF", 0, 272), LW), "act")
+            send(X("ML", m0, m0 + 136), X("MO", m0, m0 + 136), "r0_%d_%d" % (b, t))
+            tt(TB(8), IND(SI(56), LB), MA, A.mult)
+            mm([(X("PC", 0, 8), TB(8), PS1, True, True)])
+            MLs = X("TU", 144, 152)
+            cp(MLs, X("PC", 0, 8))
+            tt(TB(9), IND(SI(64), LB), MA, A.mult)
+            mm([(X("PA", 128 + h, 384, 2), BO[h], TB(9), True, True) for h in range(2)])
+            cp(X("LO", 0, 256), X("PA", 128, 384), "act")
+            AC = TB(11)
+            tt(AC, IND(X("LO", 0, 256), MLs), RC, A.is_equal)
+            cp(TF(5), IND(SC, LK), "act")
+            mm([(X("PB", 0, 128), TF(5), I32, True, True)])
+            ts(TI(2), X("PB", 0, 128), 16.0, A.add)
+            ts(TI(3), TI(2), 4, A.arith_shift_right, 1023, A.bitwise_and)
+            ts(TI(4), TI(2), 15, A.bitwise_and)
+            cp(Sa, TI(3))
+            tt(TF(7), TI(4), Si, A.mult)
+            act(TF(8), Sa, F.Identity, 0.0, PFc(ca))
+            tt(TI(5), X("PD", 256, 384), TF(7), A.subtract)
+            tt(TI(6), X("PD", 384, 512), TF(8), A.add)
+            ts(TI(7, 256), TI(5, 256), 4095, A.bitwise_and)
+            tt(TI(11), IND(X("AD", 0, 2048), FO), Zi, A.add)
+            ts(TI(10), TI(11), 1, A.arith_shift_right)
+            ts(TI(9), Zi, -1.0, A.add, 0.0, A.max)
+            mm([(X("PA", 16, 24), I16, R("KS", 64, 72), True, False)])
+            mm([(X("PA", 16, 24), R("KB", J128[1] + 15 - k, J128[1] + 143 - k), R(AC[0], AC[1] + k, AC[2], 16), False, k == 15) for k in range(16)])
+            SA = X("TU", 168, 176)
+            ts(SA, X("PA", 16, 24), PFc(ca), A.add)
+            n0 = SW * (t + 1)
+            if not last:
+                cp(X("EO", e0 + 128, e0 + 256), IND(TI(7, 256), SA))
+                send(X("EU", e0 + 128, e0 + 256), X("EO", e0 + 128, e0 + 256), "r1_%d_%d" % (b, t))
+            else:
+                cp(TF(1), IND(TI(7, 256), SA))
+            cp(TF(2) if last else X("SO", n0 + 136, n0 + 264), IND(X("ST", s0 + 136, s0 + 392), SA), "act")
+            cp(X("ZB", 0, 128) if last else X("SO", n0 + 8, n0 + 136), IND(TI(9, 256), SA))
+            if not last:
+                mm([(X("PC", 8, 16), N4, NF, True, False), (X("PC", 8, 16), AC, NS2, False, True)])
+                ts(X("SO", n0, n0 + 8), X("PC", 8, 16), 1792.0, A.add)
+                send(X("ST", n0, n0 + 264), X("SO", n0, n0 + 264), "r2_%d_%d" % (b, t))
+            else:
+                mm([(X("PC", 128, 256), BK, TB(2), True, True)])
+                ts(TF(3), X("PC", 128, 256), 8.5, A.is_ge)
+                tt(TF(3), TF(3), AC, A.subtract)
+                for h in range(2):
+                    for j, (y, src) in enumerate((("yc", TF(1)), ("ys", TF(2)), ("ya", TF(3)))):
+                        q = "sp" if (h + j) % 2 else "act"
+                        dma(q, R(y, 128 * h, 128 * h + 128, 1, 4 * b, 4 * b + 4), R(src[0], src[1], src[2], 1, 64 * h, 64 * h + 64, 16), 2, osem[q])
+                    dma("sp", R("yz", 128 * h, 128 * h + 128, 1, 64 * b, 64 * b + 64), X("ZB", 0, 128, 1, 64 * h, 64 * h + 64), 16, osem["sp"])
+            GR, HR = X("ML", m0, m0 + 128), X("ML", m0 + 128, m0 + 136)
+            mm([(X("PC", 256, 272), I16, C16, True, False)] + [(X("PC", 256 + y, 272, 2), LY[0][y], HL, False, False) for y in range(2)]
+               + [(X("PC", 256 + y, 272, 2), LY[1][y], HR, False, y == 1) for y in range(2)])
+            SL = X("TU", 152, 168)
+            ts(SL, X("PC", 256, 272), PFc(ca), A.add)
+            cp(X("WN", *blk), IND(X("CN", 0, 512), SL), "act")
+            mm([(X("PB", 0, 256), I16, X(CO, 256, 512), True, False), (X("PB", 0, 256, 2), SEL[0], GG, False, False)])
+            mm([(X("PB", 1, 256, 2), SEL[1], GR, False, True)])
+            cp(X("WO", *blk), IND(X(CO, 0, 512), SL), "act")
+            ts(X(CV, 256, 512), X("PB", 0, 256), 0.0, A.max, 255.0, A.min)
+            cp(X("WV", *blk), IND(X(CV, 0, 512), SL), "act" if not last else "dve")
+            if t >= VIS - 2:
+                a, e = (0, 256 * t + 256) if not last else blk
+                kb = (e - a) // 8
+                dma("g", R("yn", a, e, 1, 4 * b, 4 * b + 4), X("WN", a, e, 1, 0, 64, 16), kb // 8, osem["g"])
+                dma("act" if last else "sp", R("yo", a, e, 1, 64 * b, 64 * b + 64), X("WO", a, e, 1, 0, 64), kb, osem["act" if last else "sp"])
+                dma("sp", R("yv", a, e, 1, 64 * b, 64 * b + 64), X("WV", a, e, 1, 0, 64), kb, osem["sp"])
+                if last:
+                    dma("sp", R("yx", 0, 256, 1, 64 * b, 64 * b + 64), X(CV, 256, 512, 1, 0, 64), 32, osem["sp"])
+    return ops
+
+
+def overlap(a, b):
+    if psum(a):
+        return True
+    return a[1] < b[2] and b[1] < a[2] and a[4] < b[5] and b[4] < a[5]
+
+
+def plan():
+    ops = build()
+    n = len(ops)
+    hist = {}
+    dep = [set() for _ in ops]
+    for i, o in enumerate(ops):
+        acc = [(r, psum(r)) for r in o["reads"]] + [(r, True) for r in o["writes"]]
+        for r, wr in acc:
+            for (j, r2, w2) in hist.get(r[0], ()):
+                if j != i and (wr or w2) and overlap(r, r2):
+                    dep[i].add(j)
+        for r, wr in acc:
+            h = hist.setdefault(r[0], [])
+            if wr and r[3] == 1 and r[6] == 1:
+                h[:] = [x for x in h if not (psum(r) or (r[1] <= x[1][1] and x[1][2] <= r[2] and r[4] <= x[1][4] and x[1][5] <= r[5]))]
+            h.append((i, r, wr))
+        if o["recv"]:
+            dep[i] = set([o["after"]])
+    succ = [[] for _ in ops]
+    for i in range(n):
+        for j in dep[i]:
+            succ[j].append(i)
+    behind = dict((o["behind"], i) for i, o in enumerate(ops) if "behind" in o)
+    tail = [0.0] * n
+    for i in range(n - 1, -1, -1):
+        o = ops[i]
+        tail[i] = o["dur"] + o["lat"] + o.get("kb", 0) * 0.006 + max([tail[j] + HOP for j in succ[i]] or [0.0])
+    return ops, dep, succ, behind, tail
+
+
+def arrange(ops, dep, succ, behind, tail, nudge):
+    n = len(ops)
+    tail = [tail[i] + nudge.get(ops[i]["kind"], 0.0) for i in range(n)]
+    free = dict((e, 0.0) for e in ENG + ("none",))
+    bus = [0.0]
+    left = [len(d) + ("behind" in o) for d, o in zip(dep, ops)]
+    ready = dict((i, 0.0) for i in range(n) if not left[i])
+    order, fin, start = [], [0.0] * n, [0.0] * n
+    while ready:
+        best = None
+        for e in free:
+            c = [i for i in ready if ops[i]["eng"] == e]
+            if not c:
+                continue
+            t0 = max(free[e], min(ready[i] for i in c))
+            pick = max((i for i in c if ready[i] <= t0 + LOOK), key=lambda i: (tail[i] + ops[i]["bias"], -i))
+            if best is None or t0 < best[0]:
+                best = (t0, pick)
+        i = best[1]
+        o = ops[i]
+        t0 = max(free[o["eng"]], ready.pop(i))
+        start[i] = t0
+        free[o["eng"]] = t0 + o["dur"]
+        f = t0 + o["dur"] + o["lat"]
+        if "kb" in o:
+            bus[0] = max(bus[0], f) + o["kb"] * 0.006
+            f = bus[0]
+        fin[i] = f
+        order.append(i)
+        for j in succ[i] + ([behind[i]] if i in behind else []):
+            left[j] -= 1
+            if not left[j]:
+                ready[j] = max([fin[k] + (0.0 if ops[k]["eng"] == "pe" == ops[j]["eng"] or ops[j]["recv"] else HOP) for k in dep[j]] + [t0])
+    return ops, dep, order, start, fin
+
+
+NUDGE = {105: 6, 228: -0.5, 1110: -1.5, 293: 3, 1092: 6, 22: -3, 257: -1.0, 58: -4.0, 20: 3, 216: 3, 82: 3, 42: -1.5, 1104: -6, 12: -0.5, 55: -1.5, 271: -3, 92: 3, 303: -6, 260: 0.5, 4: -6.0, 314: 1.5, 278: -0.5, 210: -0.5, 91: 1.5, 99: -3, 272: 3, 65: 6, 62: -3, 61: -1.5, 19: -0.5, 44: -4.5, 234: -1.5, 240: 3, 270: 6, 306: -3, 236: 0.5, 67: 0.5, 1137: -3, 57: -0.5, 115: -3, 15: -1.5, 267: -3.0, 215: -3, 47: 3, 48: 0.5, 218: -0.5, 211: 0.5, 268: 1.5, 283: -0.5, 93: 0.5, 247: 7.5, 46: 0.5, 106: -3, 281: -1.5, 14: 0.5, 110: 3, 1007: 6, 21: 6, 274: 3, 205: -0.5, 60: 3, 26: -6, 316: -0.5, 319: 0.5, 207: 0.5, 109: -1.5, 1132: -6, 33: -0.5, 41: 3, 232: -3, 122: 0.5, 71: 1.5, 1166: -1.5, 286: 0.5, 13: 3, 43: 3, 1003: 1.5, 29: -0.5}
+GRAPH = plan()
+PLAN = arrange(*GRAPH, NUDGE)
+
+
+def rank_program(g, core, T, topo):
+    rank = T.rank_of(core)
+    if rank is None:
+        return
+    ops, dep, order = PLAN[:3]
+    nxt = T.cores[(rank + 1) % len(T.cores)]
+    prv = T.cores[(rank - 1) % len(T.cores)]
+    rid, pid = topo.addr(nxt)[:2]
+    mask = topo.mask(core, nxt)
+    n_out, n_in = len(topo.engines(core, nxt)), len(topo.engines(prv, core))
+    Q = {"g": g, "pe": g.tensor, "dve": g.vector, "act": g.scalar, "sp": g.sync}
+
+    def ap(r):
+        if not isinstance(r, tuple):
+            return r
+        if r[0] == "ind":
+            return ap(r[1]).indirect(ap(r[2]))
+        ps = slice(r[4], r[5], r[6]) if r[6] > 1 else slice(r[4], r[5])
+        cs = slice(r[1], r[2], r[3]) if r[3] > 1 else slice(r[1], r[2])
+        return T[r[0]][ps, cs]
+
+    count, mark, know = {}, {}, {}
+    seen = dict((e, {}) for e in ENG)
+    for i in order:
+        o = ops[i]
+        if o["recv"]:
+            mark[i], know[i] = (o["recv"], n_in), {o["recv"]: n_in}
+            count[o["recv"]] = n_in
+            continue
+        e = o["eng"]
+        q, kn = Q[e], seen[e]
+        need = {}
+        for j in dep[i]:
+            if e == "pe" == ops[j]["eng"]:
+                continue
+            s, v = mark[j]
+            if kn.get(s, 0) < v and need.get(s, (0, 0))[0] < v:
+                need[s] = (v, j)
+        for s, (v, j) in sorted(need.items(), key=lambda x: -x[1][1]):
+            if kn.get(s, 0) < v:
+                q.wait_ge(T.sem[s], v)
+                for s2, v2 in know[j].items():
+                    if kn.get(s2, 0) < v2:
+                        kn[s2] = v2
+        c = o["call"]
+        k = c[0]
+        sem, inc = "c_" + e, 1
+        if k == "ts":
+            if c[4] is None:
+                ins = q.tensor_scalar(ap(c[1]), ap(c[2]), ap(c[3]), None, c[5])
+            else:
+                ins = q.tensor_scalar(ap(c[1]), ap(c[2]), ap(c[3]), ap(c[4]), c[5], c[6])
+        elif k == "tt":
+            ins = q.tensor_tensor(ap(c[1]), ap(c[2]), ap(c[3]), c[4])
+        elif k == "cp":
+            ins = q.tensor_copy(ap(c[1]), ap(c[2]))
+        elif k == "act":
+            ins = q.activation(ap(c[1]), ap(c[2]), c[3], bias=ap(c[4]), scale=ap(c[5]))
+        elif k == "mm":
+            for (x, l, r, st, sp) in c[1]:
+                ins = q.matmul(ap(x), ap(l), ap(r), st, sp)
+        elif k == "ms":
+            ins = q.memset(ap(c[1]), c[2])
+        elif k == "io":
+            if SCRATCH[c[1][0]][2] == I3:
+                ins = q.iota(ap(c[1]), c[2], c[3], c[4])
+            else:
+                ins = q.iota(ap(c[1]), c[2], c[3], c[4], allow_small_or_imprecise_dtypes=True)
+        elif k == "scan":
+            ins = q.tensor_tensor_scan(ap(c[1]), ap(c[2]), ap(c[3]), 0.0, A.add, A.max)
+        elif k == "dma":
+            ins = q.dma_start(ap(c[1]), ap(c[2]))
+            sem, inc = o["sem"], 16
+        else:
+            q.remote_dma(ap(c[1]), ap(c[2]), T.sem[c[3]], T.sem.sent, pid, rid, mask)
+            ins, sem, inc = None, "sent", n_out
+        if ins is not None:
+            ins.then_inc(T.sem[sem], inc)
+        count[sem] = count.get(sem, 0) + inc
+        mark[i] = (sem, count[sem])
+        know[i] = dict(kn)
+        know[i][sem] = count[sem]
+    for s in sorted(count):
+        if seen["g"].get(s, 0) < count[s]:
+            g.wait_ge(T.sem[s], count[s])

@@ -2,42 +2,53 @@ import math
 from concourse.mybir import AluOpType as A, ActivationFunctionType as F
 
 VIS, NB = 6, 2
-SW, MW = 400, 144
+SW, MW, CW = 160, 144, 384
 BF, FP, I3, U2 = "bfloat16", "float32", "int32", "uint16"
 SCRATCH = {}
 for _b in range(NB):
-    for _n, _w, _d in (("WN", 4096, BF), ("WO", 4096, BF), ("WV", 4096, BF), ("NG", 2048, BF), ("OG", 2048, BF),
-                       ("DD", 2048, BF), ("AD", 2048, BF), ("EQ", 1024, BF), ("ST", VIS * SW, FP), ("SO", VIS * SW, FP),
+    for _n, _w, _d in (("DA", 4096, BF), ("GV", 4096, BF), ("WO", 4096, FP), ("WV", 4096, FP), ("OG", 2048, FP),
+                       ("EQ", 1024, BF), ("ST", VIS * SW, FP), ("SO", VIS * SW, FP),
                        ("EU", VIS * 128, U2), ("EO", VIS * 128, U2), ("ML", VIS * MW, BF), ("MO", VIS * MW, BF),
-                       ("CN", 512, BF), ("CA", 512, BF), ("CB", 512, BF), ("DF", 272, BF), ("LO", 256, BF),
-                       ("TF", 9 * 128, FP), ("TI", 12 * 128, I3), ("TB", 14 * 128, BF), ("TU", 256, U2),
-                       ("SF", 128, FP), ("SI", 128, I3), ("SB", 64, BF), ("ZB", 128, BF), ("CS", 128, I3), ("CF", 128, FP)):
+                       ("CA", 512, FP), ("CB", 512, FP), ("W5", 768, BF), ("N5", 512, I3), ("YN", 256, FP),
+                       ("DF", CW, BF), ("MK", VIS * CW, BF), ("XP", 256, BF), ("XS", 256, BF), ("TT", 128, FP),
+                       ("TF", 10 * 128, FP), ("TI", 2 * 128, I3), ("TB", 12 * 128, BF), ("TU", 256, U2),
+                       ("SF", 192, FP), ("SI", 64, I3), ("SB", 64, BF), ("ZB", 128, BF), ("CS", 128, I3),
+                       ("DX", 320, FP), ("DY", 160, BF)):
         SCRATCH["%s%d" % (_n, _b)] = ("sbuf", [128, _w], _d)
     for _n in "ABCD":
         SCRATCH["P%s%d" % (_n, _b)] = ("psum", [128, 512], FP)
-for _n, _w, _d in (("NI", 256, I3), ("NH", 256, BF), ("PI", 64, I3), ("PF", 128, FP), ("KB", 50 * 128, BF), ("KF", 9 * 128, FP),
-                   ("KS", 128, BF), ("OI", 80, FP), ("OU", 80, U2)):
+for _n, _w, _d in (("NI", 512, I3), ("NW", 1024, FP), ("NH", 512, BF), ("PI", 64, I3), ("PF", 128, FP), ("KB", 52 * 128, BF),
+                   ("KF", 10 * 128, FP), ("KS", 256, BF), ("OI", 80, FP), ("OU", 80, U2)):
     SCRATCH[_n] = ("sbuf", [128, _w], _d)
+OUTS = ("yn", "yo", "yv", "yx", "yc", "ys", "ya", "yz")
 ENG = ("g", "pe", "dve", "act", "sp")
-NDS = 56
+NDS = 90
 SEMAPHORES = ["c_" + e for e in ENG] + ["d%d" % i for i in range(NDS)] + ["sent"] + \
     ["r%d_%d_%d" % (m, b, t) for m in range(3) for b in range(NB) for t in range(VIS)]
 LN2 = math.log(2.0)
 TOP = 41.5
 WB = 2 * TOP / 64
-HOP, GC, CY, PC = 0.12, 1.6, 0.001, 0.00045
-NACT = 80
+BIG = 786432.0
+ONE, W32 = 1.5 * 2 ** 23, 1.5 * 2 ** 28
+PAR = dict(HOP=0.12, GC=1.56, SC=3.8, CY=0.00083, PC=0.00042, RI=0.4, RL=1.8)
 LOOK = 0.05
 LEAD = 4.0
-VCH = 4
-
-
-class V:
-    pass
+OQ = ("act", "dve", "act", "act")
+VP = (32, 32, 32, 32)
+LOGQ = dict(WO0=("dve", "act") * 4, WV0=("dve", "act") * 4, WO1=("dve", "act") * 4, WV1=("dve", "act") * 4)
+NUDGE = {}
 
 
 def R(buf, c0, c1, step=1, p0=0, p1=128, pstep=1):
     return (buf, c0, c1, step, p0, p1, pstep)
+
+
+def P(r, p0, p1, pstep=1):
+    return (r[0], r[1], r[2], r[3], p0, p1, pstep)
+
+
+def C(r, a, e, step=1):
+    return (r[0], r[1] + a, r[1] + e, step, r[4], r[5], r[6])
 
 
 def IND(win, off):
@@ -58,24 +69,38 @@ def psum(r):
     return r[0] in SCRATCH and SCRATCH[r[0]][0] == "psum"
 
 
-def build():
+def build(par=PAR):
+    GC, SC_, CY, PC = par["GC"], par["SC"], par["CY"], par["PC"]
     ops = []
-    bias = [0.0, 1000]
+    now = dict(bias=0.0, step="start", t=-1, b=0, n=0, seen={})
+
+    def step(name):
+        now["seen"][now["step"]] = now["n"]
+        now["step"], now["n"] = name, now["seen"].get(name, 0)
 
     def add(eng, call, reads, writes, dur, **kw):
-        rd = []
+        rd, wr = [], []
         for r in reads:
             if isinstance(r, tuple):
                 rd += [r[1], r[2]] if r[0] == "ind" else [r]
-        o = dict(eng=eng, call=call, reads=rd, writes=list(writes), dur=dur, lat=0.0, sem=None, after=None, recv=None)
-        o["bias"], o["kind"] = bias[0], bias[1]
-        bias[1] += 1
+        for w in writes:
+            if w[0] == "ind":
+                wr.append(w[1])
+                rd.append(w[2])
+            else:
+                wr.append(w)
+        o = dict(eng=eng, call=call, reads=rd, writes=wr, dur=dur, lat=0.0, sem=None, after=None, recv=None)
+        o["bias"], o["kind"], o["t"], o["b"] = now["bias"], now["step"], now["t"], now["b"]
+        o["pos"] = "%s.%d" % (now["step"], now["n"]) if now["t"] >= 0 else now["step"]
+        now["n"] += 1
         o.update(kw)
         ops.append(o)
         return len(ops) - 1
 
     def cost(out, ins, mul=1.0):
         n = n_of(out)
+        if out[0] == "ind":
+            return 0.06 + n * SC_ * CY
         if ins[0][0] == "ind":
             return 0.06 + n * GC * CY
         if mul == 1.0 and two(out) and all(two(i) for i in ins):
@@ -111,348 +136,431 @@ def build():
     def iota(out, pat, base=0, cm=0):
         return add("g", ("io", out, pat, base, cm), [], [out], 0.13 + 2 * n_of(out) * CY)
 
-    nds = [0]
+    def asel(out, pat, op, fill, base, cm):
+        return add("g", ("as", out, pat, op, fill, base, cm), [out], [out], 0.17 + 2 * n_of(out) * CY)
 
-    def dma(q, out, a, kb, sem=None):
-        if sem is None:
-            sem = "d%d" % nds[0]
-            nds[0] += 1
-        rd = [a] if a[0] in SCRATCH else []
-        wr = [out] if out[0] in SCRATCH else []
-        return add(q, ("dma", out, a), rd, wr, 0.1 if q != "g" else 0.8, lat=1.8, sem=sem, kb=kb)
+    nds = [0]
 
     def newsem():
         nds[0] += 1
         return "d%d" % (nds[0] - 1)
 
+    def dma(q, out, a, kb, sem=None):
+        rd = [a] if a[0] in SCRATCH else []
+        return add(q, ("dma", out, a), rd, [out], 0.1 if q != "g" else 1.0, lat=1.8, sem=sem or newsem(), kb=kb)
+
     def send(dst, src, sem):
-        i = add("g", ("rd", dst, src, sem), [src], [], 0.4, lat=1.6 + n_of(src) * (2 if two(src) else 4) * 0.0006, sem="sent")
+        i = add("g", ("rd", dst, src, sem), [src], [], par["RI"], lat=par["RL"] + n_of(src) * (2 if two(src) else 4) * 0.0006, sem="sent")
         add("none", None, [], [dst], 0.0, after=i, recv=sem)
 
     PIc = lambda j, n=1: R("PI", j, j + n)
     PFc = lambda j, n=1: R("PF", j, j + n)
     K = lambda j, n=128: R("KB", 128 * j, 128 * j + n)
     KF = lambda j, n=128: R("KF", 128 * j, 128 * j + n)
-    osem = {q: newsem() for q in ("sp", "act", "g")}
+    KS = lambda a, n: R("KS", a, a + n)
+    osem = {q: newsem() for q in ("sp", "act")}
 
+    seq = [dma("sp", R("NI", 0, 256), R("nm", 0, 4096, 1, 0, 8), 128)]
     for b in range(NB):
         for h in range(2):
             for j, nme in enumerate(("c0", "s0")):
                 dma("act", R("CS%d" % b, 0, 128, 1, 8 * j + 4 * h, 8 * j + 4 * h + 4),
                     R(nme, 128 * h, 128 * h + 128, 1, 4 * b, 4 * b + 4), 2)
-    dma("sp", R("NI", 0, 256), R("nm", 0, 4096, 1, 0, 8), 128)
-    seq = [len(ops) - 1]
+    iota(PIc(0), [[0, 1]], 0, 1)
+    iota(R("NI", 256, 512), [[1, 256]])
+    for a in (0, 256):
+        ts(R("NW", a, a + 256), R("NI", a, a + 256), 128.0, A.is_lt, -257.0, A.mult)
+        tt(R("NW", 512 + a, 768 + a), R("NW", a, a + 256), R("NI", a, a + 256), A.add)
+    act(R("NH", 0, 256), R("NW", 512, 768), F.Identity, 256.0, 256.0)
     for b in range(NB):
-        for c in range(4):
-            mset(R("WN%d" % b, 1024 * c, 1024 * c + 1024), 0.0)
-    cp(R("NH", 0, 256), R("NI", 0, 256))
-
-    def log(w, nme, b):
-        for h in range(2):
-            seq.append(dma("sp", R("%s%d" % (w, b), 0, 4096, 1, 64 * h, 64 * h + 64), R(nme, 0, 4096, 1, 64 * b, 64 * b + 64), 512))
-
-    log("WO", "vo", 0)
-    for b in range(NB):
-        for h in range(2):
-            seq.append(dma("sp", R("WN%d" % b, 0, 4096, 1, 64 * h, 64 * h + 64, 16), R("NH", 0, 256, 1, 64 * b, 64 * b + 64), 32))
-    for b in range(NB):
-        if b:
-            log("WO", "vo", b)
-        log("WV", "vn", b)
+        for w, nme in (("DA", "vo"), ("GV", "vn")):
+            for c in range(2):
+                seq.append(dma("sp", R("%s%d" % (w, b), 2048 * c, 2048 * c + 2048, 1, 0, 64), R(nme, 2048 * c, 2048 * c + 2048, 1, 64 * b, 64 * b + 64), 256))
+            seq.append(dma("sp", R("%s%d" % (w, b), 0, 4096, 1, 64, 68), R("NH", 0, 256, 1, 64 * b, 64 * b + 64), 32))
         for h in range(2):
             seq.append(dma("sp", R("ZB%d" % b, 0, 128, 1, 64 * h, 64 * h + 64), R("z0", 128 * h, 128 * h + 128, 1, 64 * b, 64 * b + 64), 16))
-            seq.append(dma("sp", R("CA%d" % b, 256, 512, 1, 64 * h, 64 * h + 64), R("xo", 0, 256, 1, 64 * b, 64 * b + 64), 32))
-    for a, e in zip(seq, seq[1:]):
-        ops[e]["behind"] = a
+        seq.append(dma("sp", R("XS%d" % b, 0, 256, 1, 0, 64), R("xo", 0, 256, 1, 64 * b, 64 * b + 64), 32))
 
-    iota(PIc(0), [[0, 1]], 0, 1)
-    cP, ca, cg8, ch, cg, c64, ca8, ca7, cq, cr = range(10)
-    for j, (sh, mk) in enumerate(((0, 15), (4, 7), (6, 1), (4, 3), (0, 63), (3, 1), (0, 7), (5, 3), (4, 1))):
+    cP, ca, cg8, ch, cg, c64, ca8, ca7, cq, cr, ck = range(11)
+    for j, (sh, mk) in enumerate(((0, 15), (4, 7), (6, 1), (4, 3), (0, 63), (3, 1), (0, 7), (5, 3), (4, 1), (3, 15))):
         ts(PIc(1 + j), PIc(0), sh, A.arith_shift_right, mk, A.bitwise_and)
-    cp(PFc(0, 10), PIc(0, 10))
-    (cbase, cP15, cz, c16a, ch128, cnh, ctp, cty, cf00, cf01, cf10, cf11, cna8, ct1, ct2, ct3, cown) = range(10, 27)
-    IC, M16, G8, M64, G4 = K(0, 144), K(2), K(3), K(4), K(5)
-    ICn = K(0)
+    cp(PFc(0, 11), PIc(0, 11))
+    (cbase, cdup, cz, c16a, cz128, cnh, ctp, cty, cf00, cf01, cf10, cf11, cna8, ct1, ct2, ct3, cw, cnb, cnz, cg4) = range(11, 31)
+    IC, M16, G8, G4, M64 = K(0), K(1), K(2), K(3), K(4, 192)
+    iota(C(M64, 0, 192), [[0, 3], [1, 64]])
+    iota(IC, [[1, 128]])
     iota(M16, [[0, 8], [1, 16]])
     iota(G8, [[1, 8], [0, 16]])
-    iota(IC, [[1, 144]])
-    RE, RS, I32, PM, D0 = KF(0), KF(1), KF(2), K(40), KF(4)
-    ts(PFc(cna8), PFc(ca8), -1.0, A.mult, 1.0, A.add)
-    ts(RS, G8, PFc(ca7), A.is_equal, PFc(ca8), A.mult)
-    ts(RE, G8, PFc(ca7), A.is_equal, PFc(cna8), A.mult)
-    ts(KF(5), M16, 1.0, A.mult)
-    tt(KF(5), KF(5), RS, A.mult)
-    tt(RE, RE, KF(5), A.add)
-    for b in range(NB):
-        s16 = lambda r: R(r[0], r[1], r[2], 1, 0, 16)
-        cp(s16(R("CF%d" % b, 0, 128)), s16(R("CS%d" % b, 0, 128)))
-        mm([(R("PC%d" % b, 0, 128), s16(RE), s16(R("CF%d" % b, 0, 128)), True, True),
-            (R("PC%d" % b, 128, 256), s16(RS), s16(R("CF%d" % b, 0, 128)), True, True)])
-        cp(R("TI%d" % b, 0, 128), R("PC%d" % b, 0, 128))
-        ts(R("TI%d" % b, 128, 256), R("TI%d" % b, 0, 128), 4095, A.bitwise_and)
-        cp(R("EU%d" % b, 0, 128), R("TI%d" % b, 128, 256))
-        cp(R("ST%d" % b, 136, 264), R("PC%d" % b, 128, 256), "act")
-        cp(R("ST%d" % b, 8, 136), R("ZB%d" % b, 0, 128), "act")
-        mset(R("ST%d" % b, 0, 8), 1792.0)
-        mset(R("DF%d" % b, 256, 272), 0.0)
-        iota(R("CN%d" % b, 256, 512), [[1, 256]])
-    J, I16, MA, RC = K(6, 144), K(8), K(9), K(10)
-    ts(PFc(cP15), PFc(cP), 15.0, A.add)
+    M64 = C(M64, 0, 128)
+    DUP, I16, MA, I16x, PM, PM2 = K(6), K(7), K(8), K(9), K(10), K(11)
+    I32, I32x, D0, MSK, RE0, REP, RSP, REN, REA, TMP = (KF(j) for j in range(10))
+    ts(PFc(ct1), PFc(cP), -64.0, A.add, 0.0, A.max)
+    ts(PFc(ct1), PFc(ct1), 15.0, A.mult, PFc(c64), A.add)
+    ts(DUP, M64, PFc(ct1), A.is_equal)
     ts(PFc(cz), PFc(ca), 0.0, A.is_equal)
-    ts(J, IC, PFc(cP15), A.is_equal, PFc(cz), A.mult)
-    ts(I16, ICn, PFc(cP), A.is_equal)
-    tt(PFc(cbase), PFc(cP), PFc(ca), A.subtract)
-    tE, tL, inv, dl, wE = PFc(32, 8), PFc(40, 8), PFc(48, 8), PFc(56, 8), R("KS", 0, 8)
+    ts(MSK, G8, PFc(ca7), A.is_equal)
+    f0, f1, f4, f5 = (PFc(96 + j) for j in range(4))
+    for f, v in ((f0, 0.0), (f1, 1.0), (f4, 4.0), (f5, 5.0)):
+        ts(f, PFc(ck), v, A.is_equal)
+    lin = lambda out, a, scale, bias=0.0: act(out, a, F.Identity, bias, scale)
+    lin(PFc(100), f1, 7.5 - 0.000354, f0)
+    lin(PFc(101), f1, 16.0, f0)
+    lin(PFc(102), f4, -1.0, PFc(101))
+    lin(PFc(103), f5, 1.0, f1)
+    lin(PFc(104), f1, 1.0 / (8 * LN2))
+    for m, al, be in ((RE0, f0, f1), (REP, PFc(100), f1), (REN, PFc(102), f1), (REA, PFc(101), PFc(103))):
+        lin(m, M16, be, al)
+        tt(m, m, MSK, A.mult)
+    lin(RSP, MSK, PFc(104))
+    ts(I16, IC, PFc(cP), A.is_equal)
+    lin(I32, I16, 1.0)
+    lin(I32x, I16, 16.0)
+    lin(I16x, I16, 32.0)
+    CODE = R("NH", 256, 512)
+    lin(PFc(105), PFc(cz), 256.0)
+    lin(CODE, R("NW", 768, 1024), PFc(105), PFc(105))
+    lin(PFc(cnh), PFc(ch), -1.0, 1.0)
+    SEL = [K(12), K(13)]
+    for h, fl in ((0, cnh), (1, ch)):
+        ts(SEL[h], M64, PFc(c64), A.is_equal, PFc(fl), A.mult)
+    fill = lambda out, v: iota(out, [[0, n_of(out)]], v)
+
+    def spread(b, src, out):
+        o = R("PD%d" % b, 256, 512)
+        mm([(o, I16, CODE, True, False)] + [(C(o, y, 256, 2), SEL[y], src, False, y == 1) for y in range(2)])
+        cp(out, o, "act")
+
+    for b in range(NB):
+        X = lambda nme, a, e, *k: R("%s%d" % (nme, b), a, e, *k)
+        fill(X("TT", 0, 128), 0)
+        cp(X("TT", 0, 128, 1, 0, 16), X("CS", 0, 128, 1, 0, 16))
+        mm([(X("PC", 0, 128), P(RE0, 0, 16), X("TT", 0, 128, 1, 0, 16), True, True),
+            (X("PC", 128, 144), X("TT", 0, 128, 1, 0, 16), P(C(I32, 0, 16), 0, 16), True, True)])
+        cp(X("TI", 0, 128), X("PC", 0, 128))
+        ts(X("TI", 128, 256), X("TI", 0, 128), 4095, A.bitwise_and)
+        cp(X("EU", 0, 128), X("TI", 128, 256))
+        cp(X("ST", 0, 16), X("PC", 128, 144), "act")
+        fill(X("ST", 16, 24), 1792)
+        cp(X("ST", 24, 152), X("ZB", 0, 128), "act")
+        fill(X("SF", 80, 88), -32)
+        fill(X("DF", 256, CW), 0)
+        for w, s, banks in (("WO", "DA", "ABCD"), ("WV", "GV", "CD")):
+            step("log%s%d" % (w, b))
+            for c in range(8):
+                bank = X("P" + banks[c % len(banks)], 0, 512)
+                mm([(bank, P(DUP, 0, 68), X(s, 512 * c, 512 * c + 512, 1, 0, 68), True, True)])
+                cp(X(w, 512 * c, 512 * c + 512), bank, LOGQ[w + str(b)][c])
+        step("start")
+        mm([(X("PD", 0, 128, 1, 64 * y, 64 * y + 64), P(C(I16, 0, 64), 0, 64), X("XS", y, 256, 2, 0, 64), True, True) for y in range(2)])
+        cp(X("XP", 0, 128), X("PD", 0, 128), "act")
+        spread(b, X("XP", 0, 128), X("CA", 256, 512))
+    tE, tL, inv, dl, wE = PFc(32, 8), PFc(40, 8), PFc(48, 8), PFc(56, 8), KS(0, 8)
+    lin(PFc(cbase), PFc(cg8), 16.0)
     iota(PIc(16, 8), [[1, 8]], 1, 1)
-    iota(PIc(24, 8), [[-1, 8]], 15, 1)
+    iota(R("OI", 64, 72), [[-1, 8]], 15)
+    ts(PIc(24, 8), R("OI", 64, 72), PFc(ck), A.add)
     ts(PIc(32, 16), PIc(16, 16), 15, A.bitwise_and)
-    ts(inv, PIc(40, 8), PFc(cbase), A.add)
+    lin(PFc(cnb), PFc(ca7), 16.0)
+    ts(inv, PIc(40, 8), PFc(cnb), A.add)
     ts(tE, PIc(32, 8), PFc(ca), A.min, PFc(cbase), A.add)
     ts(tL, PIc(32, 8), PFc(ca), A.max, PFc(cbase), A.add)
     tt(dl, tL, tE, A.subtract)
-    act(wE, dl, F.Exp, -60 * LN2, 8 * LN2, 1.5)
-    cp(PFc(72, 8), wE)
-    ts(PFc(79), PFc(79), PFc(cna8), A.mult)
-    DM = [K(12 + d) for d in range(8)]
-    WM = [K(20 + d) for d in range(8)]
-    PN = [K(28 + d) for d in range(8)]
+    act(wE, dl, F.Exp, -60 * LN2, 8 * LN2, 1.3)
+    lin(PFc(cna8), PFc(ca8), -1.0, 1.0)
+    lin(PFc(72, 7), C(wE, 0, 7), 1.0)
+    lin(PFc(79), C(wE, 7, 8), PFc(cna8))
+    DM = [K(14 + d) for d in range(8)]
+    WM = [K(22 + d) for d in range(8)]
+    PN = [K(30 + d) for d in range(8)]
     for d in range(8):
-        ts(DM[d], ICn, PFc(48 + d), A.is_equal)
-        tt(DM[d], DM[d], I16, A.subtract)
+        ts(DM[d], IC, PFc(48 + d), A.is_equal)
+    for c in range(2):
+        asel(K(14 + 4 * c, 512), [[0, 4], [1, 8], [8, 16]], A.not_equal, -1.0, 0, -1)
     for d in range(8):
-        ts(WM[d], ICn, PFc(32 + d), A.is_equal, PFc(72 + d), A.mult)
+        ts(WM[d], IC, PFc(32 + d), A.is_equal, PFc(72 + d), A.mult)
     for d in range(8):
-        ts(PN[d], ICn, PFc(40 + d), A.is_equal, -131072.0, A.mult)
-    S32, NS1, PS1, NS2, C256, C16 = (R("KS", 16, 24), R("KS", 24, 32), R("KS", 32, 40), R("KS", 40, 48), R("KS", 48, 56), R("KS", 64, 80))
-    for r, v in ((S32, 32.0), (NS1, -1.0), (PS1, 1.0), (NS2, -2.0)):
-        ts(r, K(0, 8), PFc(cg8), A.is_equal, v, A.mult)
-    ts(C256, K(0, 8), 256.0, A.mult)
-    ts(C16, K(0, 16), 16.0, A.mult)
-    ts(D0, M16, 0.0, A.is_equal, -1000001.0, A.mult)
-    ts(D0, D0, 1.0, A.add)
+        ts(PN[d], IC, PFc(40 + d), A.is_equal, -262144.0, A.mult)
+    S64, NS1, PS1, C256, W4, C16, C16h, CA24, AR = (KS(16, 8), KS(24, 8), KS(32, 8), KS(40, 8), KS(48, 8), KS(64, 16), KS(80, 16),
+                                                    KS(96, 24), [KS(128, 24), KS(160, 24)])
+    SELN = PFc(112, 8)
+    ts(PS1, K(0, 8), PFc(cg8), A.is_equal)
+    for r, v in ((SELN, PFc(cz)), (S64, 64.0), (NS1, -1.0)):
+        lin(r, PS1, v)
+    iota(C256, [[256, 8]])
+    iota(C16, [[16, 16]])
+    iota(C16h, [[0, 2], [16, 8]])
+    for j, v in enumerate((1, 0, 56)):
+        fill(C(CA24, 8 * j, 8 * j + 8), v)
+    iota(KS(192, 24), [[0, 3], [1, 8]])
+    lin(PFc(cnz), PFc(cz), -1.0)
+    lin(PFc(cg4), PFc(cg), 1.0, 4.0)
+    for h, c in ((0, cg), (1, cg4)):
+        ts(AR[h], KS(192, 24), PFc(c), A.is_equal, PFc(cnz), A.mult)
+    fill(D0, 1)
+    asel(D0, [[0, 8], [1, 16]], A.not_equal, -4000000.0, 0, 0)
     ts(MA, M16, PFc(ca), A.is_equal)
-    ts(I32, ICn, PFc(cP), A.is_equal)
-    DC, D16, DK, J128, N4 = KF(6), KF(7), KF(8), K(48, 144), K(39)
-    act(DC, I32, F.Identity, 0.0, 7.5 - 0.000354)
-    act(D16, I32, F.Identity, 0.0, 16.0)
-    ts(PFc(27), PFc(ca), -1.0, A.mult, 16.0, A.add)
-    act(DK, I32, F.Identity, 0.0, PFc(27))
-    act(J128, J, F.Identity, 0.0, 128.0)
-    act(N4, I32, F.Identity, 0.0, 32.0)
-    ts(PFc(c16a), PFc(ca), 16.0, A.mult, 15.0, A.add)
-    ts(PFc(ch128), PFc(ch), 128.0, A.mult)
-    ts(RC, ICn, PFc(ch128), A.add)
-    ts(PFc(cnh), PFc(ch), -1.0, A.mult, 1.0, A.add)
+    J2, IOH, IU, SF64, ONES = K(38, 192), K(40, 256), K(42, 64), K(43, 64), K(44)
+    lin(PFc(cz128), PFc(cz), 128.0)
+    ts(J2, K(4, 192), PFc(c64), A.is_equal, PFc(cz128), A.mult)
+    lin(PFc(c16a), PFc(ca), 16.0, 15.0)
+    fill(ONES, 1)
     O = lambda a, n: R("OI", a, a + n)
     iota(O(0, 8), [[1, 8]])
-    iota(O(8, 8), [[16, 8]], 15)
+    iota(O(8, 8), [[16, 8]], 1)
     iota(O(16, 16), [[1, 8], [0, 2]])
     iota(O(32, 4), [[2, 4]], 8)
-    iota(O(36, 8), [[0, 2], [2, 4]])
-    iota(O(44, 2), [[2, 2]])
-    ts(O(32, 14), O(32, 14), PFc(ca8), A.add)
-    cp(R("OU", 0, 46), O(0, 46))
-    LB, LK, LOH, LU, LF = (R("OU", a, a + n) for a, n in ((0, 8), (8, 8), (16, 16), (32, 4), (36, 10)))
-    IOH, IU = K(36, 256), K(38, 64)
+    ts(O(32, 4), O(32, 4), PFc(ca8), A.add)
+    cp(R("OU", 0, 36), O(0, 36))
+    LB, LOH, LU = (R("OU", a, a + n) for a, n in ((0, 8), (16, 16), (32, 4)))
     iota(IOH, [[0, 8], [1, 2], [2, 16]])
     iota(IU, [[0, 8], [1, 8]])
-    ts(PFc(cown), PFc(c64), -WB, A.mult, TOP, A.add)
-    ts(PFc(ct1), PFc(ch), -300.0, A.mult)
-    tt(PFc(64), PFc(cown), PFc(ct1), A.add)
-    ts(PFc(65), PFc(c64), -WB, A.mult, PFc(ch), A.mult)
-    ts(PFc(65), PFc(65), TOP, A.add)
-    act(PFc(66, 2), PFc(64, 2), F.Exp)
-    iota(M64, [[0, 2], [1, 64]])
-    iota(G4, [[0, 2], [1, 4], [0, 16]])
-    SEL = [K(41), K(42)]
-    BO = [K(43), K(44)]
-    LY = [[K(45), K(46)], [K(47), K(11)]]
+    iota(SF64, [[1, 8], [0, 8]])
+    ts(SF64, SF64, PFc(cg8), A.is_equal)
+    act(PFc(cw), PFc(c64), F.Exp, -WB, -WB)
+    lin(PFc(66), PFc(cw), PFc(cnh))
+    lin(PFc(67), PFc(cw), PFc(ch), PFc(cnh))
+    IH = [K(49), K(50)]
     for h, fl in ((0, cnh), (1, ch)):
-        ts(SEL[h], M64, PFc(c64), A.is_equal, PFc(fl), A.mult)
-        ts(BO[h], G4, PFc(cg), A.is_equal, PFc(fl), A.mult)
-    ts(PFc(ct2), PFc(cr), 64.0, A.mult, PFc(ca), A.add)
-    ts(PFc(ctp), PFc(cq), 16.0, A.mult, PFc(ct2), A.add)
-    ts(PM, ICn, PFc(ctp), A.is_equal)
-    ts(PFc(ct3), PFc(ca7), 2.0, A.mult, PFc(ch), A.add)
-    ts(PFc(cty), PFc(cg), 16.0, A.mult, PFc(ct3), A.add)
+        lin(IH[h], I16, PFc(fl))
+    lin(PFc(106), PFc(ca), -WB / 2)
+    act(W4, O(8, 8), F.Exp, PFc(106), -WB / 2)
+    LY = [[K(45), K(46)], [K(47), K(48)]]
+    lin(PFc(ct2), PFc(cr), 64.0, PFc(ca))
+    lin(PFc(ctp), PFc(cq), 16.0, PFc(ct2))
+    ts(PM, IC, PFc(ctp), A.is_equal)
+    lin(PM2, PM, 2.0)
+    lin(PFc(ct3), PFc(ca7), 2.0, PFc(ch))
+    lin(PFc(cty), PFc(cg), 16.0, PFc(ct3))
+    ts(G4, M64, PFc(cty), A.is_equal, 256.0, A.mult)
     for h, fl in ((0, cnh), (1, ch)):
         for y, fy in ((0, cna8), (1, ca8)):
             c = cf00 + 2 * h + y
-            ts(PFc(c), PFc(fl), PFc(fy), A.mult, 256.0, A.mult)
-            ts(LY[h][y], M64, PFc(cty), A.is_equal, PFc(c), A.mult)
-    BK = K(5)
-    ts(BK, G8, PFc(cg8), A.is_equal)
-    csem = [[newsem() for _ in range(3)] for _ in range(NB)]
+            lin(PFc(c), PFc(fl), PFc(fy))
+            lin(LY[h][y], G4, PFc(c))
+    step("zero")
+    for b in range(NB):
+        for t in range(VIS):
+            iota(R("MK%d" % b, CW * t, CW * t + CW), [[0, CW]])
+        iota(R("N5%d" % b, 0, 512), [[0, 2], [1, 256]])
+    csem = [[newsem() for _ in range(2)] for _ in range(NB)]
 
     for t in range(VIS):
         for b in range(NB):
             last = t == VIS - 1
-            bias[1] = 200 * b
             X = lambda nme, a, e, *k: R("%s%d" % (nme, b), a, e, *k)
             TF = lambda j, n=128: X("TF", 128 * j, 128 * j + n)
             TI = lambda j, n=128: X("TI", 128 * j, 128 * j + n)
             TB = lambda j, n=128: X("TB", 128 * j, 128 * j + n)
-            s0 = SW * t
-            Ai, Zi, Si, Sa = X("ST", s0, s0 + 8), X("ST", s0 + 8, s0 + 136), X("ST", s0 + 136, s0 + 264), X("ST", s0 + 264, s0 + 392)
-            bias[0] = LEAD if b == 0 else 0.0
-            e0 = 128 * t
-            CO, CV = ("CA", "CB") if t % 2 == 0 else ("CB", "CA")
-            blk = (256 * t, 256 * t + 256)
-            for j, (c, w) in enumerate((("CN", "WN"), (CO, "WO"), (CV, "WV"))):
-                dma("sp", X(c, 0, 256), X(w, *blk), 64, csem[b]["NAB".index(c[1])])
-            for c in range(2):
-                for a, e, q in ((64 * c, min(64 * c + 64, NACT), "act"), (max(64 * c, NACT), 64 * c + 64, "dve")):
-                    if a < e:
-                        cp(X("NG", 16 * a, 16 * e), IND(X("WN", 0, 4096), X("EU", e0 + a, e0 + e)), q)
-                mm([(X("PC", 64 * c, 64 * c + 64), R("KB", J[1] + 15 - k, J[1] + 143 - k), X("NG", 1024 * c + k, 1024 * c + 1024, 16), k == 0, k == 15)
-                    for k in range(16)])
-            cp(TB(0), X("PC", 0, 128), "act")
-            w = 128 // VCH
-            for c in range(VCH):
-                cp(X("OG", 16 * w * c, 16 * w * (c + 1)), IND(X("WO", 0, 4096), X("EU", e0 + w * c, e0 + w * (c + 1))), "act")
-            act(TF(0), Si, F.Identity, 0.0, 1.0 / (8 * LN2))
-            cp(TF(1), X("EU", e0, e0 + 128))
-            for o, m in ((X("PC", 384, 512), DC), (X("PD", 256, 384), D16), (X("PD", 384, 512), DK)):
-                mm([(o, I32, TF(1), True, False), (o, m, Si, False, True)])
-            for c, bank in enumerate(("PA", "PB")):
-                mm([(X(bank, 128 * d, 128 * d + 128), DM[4 * c + d], TB(0), True, True) for d in range(4)])
-                ts(X("EQ", 512 * c, 512 * c + 512), X(bank, 0, 512), 0.0, A.is_equal)
-            for c in range(2):
-                mm([(X("PC", 128, 256), WM[d], X("EQ", 128 * d, 128 * d + 128), d == 0, d == 7) for d in range(4 * c, 4 * c + 4)])
-            mm([(X("PD", 0, 128), X("EQ", 128 * d, 128 * d + 128), PN[d], d == 0, False) for d in range(8)])
-            act(X("PC", 256, 384), X("PC", 128, 256), F.Ln, 2.0 ** -60, 1.0, 1.5 if t + b == 0 else 0.0)
-            tt(TF(3), X("PC", 256, 384), TF(0), A.mult)
-            tt(TI(0), X("PC", 384, 512), TF(3), A.add)
-            ts(TI(1), TI(0), 4095, A.bitwise_and)
-            cp(X("TU", 0, 128), TI(1))
-            for c in range(VCH):
-                a, e = 16 * w * c, 16 * w * (c + 1)
-                tt(X("DD", a, e), IND(X("WV", 0, 4096), X("TU", w * c, w * (c + 1))), X("OG", a, e), A.subtract)
-                act(X("AD", a, e), X("DD", a, e), F.Abs)
-                if (c + 1) % (VCH // 4) == 0:
-                    hh = c // (VCH // 4)
-                    mm([(X("PD", k, 128, 16, 32 * hh, 32 * hh + 32), X("AD", 512 * hh + k, 512 * hh + 512, 16), S32, False, k == 15)
-                        for k in range(16)])
-            SC = TF(4)
-            add("dve", ("scan", SC, D0, X("PD", 0, 128)), [D0, X("PD", 0, 128)], [SC], 0.03 + 128 * CY)
             SI = lambda a, n=8: X("SI", a, a + n)
             SF = lambda a, n=8: X("SF", a, a + n)
-            cp(SI(0), R(SC[0], SC[1] + 15, SC[2], 16))
+            s0, e0, m0, n0 = SW * t, 128 * t, MW * t, SW * (t + 1)
+            CSi, Si, Ai, Zi = X("ST", s0, s0 + 16), X("ST", s0 + 8, s0 + 16), X("ST", s0 + 16, s0 + 24), X("ST", s0 + 24, s0 + 152)
+            now.update(bias=LEAD if b == 0 else 0.0, t=t, b=b, step="", seen={})
+            CO, CV = ("CA", "CB") if t % 2 == 0 else ("CB", "CA")
+            Xo, Xn = X("XP", 128 * (t % 2), 128 * (t % 2) + 128), X("XP", 128 - 128 * (t % 2), 256 - 128 * (t % 2))
+            blk = (256 * t, 256 * t + 256)
+            step("old")
+            if not last:
+                for c, w in ((CO, "WO"), (CV, "WV")):
+                    dma("sp", X(c, 0, 256), X(w, *blk), 128, csem[b]["AB".index(c[1])])
+            else:
+                for h, nme in enumerate(("vo", "vn")):
+                    seq.append(dma("sp", X("W5", 0, 256, 1, 64 * h, 64 * h + 64), R(nme, blk[0], blk[1], 1, 64 * b, 64 * b + 64), 32))
+                dma("sp", X("N5", 0, 256, 1, 0, 64, 16), R("nm", blk[0], blk[1], 1, 4 * b, 4 * b + 4), 4)
+            step("turn")
+            T16, T48 = X("TT", 0, 128, 1, 0, 16), X("TT", 0, 128, 1, 0, 48)
+            if t:
+                mm([(X("PC", 0, 128, 1, 0, 16), CSi, I32, True, True)])
+                cp(T16, X("PC", 0, 128, 1, 0, 16), "act")
+            step("rows")
+            mm([(X("PC", 128, 256), P(REP, 0, 16), T16, True, True)])
+            mm([(X("PC", 256, 384), P(RSP, 0, 16), T16, True, True)])
+            step("base")
+            mm([(X("PD", 128, 144), I32, CSi, True, False), (X("PD", 128, 136), I32x, Si, False, True)])
+            step("zq")
+            ZQ, ZW = TF(0), TF(1, 256)
+            act(ZQ, Zi, F.Identity, -0.25, 0.5)
+            act(TF(1), Zi, F.Relu, -1.0, 1.0)
+            for c, bank in enumerate(("PA", "PB")):
+                for y in range(2):
+                    p = 2 * c + y
+                    step("O%d" % p)
+                    cp(X("OG", 512 * p, 512 * p + 512), IND(X("WO", 0, 4096), X("EU", e0 + 32 * p, e0 + 32 * p + 32)), OQ[p])
+                    step("name%d" % c)
+                    for kk in range(0, 4, 2):
+                        mm([(X(bank, 32 * y + 8 * k, 32 * y + 8 * k + 8), X("OG", 512 * p + k, 512 * p + 512, 4), SELN, True, True) for k in (kk, kk + 1)])
+                N1, N2 = C(TB(0), 64 * c, 64 * c + 64), C(TB(1), 64 * c, 64 * c + 64)
+                act(N1, X(bank, 0, 64), F.Identity, -127.5)
+                mm([(X(bank, 64 + 32 * y, 96 + 32 * y, 1, 32 * q, 32 * q + 32), C(N1, 32 * y, 32 * y + 32), C(I16, q, 128, 4), True, True)
+                    for y in range(2) for q in range(4)])
+                cp(N2, X(bank, 64, 128), "act")
+                mm([(X(bank, d, 512, 8), DM[d], N2, True, True) for d in range(8)])
+                step("eq%d" % c)
+                ts(X("EQ", 512 * c, 512 * c + 512), X(bank, 0, 512), 0.0, A.is_equal)
+                step("last%d" % c)
+                mm([(X(bank, 0, 64), WM[d], X("EQ", 512 * c + d, 512 * c + 512, 8), d == 0, d == 7) for d in range(8)])
+                h64 = lambda r: C(r, 64 * c, 64 * c + 64)
+                act(h64(TF(3)), X(bank, 0, 64), F.Ln, 2.0 ** -60, 1.0, 1.5 if t + b + c == 0 else 0.0)
+                tt(h64(TF(4)), h64(X("PC", 256, 384)), h64(TF(3)), A.mult)
+                tt(h64(TI(0)), h64(X("PC", 128, 256)), h64(TF(4)), A.add)
+                ts(h64(TI(1)), h64(TI(0)), 4095, A.bitwise_and)
+                cp(h64(X("TU", 0, 128)), h64(TI(1)))
+            step("head")
+            mm([(X("PD", 0, 128), X("EQ", d, 1024, 8), PN[d], d == 0, False) for d in range(8)])
+            r0, DD, AD = 0, X("DA", 0, 2048), X("DA", 2048, 4096)
+            for c, w in enumerate(VP):
+                a, e = 16 * r0, 16 * (r0 + w)
+                step("V%d" % c)
+                tt(C(DD, a, e), IND(X("WV", 0, 4096), X("TU", r0, r0 + w)), X("OG", a, e), A.subtract)
+                step("abs%d" % c)
+                act(C(AD, a, e), C(DD, a, e), F.Abs, 0.0, 0.5)
+                for hh in range(r0 // 32, (r0 + w) // 32):
+                    mm([(X("PD", k, 128, 16, 32 * hh, 32 * hh + 32), C(AD, 512 * hh + k, 512 * hh + 512, 16), S64, False, k == 15)
+                        for k in range(16)])
+                r0 += w
+            step("pick")
+            SC = TF(5)
+            add("dve", ("scan", SC, D0, X("PD", 0, 128)), [D0, X("PD", 0, 128)], [SC], 0.03 + 128 * CY)
+            KEY = C(SC, 15, 128, 16)
+            ts(SI(0), KEY, 16.0, A.add)
             ts(SI(8), SI(0), 15, A.bitwise_and)
-            mm([(X("PA", 0, 8), I16, C256, True, False)])
-            tt(TB(1), IND(SI(8), LB), MA, A.mult)
-            mm([(X("PA", 0, 8), TB(1), NS1, False, True)])
+            tt(TB(2), IND(SI(8), LB), MA, A.mult)
+            mm([(X("PA", 0, 8), I16, C256, True, False), (X("PA", 0, 8), TB(2), NS1, False, True)])
             FO = X("TU", 128, 136)
             ts(FO, X("PA", 0, 8), PFc(c16a), A.add)
-            tt(TB(2), IND(X("AD", 0, 2048), FO), Zi, A.is_ge)
-            mm([(X("PA", 8, 16), TB(2), S32, True, True)])
-            NF = X("SB", 0, 8)
-            ts(NF, X("PA", 8, 16), 272.0, A.is_ge)
-            ts(SI(16), R(SC[0], SC[1] + 15, SC[2], 16), 1.0 / 32, A.mult, -3504.24, A.add)
-            tt(SI(24), SI(16), SI(16), A.mult)
-            tt(SI(32), SI(24), Ai, A.add)
-            ts(SI(40), SI(32), 5, A.arith_shift_right, 31, A.bitwise_and)
-            ts(SI(48), SI(32), 10, A.arith_shift_right, 7, A.bitwise_and)
-            ts(SI(56), SI(32), 5, A.arith_shift_right, 255, A.bitwise_and)
-            OH, UU = TB(3, 256), TB(5, 64)
-            UW = lambda j, a, n: X("TB", 1536 + 64 * j + a, 1536 + 64 * j + a + n)
-            tt(OH, IND(SI(40), LOH), IOH, A.is_equal)
-            tt(UU, IND(SI(40, 16), LU), IU, A.is_equal)
-            ts(TB(6, 64), UU, PFc(66), A.mult)
-            act(X("TB", 832, 896), UU, F.Identity, 0.0, PFc(67))
-            act(TB(7, 32), TB(5, 32), F.Identity, 0.0, 2.0 ** 60)
-            tt(TB(12, 160), IND(NF, LF), TB(6, 160), A.mult)
+            tt(TB(3), IND(AD, FO), ZQ, A.is_ge)
+            step("mark")
+            ts(SF(0), KEY, W32, A.add, -W32, A.add)
+            act(SF(8), SF(0), F.Square, -3504.0, 1.0 / 32)
+            tt(SI(16), SF(8), Ai, A.add)
+            ts(SI(24), SI(16), 5, A.arith_shift_right, 31, A.bitwise_and)
+            ts(SI(32), SI(16), 10, A.arith_shift_right, 7, A.bitwise_and)
+            OH, UU, UF, UW = TB(4, 256), TB(6, 64), C(TB(6), 64, 128), TB(7)
+            tt(UU, IND(SI(24, 16), LU), IU, A.is_equal)
+            tt(OH, IND(SI(24), LOH), IOH, A.is_equal)
+            step("claim")
+            mm([(X("PA", 16, 80), I16x, UU, True, False), (X("PA", 16, 80), TB(3), SF64, False, True)])
+            for y in range(2):
+                ts(C(UW, y, 128, 2), X("PA", 16, 80), 40.5, A.is_ge, PFc(66 + y), A.mult)
+            ts(UF, X("PA", 16, 80), 40.5, A.is_ge)
+            o = lambda a, e, q, st=1: X("PA", 96 + a, 96 + e, st, 32 * q, 32 * q + 32)
+            l = lambda h, q: C(OH, 128 * h + 32 * q, 128 * h + 32 * q + 32)
+            uw = lambda h, q: C(UW, 64 * h + 16 * q, 64 * h + 16 * q + 16)
+            uf = lambda h, q: C(UF, 32 * h + 8 * q, 32 * h + 8 * q + 8)
+            mm([(o(0, 16, q), l(0, q), uw(0, q), True, True) for q in range(4)])
             lst = []
             for q in range(4):
-                o = lambda j: X("PA", 32 + 8 * j, 40 + 8 * j, 1, 32 * q, 32 * q + 32)
-                l = lambda h: R(OH[0], OH[1] + 128 * h + 32 * q, OH[1] + 128 * h + 32 * q + 32)
-                lst += [(o(0), l(0), UW(0, 8 * q, 8), True, True), (o(1), l(0), UW(1, 8 * q, 8), True, True)]
-                for j in range(2):
-                    lst += [(o(2 + j), l(0), UW(2, 8 * q, 8), True, False), (o(2 + j), l(1), UW(j, 32 + 8 * q, 8), False, True)]
+                lst += [(o(16, 32, q), l(1, q), uw(1, q), True, False)] + [(o(16 + y, 32, q, 2), l(0, q), uf(0, q), False, y == 1) for y in range(2)]
+            lst.append((X("PA", 128, 136), I16, W4, True, False))
+            for q in range(4):
+                lst += [(o(32, 40, q), l(h, q), uf(h, q), False, h == 1) for h in range(2)]
             mm(lst)
-            ts(SF(0, 32), X("PA", 32, 64), math.exp(-TOP), A.max, math.exp(TOP), A.min)
-            act(X("SB", 16, 48), SF(0, 32), F.Ln)
-            mm([(X("PA", 64, 72), PM, X("SB", 16 + 8 * q, 24 + 8 * q), q == 0, q == 3) for q in range(4)])
+            ts(SF(16, 40), X("PA", 96, 136), math.exp(-2 * TOP), A.max, 1.0, A.min)
+            act(X("SB", 0, 40), SF(16, 40), F.Ln, 0.0, math.exp(TOP))
+            mm([(X("PA", 144, 152), PM, X("SB", 16 * j + y, 16 * j + 16, 2), j + y == 0, False) for j in range(2) for y in range(2)]
+               + [(X("PA", 144, 152), PM2, X("SB", 32, 40), False, True)])
             LW = X("TU", 136, 144)
-            lv = (-1.0 / WB, A.mult, 128.375, A.add)
-            ts(SI(64), X("PA", 64, 72), *lv)
-            ts(LW, X("PA", 64, 72), *lv)
-            m0 = MW * t
-            HL = X("MO", m0 + 128, m0 + 136)
-            ts(HL, X("PA", 64, 72), -127.5 * WB, A.is_gt)
-            cp(TB(10), IND(X("DD", 0, 2048), FO), "act")
-            mm([(X("PB", 128 + 128 * h, 256 + 128 * h), SEL[h], TB(10), True, True) for h in range(2)])
-            cp(X("DF", 0, 256), X("PB", 128, 384), "act")
-            GG = X("MO", m0, m0 + 128)
-            cp(GG, IND(X("DF", 0, 272), LW), "act")
+            ts(LW, X("PA", 144, 152), -1.0 / WB, A.mult, 191.125, A.add)
+            step("flag")
+            HL, GG = X("MO", m0 + 128, m0 + 136), X("MO", m0, m0 + 128)
+            ts(HL, X("PA", 144, 152), -64.5 * WB, A.is_gt)
+            step("df")
+            cp(TB(8), IND(DD, FO), "act")
+            mm([(X("PB", 128 * h, 128 + 128 * h), SEL[h], TB(8), True, True) for h in range(2)])
+            cp(X("DF", 0, 256), X("PB", 0, 256), "act")
+            step("dm")
+            cp(GG, IND(X("DF", 0, CW), LW), "act")
             send(X("ML", m0, m0 + 136), X("MO", m0, m0 + 136), "r0_%d_%d" % (b, t))
-            tt(TB(8), IND(SI(56), LB), MA, A.mult)
-            mm([(X("PC", 0, 8), TB(8), PS1, True, True)])
-            MLs = X("TU", 144, 152)
-            cp(MLs, X("PC", 0, 8))
-            tt(TB(9), IND(SI(64), LB), MA, A.mult)
-            mm([(X("PA", 128 + h, 384, 2), BO[h], TB(9), True, True) for h in range(2)])
-            cp(X("LO", 0, 256), X("PA", 128, 384), "act")
-            AC = TB(11)
-            tt(AC, IND(X("LO", 0, 256), MLs), RC, A.is_equal)
-            cp(TF(5), IND(SC, LK), "act")
-            mm([(X("PB", 0, 128), TF(5), I32, True, True)])
-            ts(TI(2), X("PB", 0, 128), 16.0, A.add)
-            ts(TI(3), TI(2), 4, A.arith_shift_right, 1023, A.bitwise_and)
-            ts(TI(4), TI(2), 15, A.bitwise_and)
-            cp(Sa, TI(3))
-            tt(TF(7), TI(4), Si, A.mult)
-            act(TF(8), Sa, F.Identity, 0.0, PFc(ca))
-            tt(TI(5), X("PD", 256, 384), TF(7), A.subtract)
-            tt(TI(6), X("PD", 384, 512), TF(8), A.add)
-            ts(TI(7, 256), TI(5, 256), 4095, A.bitwise_and)
-            tt(TI(11), IND(X("AD", 0, 2048), FO), Zi, A.add)
-            ts(TI(10), TI(11), 1, A.arith_shift_right)
-            ts(TI(9), Zi, -1.0, A.add, 0.0, A.max)
-            mm([(X("PA", 16, 24), I16, R("KS", 64, 72), True, False)])
-            mm([(X("PA", 16, 24), R("KB", J128[1] + 15 - k, J128[1] + 143 - k), R(AC[0], AC[1] + k, AC[2], 16), False, k == 15) for k in range(16)])
-            SA = X("TU", 168, 176)
-            ts(SA, X("PA", 16, 24), PFc(ca), A.add)
-            n0 = SW * (t + 1)
+            step("future")
+            XD = SF(64, 24)
+            ts(SI(40), SI(0), 4, A.arith_shift_right, 1023, A.bitwise_and)
+            tt(SF(64), SI(8), Si, A.mult)
+            tt(SF(72), SI(40), Si, A.subtract)
+            mm([(X("PC", 0, 128, 1, 32, 48), SF(64, 16), I32, True, True)])
+            cp(X("TT", 0, 128, 1, 32, 48), X("PC", 0, 128, 1, 32, 48), "act")
+            for j, m in enumerate((REN, REA)):
+                mm([(X("PC", 128 + 128 * j, 256 + 128 * j), P(m, 0, 48), T48, True, True)])
+            act(TB(9, 256), X("PC", 128, 384), F.Identity, BIG - 2047.5)
+            tt(TF(6, 256), X("PC", 128, 384), TB(9, 256), A.subtract)
+            step("fired")
+            mm([(X("PD", 144, 152), I16 if last else I16x, C(UF, y, 64, 8), y == 0, y == 7) for y in range(8)])
+            step("za")
+            tt(TF(2), IND(AD, FO), ZQ, A.add)
+            step("acts")
+            MK = X("MK", CW * t, CW * t + CW)
+            cp(IND(MK, LW), ONES)
+            mm([(X("PA", 160, 176), I16, C16h, True, False)]
+               + [(X("PA", 160, 176), C(J2, 64 - k, 192 - k), C(MK, k, 256, 16), False, k == 15) for k in range(16)])
+            SA = X("TU", 144, 152)
+            for h in range(2):
+                ts(P(SA, 64 * h, 64 * h + 64), X("PA", 160 + 8 * h, 168 + 8 * h, 1, 64 * h, 64 * h + 64), P(PFc(ca), 64 * h, 64 * h + 64), A.add)
             if not last:
-                cp(X("EO", e0 + 128, e0 + 256), IND(TI(7, 256), SA))
+                ts(X("EO", e0 + 128, e0 + 256), IND(TF(6, 256), SA), BIG, A.add)
                 send(X("EU", e0 + 128, e0 + 256), X("EO", e0 + 128, e0 + 256), "r1_%d_%d" % (b, t))
             else:
-                cp(TF(1), IND(TI(7, 256), SA))
-            cp(TF(2) if last else X("SO", n0 + 136, n0 + 264), IND(X("ST", s0 + 136, s0 + 392), SA), "act")
-            cp(X("ZB", 0, 128) if last else X("SO", n0 + 8, n0 + 136), IND(TI(9, 256), SA))
+                ts(TF(8), IND(TF(6, 256), SA), BIG, A.add)
+                step("end")
+                fill(SF(80), -1)
+            step("state")
+            mm(([] if last else [(X("PB", 256, 280), I16, CA24, True, False)])
+               + [(X("PB", 256, 280), C(MK, 128 * h, 128 * h + 128), AR[h], last and h == 0, h == 1) for h in range(2)])
+            tt(SF(96, 24), X("PB", 256, 280), XD, A.mult)
+            tt(SF(128, 24) if last else X("SO", n0, n0 + 24), X("PD", 128, 152), SF(96, 24), A.subtract)
+            ts(X("ZB", 0, 128) if last else X("SO", n0 + 24, n0 + 152), IND(ZW, SA), ONE, A.add, -ONE, A.add)
             if not last:
-                mm([(X("PC", 8, 16), N4, NF, True, False), (X("PC", 8, 16), AC, NS2, False, True)])
-                ts(X("SO", n0, n0 + 8), X("PC", 8, 16), 1792.0, A.add)
-                send(X("ST", n0, n0 + 264), X("SO", n0, n0 + 264), "r2_%d_%d" % (b, t))
+                send(X("ST", n0, n0 + 152), X("SO", n0, n0 + 152), "r2_%d_%d" % (b, t))
             else:
-                mm([(X("PC", 128, 256), BK, TB(2), True, True)])
-                ts(TF(3), X("PC", 128, 256), 8.5, A.is_ge)
-                tt(TF(3), TF(3), AC, A.subtract)
+                mm([(X("PC", 0, 128, 1, 0, 16), SF(136, 16), I32, True, True)])
+                cp(P(TF(9), 0, 16), X("PC", 0, 128, 1, 0, 16), "act")
                 for h in range(2):
-                    for j, (y, src) in enumerate((("yc", TF(1)), ("ys", TF(2)), ("ya", TF(3)))):
-                        q = "sp" if (h + j) % 2 else "act"
-                        dma(q, R(y, 128 * h, 128 * h + 128, 1, 4 * b, 4 * b + 4), R(src[0], src[1], src[2], 1, 64 * h, 64 * h + 64, 16), 2, osem[q])
+                    y = lambda nme: R(nme, 128 * h, 128 * h + 128, 1, 4 * b, 4 * b + 4)
+                    dma("act", y("yc"), P(TF(8), 64 * h, 64 * h + 64, 16), 2, osem["act"])
+                    dma("sp", y("ys"), P(TF(9), 4 * h, 4 * h + 4), 2, osem["sp"])
+                    dma("act", y("ya"), P(TF(9), 8 + 4 * h, 12 + 4 * h), 2, osem["act"])
                     dma("sp", R("yz", 128 * h, 128 * h + 128, 1, 64 * b, 64 * b + 64), X("ZB", 0, 128, 1, 64 * h, 64 * h + 64), 16, osem["sp"])
+            step("slot")
             GR, HR = X("ML", m0, m0 + 128), X("ML", m0 + 128, m0 + 136)
-            mm([(X("PC", 256, 272), I16, C16, True, False)] + [(X("PC", 256 + y, 272, 2), LY[0][y], HL, False, False) for y in range(2)]
-               + [(X("PC", 256 + y, 272, 2), LY[1][y], HR, False, y == 1) for y in range(2)])
+            o = X("PB", 288, 304)
+            mm([(o, I16, C16, True, False)] + [(C(o, y, 16, 2), LY[0][y], HL, False, False) for y in range(2)]
+               + [(C(o, y, 16, 2), LY[1][y], HR, False, y == 1) for y in range(2)])
             SL = X("TU", 152, 168)
-            ts(SL, X("PC", 256, 272), PFc(ca), A.add)
-            cp(X("WN", *blk), IND(X("CN", 0, 512), SL), "act")
-            mm([(X("PB", 0, 256), I16, X(CO, 256, 512), True, False), (X("PB", 0, 256, 2), SEL[0], GG, False, False)])
-            mm([(X("PB", 1, 256, 2), SEL[1], GR, False, True)])
-            cp(X("WO", *blk), IND(X(CO, 0, 512), SL), "act")
-            ts(X(CV, 256, 512), X("PB", 0, 256), 0.0, A.max, 255.0, A.min)
-            cp(X("WV", *blk), IND(X(CV, 0, 512), SL), "act" if not last else "dve")
-            if t >= VIS - 2:
-                a, e = (0, 256 * t + 256) if not last else blk
-                kb = (e - a) // 8
-                dma("g", R("yn", a, e, 1, 4 * b, 4 * b + 4), X("WN", a, e, 1, 0, 64, 16), kb // 8, osem["g"])
-                dma("act" if last else "sp", R("yo", a, e, 1, 64 * b, 64 * b + 64), X("WO", a, e, 1, 0, 64), kb, osem["act" if last else "sp"])
-                dma("sp", R("yv", a, e, 1, 64 * b, 64 * b + 64), X("WV", a, e, 1, 0, 64), kb, osem["sp"])
-                if last:
-                    dma("sp", R("yx", 0, 256, 1, 64 * b, 64 * b + 64), X(CV, 256, 512, 1, 0, 64), 32, osem["sp"])
+            ts(SL, o, PFc(ca), A.add)
+            if not last:
+                cp(X("WO", *blk), IND(X(CO, 0, 512), SL), "act")
+            step("object")
+            o = X("PD", 256, 384)
+            mm([(o, I16, Xo, True, False), (o, IH[0], GG, False, False), (o, IH[1], GR, False, True)])
+            ts(Xn, o, 0.0, A.max, 255.0, A.min)
+            rows = (1, 64 * b, 64 * b + 64)
+            if not last:
+                spread(b, Xn, X(CV, 256, 512))
+                cp(X("WV", *blk), IND(X(CV, 0, 512), SL), "act")
+            else:
+                o = X("PD", 256, 512)
+                mm([(P(C(o, y, 256, 2), 64 * h, 64 * h + 64), C(SEL[y], 0, 64), src, True, True) for h, src in enumerate((Xo, Xn)) for y in range(2)])
+                cp(X("W5", 256, 512), o, "act")
+                cp(X("W5", 512, 768), IND(X("W5", 0, 512), SL), "act")
+                cp(X("YN", 0, 256), IND(X("N5", 0, 512), SL))
+                dma("sp", R("yx", 0, 256, *rows), X("W5", 256, 512, 1, 64, 128), 32, osem["sp"])
+                dma("act", R("yo", blk[0], blk[1], *rows), X("W5", 512, 768, 1, 0, 64), 32, osem["act"])
+                dma("sp", R("yv", blk[0], blk[1], *rows), X("W5", 512, 768, 1, 64, 128), 32, osem["sp"])
+                dma("sp", R("yn", blk[0], blk[1], 1, 4 * b, 4 * b + 4), X("YN", 0, 256, 1, 0, 64, 16), 4, osem["sp"])
+            if t == VIS - 2:
+                step("out")
+                e = blk[1]
+                for h, (w, y) in enumerate((("WO", "yo"), ("WV", "yv"))):
+                    dma("g", R(y, 0, e, *rows), X(w, 0, e, 1, 0, 64), e // 8)
+                    dma("sp", X("DX", 0, 80, 1, 64 * h, 64 * h + 64), X(w, 0, e, 1, 0, 64, 16), 20)
+                act(X("DY", 0, 80), X("DX", 0, 80), F.Identity, -127.5)
+                tt(X("DY", 80, 160), X("DX", 0, 80), X("DY", 0, 80), A.subtract)
+                ts(X("DX", 80, 160), X("DY", 0, 80), 0.0, A.is_lt, 257.0, A.mult)
+                act(X("DX", 160, 240), X("DY", 0, 80), F.Identity, -1.0, 1.0 / 256)
+                tt(X("DX", 240, 320), X("DX", 80, 160), X("DX", 160, 240), A.add)
+                for h, y in enumerate(("yo", "yv")):
+                    dma("sp", R(y, 0, e, 1, 64 * b, 64 * b + 64, 16), X("DY", 80, 160, 1, 64 * h, 64 * h + 64), 10, osem["sp"])
+                dma("sp", R("yn", 0, e, 1, 4 * b, 4 * b + 4), X("DX", 240, 320, 1, 0, 64), 20, osem["sp"])
+    for a, e in zip(seq, seq[1:]):
+        ops[e]["behind"] = a
     return ops
 
 
@@ -462,20 +570,20 @@ def overlap(a, b):
     return a[1] < b[2] and b[1] < a[2] and a[4] < b[5] and b[4] < a[5]
 
 
-def plan():
-    ops = build()
+def plan(par=PAR):
+    ops = build(par)
     n = len(ops)
     hist = {}
     dep = [set() for _ in ops]
     for i, o in enumerate(ops):
-        acc = [(r, psum(r)) for r in o["reads"]] + [(r, True) for r in o["writes"]]
+        acc = [(r, False) for r in o["reads"]] + [(r, True) for r in o["writes"]]
         for r, wr in acc:
             for (j, r2, w2) in hist.get(r[0], ()):
-                if j != i and (wr or w2) and overlap(r, r2):
+                if j != i and (wr or w2 or (psum(r) and ops[j]["eng"] != o["eng"])) and overlap(r, r2):
                     dep[i].add(j)
         for r, wr in acc:
             h = hist.setdefault(r[0], [])
-            if wr and r[3] == 1 and r[6] == 1:
+            if wr and (psum(r) or (r[3] == 1 and r[6] == 1)):
                 h[:] = [x for x in h if not (psum(r) or (r[1] <= x[1][1] and x[1][2] <= r[2] and r[4] <= x[1][4] and x[1][5] <= r[5]))]
             h.append((i, r, wr))
         if o["recv"]:
@@ -488,31 +596,34 @@ def plan():
     tail = [0.0] * n
     for i in range(n - 1, -1, -1):
         o = ops[i]
-        tail[i] = o["dur"] + o["lat"] + o.get("kb", 0) * 0.006 + max([tail[j] + HOP for j in succ[i]] or [0.0])
+        tail[i] = o["dur"] + o["lat"] + o.get("kb", 0) * 0.006 + max([tail[j] + par["HOP"] for j in succ[i]] or [0.0])
     return ops, dep, succ, behind, tail
 
 
-def arrange(ops, dep, succ, behind, tail, nudge):
+def arrange(ops, dep, succ, behind, tail, nudge, hop=PAR["HOP"]):
     n = len(ops)
-    tail = [tail[i] + nudge.get(ops[i]["kind"], 0.0) for i in range(n)]
+    tail = [tail[i] + nudge.get(ops[i]["kind"], 0.0) + ops[i]["bias"] for i in range(n)]
     free = dict((e, 0.0) for e in ENG + ("none",))
     bus = [0.0]
     left = [len(d) + ("behind" in o) for d, o in zip(dep, ops)]
-    ready = dict((i, 0.0) for i in range(n) if not left[i])
+    ready = dict((e, {}) for e in free)
+    for i in range(n):
+        if not left[i]:
+            ready[ops[i]["eng"]][i] = 0.0
     order, fin, start = [], [0.0] * n, [0.0] * n
-    while ready:
+    while len(order) < n:
         best = None
         for e in free:
-            c = [i for i in ready if ops[i]["eng"] == e]
+            c = ready[e]
             if not c:
                 continue
-            t0 = max(free[e], min(ready[i] for i in c))
-            pick = max((i for i in c if ready[i] <= t0 + LOOK), key=lambda i: (tail[i] + ops[i]["bias"], -i))
+            t0 = max(free[e], min(c.values()))
             if best is None or t0 < best[0]:
-                best = (t0, pick)
-        i = best[1]
+                best = (t0, e)
+        c = ready[best[1]]
+        i = max((i for i in c if c[i] <= best[0] + LOOK), key=lambda i: (tail[i], -i))
         o = ops[i]
-        t0 = max(free[o["eng"]], ready.pop(i))
+        t0 = max(free[o["eng"]], c.pop(i))
         start[i] = t0
         free[o["eng"]] = t0 + o["dur"]
         f = t0 + o["dur"] + o["lat"]
@@ -524,13 +635,97 @@ def arrange(ops, dep, succ, behind, tail, nudge):
         for j in succ[i] + ([behind[i]] if i in behind else []):
             left[j] -= 1
             if not left[j]:
-                ready[j] = max([fin[k] + (0.0 if ops[k]["eng"] == "pe" == ops[j]["eng"] or ops[j]["recv"] else HOP) for k in dep[j]] + [t0])
+                ready[ops[j]["eng"]][j] = max([fin[k] + (0.0 if ops[k]["eng"] == "pe" == ops[j]["eng"] or ops[j]["recv"] else hop) for k in dep[j]] + [t0])
     return ops, dep, order, start, fin
 
 
-NUDGE = {105: 6, 228: -0.5, 1110: -1.5, 293: 3, 1092: 6, 22: -3, 257: -1.0, 58: -4.0, 20: 3, 216: 3, 82: 3, 42: -1.5, 1104: -6, 12: -0.5, 55: -1.5, 271: -3, 92: 3, 303: -6, 260: 0.5, 4: -6.0, 314: 1.5, 278: -0.5, 210: -0.5, 91: 1.5, 99: -3, 272: 3, 65: 6, 62: -3, 61: -1.5, 19: -0.5, 44: -4.5, 234: -1.5, 240: 3, 270: 6, 306: -3, 236: 0.5, 67: 0.5, 1137: -3, 57: -0.5, 115: -3, 15: -1.5, 267: -3.0, 215: -3, 47: 3, 48: 0.5, 218: -0.5, 211: 0.5, 268: 1.5, 283: -0.5, 93: 0.5, 247: 7.5, 46: 0.5, 106: -3, 281: -1.5, 14: 0.5, 110: 3, 1007: 6, 21: 6, 274: 3, 205: -0.5, 60: 3, 26: -6, 316: -0.5, 319: 0.5, 207: 0.5, 109: -1.5, 1132: -6, 33: -0.5, 41: 3, 232: -3, 122: 0.5, 71: 1.5, 1166: -1.5, 286: 0.5, 13: 3, 43: 3, 1003: 1.5, 29: -0.5}
+def ranked(key, pre, suc):
+    left = [len(p) for p in pre]
+    ready = sorted(((key[i], i) for i in range(len(pre)) if not left[i]), reverse=True)
+    out = []
+    while ready:
+        i = ready.pop()[1]
+        out.append(i)
+        for j, _ in suc[i]:
+            left[j] -= 1
+            if not left[j]:
+                ready.append((key[j], j))
+        ready.sort(reverse=True)
+    return out
+
+
+def place(ops, seq, pre, back):
+    busy, t = {}, [0.0] * len(ops)
+    for j in seq:
+        o = ops[j]
+        d = o["dur"]
+        if back:
+            r = max([t[i] + ops[i]["dur"] + lag - d for i, lag in pre[j]] + [o["lat"] + o.get("kb", 0) * 0.006])
+        else:
+            r = max([t[i] + lag for i, lag in pre[j]] + [0.0])
+        if d:
+            q = busy.setdefault(o["eng"], [])
+            k = len(q)
+            while k and q[k - 1][1] > r:
+                k -= 1
+            while k < len(q) and q[k][0] < r + d - 1e-9:
+                r = max(r, q[k][1])
+                k += 1
+            q.insert(k, (r, r + d))
+        t[j] = r
+    return t
+
+
+def flip(pre):
+    suc = [[] for _ in pre]
+    for j, p in enumerate(pre):
+        for i, lag in p:
+            suc[i].append((j, lag))
+    return suc
+
+
+def lay(ops, dep, cycle, hop):
+    n = len(ops)
+    pre = [[(i, ops[i]["dur"] + ops[i]["lat"] + ops[i].get("kb", 0) * 0.006 + (0.0 if ops[i]["eng"] == "pe" == o["eng"] or o["recv"] else hop))
+            for i in dep[j]] + ([(o["behind"], max(0.1, ops[o["behind"]]["kb"] * 0.006))] if "behind" in o else []) for j, o in enumerate(ops)]
+    suc = flip(pre)
+    rank = dict((w.split("/")[0], (int(w.split("/")[1]), a)) for x in cycle.values() for a, w in enumerate(x.split()))
+    known = set(i for i, o in enumerate(ops) if o["t"] >= 0 and o["pos"] in rank and (o["t"] < VIS - 1 or o["kind"] not in ("state", "object", "slot", "old")))
+    queue = {}
+    for i in known:
+        o = ops[i]
+        queue.setdefault(o["eng"], []).append((2 * o["t"] + o["b"] + rank[o["pos"]][0], rank[o["pos"]][1], i))
+    known |= set(i for i, o in enumerate(ops) if o["recv"] and o["after"] in known)
+    p2 = [[(j, lag) for j, lag in pre[i] if j in known] if i in known else [] for i in range(n)]
+    for q in queue.values():
+        q.sort()
+        for a, b in zip(q, q[1:]):
+            p2[b[2]].append((a[2], ops[a[2]]["dur"]))
+    key = [None] * n
+    for j in ranked(range(n), p2, flip(p2)):
+        if j in known:
+            key[j] = max([key[i] + lag for i, lag in p2[j]] + [0.0])
+    for j in range(n - 1, -1, -1):
+        if key[j] is None and ops[j]["t"] < 0:
+            key[j] = min([key[i] - lag for i, lag in suc[j] if key[i] is not None] or [None])
+    for j in ranked(range(n), pre, suc):
+        if key[j] is None:
+            key[j] = max([key[i] + lag for i, lag in pre[j]] + [0.0])
+    t = place(ops, ranked(key, pre, suc), pre, False)
+    for _ in range(2):
+        t = place(ops, ranked([-t[i] - o["dur"] for i, o in enumerate(ops)], suc, pre), suc, True)
+        t = place(ops, ranked([-t[i] - o["dur"] for i, o in enumerate(ops)], pre, suc), pre, False)
+    return ops, dep, ranked(t, pre, suc), t, [t[i] + o["dur"] + o["lat"] for i, o in enumerate(ops)]
+
+
+CYCLE = dict(
+    pe="name0.2/1 name0.3/1 rows.0/1 name1.0/1 name0.5/1 pick.4/2 rows.1/1 name1.1/1 name1.2/1 claim.0/2 name0.7/1 name1.3/1 future.3/2 claim.4/2 claim.5/2 last0.0/1 name1.5/1 df.1/2 claim.8/2 future.5/2 future.6/2 name1.7/1 acts.1/2 state.0/2 last1.0/1 fired.0/2 slot.0/2 object.0/2 base.0/1 head.0/1 abs0.1/1 object.2/2 turn.0/0 name0.0/0 abs1.1/1 name0.1/0 abs2.1/1 abs3.1/1",
+    dve="pick.0/2 pick.1/2 mark.0/2 pick.2/2 pick.3/2 mark.2/2 future.0/2 mark.4/2 mark.3/2 pick.5/2 future.2/2 mark.5/2 pick.6/2 future.1/2 mark.6/2 claim.1/2 claim.3/2 claim.2/2 eq0.0/1 claim.6/2 za.0/2 last0.2/1 claim.9/2 last0.3/1 flag.0/2 acts.0/2 last0.4/1 eq1.0/1 future.8/2 acts.2/2 acts.3/2 state.1/2 last0.5/1 acts.4/2 state.2/2 last1.2/1 state.3/2 last1.3/1 V0.0/1 last1.4/1 slot.1/2 V1.0/1 last1.5/1 object.1/2 V2.0/1 V3.0/1 O1.0/0",
+    sp="old.1/0 old.0/1",
+    act="name0.4/1 mark.1/2 O3.0/1 name0.6/1 df.0/2 name1.4/1 future.4/2 claim.7/2 last0.1/1 df.2/2 name1.6/1 dm.0/2 zq.1/1 future.7/2 object.3/3 object.4/3 last1.1/1 zq.0/1 abs0.0/1 slot.2/2 abs1.0/1 O0.0/0 abs2.0/1 abs3.0/1 turn.1/0 O2.0/0",
+    g="dm.1/2 acts.5/2 state.4/2")
 GRAPH = plan()
-PLAN = arrange(*GRAPH, NUDGE)
+PLAN = lay(GRAPH[0], GRAPH[1], CYCLE, PAR["HOP"])
 
 
 def rank_program(g, core, T, topo):
@@ -601,6 +796,8 @@ def rank_program(g, core, T, topo):
                 ins = q.iota(ap(c[1]), c[2], c[3], c[4])
             else:
                 ins = q.iota(ap(c[1]), c[2], c[3], c[4], allow_small_or_imprecise_dtypes=True)
+        elif k == "as":
+            ins = q.affine_select(ap(c[1]), ap(c[1]), c[2], c[3], c[4], c[5], c[6])
         elif k == "scan":
             ins = q.tensor_tensor_scan(ap(c[1]), ap(c[2]), ap(c[3]), 0.0, A.add, A.max)
         elif k == "dma":

@@ -8,17 +8,17 @@ SCRATCH = {}
 for _b in range(NB):
     for _n, _w, _d in (("DA", 4096, BF), ("GV", 4096, BF), ("WO", 4096, FP), ("WV", 4096, FP), ("OG", 2048, FP),
                        ("EQ", 1024, BF), ("ST", VIS * SW, FP), ("SO", VIS * SW, FP),
-                       ("EU", VIS * 128, U2), ("EO", VIS * 128, U2), ("ML", VIS * MW, BF), ("MO", VIS * MW, BF),
+                       ("ZI", VIS * 128, BF), ("ZO", VIS * 128, BF), ("EU", VIS * 128, U2), ("EO", VIS * 128, U2), ("ML", VIS * MW, BF), ("MO", VIS * MW, BF),
                        ("CA", 512, FP), ("CB", 512, FP), ("W5", 768, BF), ("N5", 512, I3), ("YN", 256, FP),
-                       ("DF", CW, BF), ("MK", VIS * CW, BF), ("XP", 256, BF), ("XS", 256, BF), ("TT", 128, FP),
-                       ("TF", 10 * 128, FP), ("TI", 2 * 128, I3), ("TB", 12 * 128, BF), ("TU", 256, U2),
-                       ("SF", 192, FP), ("SI", 64, I3), ("SB", 64, BF), ("ZB", 128, BF), ("CS", 128, I3),
+                       ("DF", CW, BF), ("MK", VIS * CW, BF), ("XP", 256, BF), ("XS", 256, BF), ("TT", 128, FP), ("TH", 128, BF), ("HB", 64, BF),
+                       ("TF", 10 * 128, FP), ("TI", 2 * 128, I3), ("TB", 12 * 128, BF), ("TU", 384, U2),
+                       ("SF", 192, FP), ("SI", 64, I3), ("SB", 64, BF), ("CS", 128, I3),
                        ("DX", 320, FP), ("DY", 160, BF)):
         SCRATCH["%s%d" % (_n, _b)] = ("sbuf", [128, _w], _d)
     for _n in "ABCD":
         SCRATCH["P%s%d" % (_n, _b)] = ("psum", [128, 512], FP)
-for _n, _w, _d in (("NI", 512, I3), ("NW", 1024, FP), ("NH", 512, BF), ("PI", 64, I3), ("PF", 128, FP), ("KB", 52 * 128, BF),
-                   ("KF", 10 * 128, FP), ("KS", 256, BF), ("OI", 80, FP), ("OU", 80, U2)):
+for _n, _w, _d in (("NI", 512, I3), ("NW", 1024, FP), ("NH", 512, BF), ("PI", 64, I3), ("PF", 128, FP), ("KB", 59 * 128, BF),
+                   ("KF", 2 * 128, FP), ("KS", 256, BF), ("OI", 80, FP), ("OU", 80, U2)):
     SCRATCH[_n] = ("sbuf", [128, _w], _d)
 OUTS = ("yn", "yo", "yv", "yx", "yc", "ys", "ya", "yz")
 ENG = ("g", "pe", "dve", "act", "sp")
@@ -28,14 +28,20 @@ SEMAPHORES = ["c_" + e for e in ENG] + ["d%d" % i for i in range(NDS)] + ["sent"
 LN2 = math.log(2.0)
 TOP = 41.5
 WB = 2 * TOP / 64
+W1 = 185.0 / 1024
 BIG = 786432.0
 ONE, W32 = 1.5 * 2 ** 23, 1.5 * 2 ** 28
-PAR = dict(HOP=0.12, GC=1.56, SC=3.8, CY=0.00083, PC=0.00042, RI=0.4, RL=1.8)
+PAR = dict(HOP=0.2, GC=1.3, SC=3.8, CY=0.00083, PC=0.00042, RI=0.4, RL=1.7, FX=0.015, PX=0.0)
 LOOK = 0.05
 LEAD = 4.0
-OQ = ("act", "dve", "act", "act")
+OQ = (32, 0, 0, 0)
 VP = (32, 32, 32, 32)
 LOGQ = dict(WO0=("dve", "act") * 4, WV0=("dve", "act") * 4, WO1=("dve", "act") * 4, WV1=("dve", "act") * 4)
+LOGB = dict(WO0=("PA0", "PD0", "PA1", "PB1", "PD1"), WV0=("PA1", "PB1", "PD1"), WO1=("PA1", "PD1", "PB1"), WV1=("PD1",))
+PEMOD, SQ, SPEC = (), "act", True
+HQ, SP = "act", ((0, 96), (96, 128))
+FUT, MERGE = True, 0
+BYG = ("WV1",)
 NUDGE = {}
 
 
@@ -105,7 +111,7 @@ def build(par=PAR):
             return 0.06 + n * GC * CY
         if mul == 1.0 and two(out) and all(two(i) for i in ins):
             mul = 0.5
-        return 0.03 + max(64, n * mul) * CY
+        return par["FX"] + max(64, n * mul) * CY
 
     def ts(out, a, s1, o0, s2=None, o1=None):
         return add("dve", ("ts", out, a, s1, s2, o0, o1), [a, s1, s2], [out], cost(out, [a]))
@@ -125,7 +131,7 @@ def build(par=PAR):
     def mm(lst):
         d, rd, wr = 0.0, [], []
         for (o, l, r, st, sp) in lst:
-            d += max(min(64, n_of(l)), n_of(r)) * (1 if two(l) else 4) * PC
+            d += max(min(64, n_of(l)), n_of(r)) * (1 if two(l) else 4) * PC + par["PX"]
             rd += [l, r]
             wr.append(o)
         return add("pe", ("mm", lst), rd, wr, 0.03 + d)
@@ -136,8 +142,8 @@ def build(par=PAR):
     def iota(out, pat, base=0, cm=0):
         return add("g", ("io", out, pat, base, cm), [], [out], 0.13 + 2 * n_of(out) * CY)
 
-    def asel(out, pat, op, fill, base, cm):
-        return add("g", ("as", out, pat, op, fill, base, cm), [out], [out], 0.17 + 2 * n_of(out) * CY)
+    def asel(out, pat, op, fill, base, cm, a=None):
+        return add("g", ("as", out, pat, op, fill, base, cm, a or out), [a or out], [out], 0.17 + 2 * n_of(out) * CY)
 
     nds = [0]
 
@@ -174,11 +180,17 @@ def build(par=PAR):
     act(R("NH", 0, 256), R("NW", 512, 768), F.Identity, 256.0, 256.0)
     for b in range(NB):
         for w, nme in (("DA", "vo"), ("GV", "vn")):
+            if w == "GV" and "WV%d" % b in BYG:
+                for c in range(2):
+                    for h in range(2):
+                        seq.append(dma("sp", R("GV%d" % b, 2048 * c, 2048 * c + 2048, 1, 64 * h, 64 * h + 64),
+                                       R(nme, 2048 * c, 2048 * c + 2048, 1, 64 * b, 64 * b + 64), 256))
+                continue
             for c in range(2):
                 seq.append(dma("sp", R("%s%d" % (w, b), 2048 * c, 2048 * c + 2048, 1, 0, 64), R(nme, 2048 * c, 2048 * c + 2048, 1, 64 * b, 64 * b + 64), 256))
             seq.append(dma("sp", R("%s%d" % (w, b), 0, 4096, 1, 64, 68), R("NH", 0, 256, 1, 64 * b, 64 * b + 64), 32))
         for h in range(2):
-            seq.append(dma("sp", R("ZB%d" % b, 0, 128, 1, 64 * h, 64 * h + 64), R("z0", 128 * h, 128 * h + 128, 1, 64 * b, 64 * b + 64), 16))
+            seq.append(dma("sp", R("ZI%d" % b, 0, 128, 1, 64 * h, 64 * h + 64), R("z0", 128 * h, 128 * h + 128, 1, 64 * b, 64 * b + 64), 16))
         seq.append(dma("sp", R("XS%d" % b, 0, 256, 1, 0, 64), R("xo", 0, 256, 1, 64 * b, 64 * b + 64), 32))
 
     cP, ca, cg8, ch, cg, c64, ca8, ca7, cq, cr, ck = range(11)
@@ -193,29 +205,35 @@ def build(par=PAR):
     iota(G8, [[1, 8], [0, 16]])
     M64 = C(M64, 0, 128)
     DUP, I16, MA, I16x, PM, PM2 = K(6), K(7), K(8), K(9), K(10), K(11)
-    I32, I32x, D0, MSK, RE0, REP, RSP, REN, REA, TMP = (KF(j) for j in range(10))
+    I32, D0, MSK = KF(0), KF(1), K(58)
     ts(PFc(ct1), PFc(cP), -64.0, A.add, 0.0, A.max)
     ts(PFc(ct1), PFc(ct1), 15.0, A.mult, PFc(c64), A.add)
     ts(DUP, M64, PFc(ct1), A.is_equal)
     ts(PFc(cz), PFc(ca), 0.0, A.is_equal)
     ts(MSK, G8, PFc(ca7), A.is_equal)
-    f0, f1, f4, f5 = (PFc(96 + j) for j in range(4))
-    for f, v in ((f0, 0.0), (f1, 1.0), (f4, 4.0), (f5, 5.0)):
-        ts(f, PFc(ck), v, A.is_equal)
     lin = lambda out, a, scale, bias=0.0: act(out, a, F.Identity, bias, scale)
-    lin(PFc(100), f1, 7.5 - 0.000354, f0)
-    lin(PFc(101), f1, 16.0, f0)
-    lin(PFc(102), f4, -1.0, PFc(101))
-    lin(PFc(103), f5, 1.0, f1)
-    lin(PFc(104), f1, 1.0 / (8 * LN2))
-    for m, al, be in ((RE0, f0, f1), (REP, PFc(100), f1), (REN, PFc(102), f1), (REA, PFc(101), PFc(103))):
+    lin(PFc(cna8), PFc(ca8), -1.0, 1.0)
+    c0, s0, s1, f2, d2, aP, aS, a16, aN, bA = (PFc(80 + j) for j in range(10))
+    for f, v, fl in ((c0, 0.0, cna8), (s0, 0.0, ca8), (s1, 1.0, ca8), (f2, 2.0, cna8), (d2, 2.0, ca8)):
+        ts(f, PFc(cq), v, A.is_equal, PFc(fl), A.mult)
+    lin(aP, s0, 7.5, c0)
+    lin(aP, s1, -0.000354, aP)
+    lin(aS, s0, W1)
+    lin(aS, s1, 1.0 / (8 * LN2) - W1, aS)
+    lin(a16, s0, 16.0, c0)
+    lin(aN, f2, -1.0, a16)
+    lin(bA, d2, 1.0, s0)
+    RE0, REP, RSP, REN, REA, I16y = (K(52 + j) for j in range(6))
+    for m, al, be in ((RE0, c0, s0), (REP, aP, s0), (REN, aN, s0), (REA, a16, bA)):
         lin(m, M16, be, al)
         tt(m, m, MSK, A.mult)
-    lin(RSP, MSK, PFc(104))
+    lin(RSP, MSK, aS)
     ts(I16, IC, PFc(cP), A.is_equal)
     lin(I32, I16, 1.0)
-    lin(I32x, I16, 16.0)
+    lin(I16y, I16, 16.0)
     lin(I16x, I16, 32.0)
+    NI16 = K(51)
+    lin(NI16, I16, -1.0)
     CODE = R("NH", 256, 512)
     lin(PFc(105), PFc(cz), 256.0)
     lin(CODE, R("NW", 768, 1024), PFc(105), PFc(105))
@@ -232,22 +250,24 @@ def build(par=PAR):
 
     for b in range(NB):
         X = lambda nme, a, e, *k: R("%s%d" % (nme, b), a, e, *k)
-        fill(X("TT", 0, 128), 0)
         cp(X("TT", 0, 128, 1, 0, 16), X("CS", 0, 128, 1, 0, 16))
-        mm([(X("PC", 0, 128), P(RE0, 0, 16), X("TT", 0, 128, 1, 0, 16), True, True),
-            (X("PC", 128, 144), X("TT", 0, 128, 1, 0, 16), P(C(I32, 0, 16), 0, 16), True, True)])
-        cp(X("TI", 0, 128), X("PC", 0, 128))
-        ts(X("TI", 128, 256), X("TI", 0, 128), 4095, A.bitwise_and)
-        cp(X("EU", 0, 128), X("TI", 128, 256))
+        mm([(X("PC", 128, 144), X("TT", 0, 128, 1, 0, 16), P(C(I32, 0, 16), 0, 16), True, True)])
         cp(X("ST", 0, 16), X("PC", 128, 144), "act")
         fill(X("ST", 16, 24), 1792)
-        cp(X("ST", 24, 152), X("ZB", 0, 128), "act")
         fill(X("SF", 80, 88), -32)
         fill(X("DF", 256, CW), 0)
-        for w, s, banks in (("WO", "DA", "ABCD"), ("WV", "GV", "CD")):
+        for w, s in (("WO", "DA"), ("WV", "GV")):
             step("log%s%d" % (w, b))
+            if w + str(b) in BYG:
+                for c in range(4):
+                    asel(X(w, 1024 * c, 1024 * c + 1024), [[0, 1024]], A.is_ge, 0.0, 0, 0, X(s, 1024 * c, 1024 * c + 1024))
+                for h in range(2):
+                    i = dma("g", X(w, 0, 4096, 1, 64 * h, 64 * h + 64, 16), R("NH", 0, 256, 1, 64 * b, 64 * b + 64), 128)
+                    ops[i]["call"] = ("acc",) + ops[i]["call"][1:]
+                continue
+            banks = LOGB[w + str(b)]
             for c in range(8):
-                bank = X("P" + banks[c % len(banks)], 0, 512)
+                bank = R(banks[c % len(banks)], 0, 512)
                 mm([(bank, P(DUP, 0, 68), X(s, 512 * c, 512 * c + 512, 1, 0, 68), True, True)])
                 cp(X(w, 512 * c, 512 * c + 512), bank, LOGQ[w + str(b)][c])
         step("start")
@@ -265,8 +285,8 @@ def build(par=PAR):
     ts(tE, PIc(32, 8), PFc(ca), A.min, PFc(cbase), A.add)
     ts(tL, PIc(32, 8), PFc(ca), A.max, PFc(cbase), A.add)
     tt(dl, tL, tE, A.subtract)
-    act(wE, dl, F.Exp, -60 * LN2, 8 * LN2, 1.3)
-    lin(PFc(cna8), PFc(ca8), -1.0, 1.0)
+    act(PFc(cw), PFc(c64), F.Exp, -WB, -WB, 1.3)
+    ops[act(wE, dl, F.Exp, -60 * LN2, 8 * LN2)]["reads"].append(PFc(cw))
     lin(PFc(72, 7), C(wE, 0, 7), 1.0)
     lin(PFc(79), C(wE, 7, 8), PFc(cna8))
     DM = [K(14 + d) for d in range(8)]
@@ -316,14 +336,13 @@ def build(par=PAR):
     iota(IU, [[0, 8], [1, 8]])
     iota(SF64, [[1, 8], [0, 8]])
     ts(SF64, SF64, PFc(cg8), A.is_equal)
-    act(PFc(cw), PFc(c64), F.Exp, -WB, -WB)
     lin(PFc(66), PFc(cw), PFc(cnh))
     lin(PFc(67), PFc(cw), PFc(ch), PFc(cnh))
     IH = [K(49), K(50)]
     for h, fl in ((0, cnh), (1, ch)):
         lin(IH[h], I16, PFc(fl))
     lin(PFc(106), PFc(ca), -WB / 2)
-    act(W4, O(8, 8), F.Exp, PFc(106), -WB / 2)
+    ops[act(W4, O(8, 8), F.Exp, PFc(106), -WB / 2)]["reads"].append(PFc(cw))
     LY = [[K(45), K(46)], [K(47), K(48)]]
     lin(PFc(ct2), PFc(cr), 64.0, PFc(ca))
     lin(PFc(ctp), PFc(cq), 16.0, PFc(ct2))
@@ -354,7 +373,9 @@ def build(par=PAR):
             SI = lambda a, n=8: X("SI", a, a + n)
             SF = lambda a, n=8: X("SF", a, a + n)
             s0, e0, m0, n0 = SW * t, 128 * t, MW * t, SW * (t + 1)
-            CSi, Si, Ai, Zi = X("ST", s0, s0 + 16), X("ST", s0 + 8, s0 + 16), X("ST", s0 + 16, s0 + 24), X("ST", s0 + 24, s0 + 152)
+            CSi, Si, Ai, Zi = X("ST", s0, s0 + 16), X("ST", s0 + 8, s0 + 16), X("ST", s0 + 16, s0 + 24), X("ZI", e0, e0 + 128)
+            if SPEC and t:
+                Zi = X("ST", s0 + 24, s0 + 152)
             now.update(bias=LEAD if b == 0 else 0.0, t=t, b=b, step="", seen={})
             CO, CV = ("CA", "CB") if t % 2 == 0 else ("CB", "CA")
             Xo, Xn = X("XP", 128 * (t % 2), 128 * (t % 2) + 128), X("XP", 128 - 128 * (t % 2), 256 - 128 * (t % 2))
@@ -362,21 +383,28 @@ def build(par=PAR):
             step("old")
             if not last:
                 for c, w in ((CO, "WO"), (CV, "WV")):
-                    dma("sp", X(c, 0, 256), X(w, *blk), 128, csem[b]["AB".index(c[1])])
+                    i = dma("sp", X(c, 0, 256), X(w, *blk), 128, csem[b]["AB".index(c[1])])
+                    seq += [] if t else [i]
             else:
                 for h, nme in enumerate(("vo", "vn")):
                     seq.append(dma("sp", X("W5", 0, 256, 1, 64 * h, 64 * h + 64), R(nme, blk[0], blk[1], 1, 64 * b, 64 * b + 64), 32))
                 dma("sp", X("N5", 0, 256, 1, 0, 64, 16), R("nm", blk[0], blk[1], 1, 4 * b, 4 * b + 4), 4)
             step("turn")
-            T16, T48 = X("TT", 0, 128, 1, 0, 16), X("TT", 0, 128, 1, 0, 48)
-            if t:
-                mm([(X("PC", 0, 128, 1, 0, 16), CSi, I32, True, True)])
-                cp(T16, X("PC", 0, 128, 1, 0, 16), "act")
+            T64, HB = X("TH", 0, 128, 1, 0, 64), lambda a, n: X("HB", a, a + n)
+            cp(HB(0, 16), CSi, HQ)
+            tt(HB(16, 16), CSi, HB(0, 16), A.subtract)
+            mm([(X("PC", 0, 128, 1, 32 * y, 32 * y + 32), HB(0, 32), I16, True, True) for y in range(2)])
+            cp(T64, X("PC", 0, 128, 1, 0, 64), "act")
+            EU = X("EU", e0, e0 + 128)
+            if not (SPEC and t):
+                step("E")
+                o = X("PC", 384, 512)
+                mm([(o, P(RE0, 0, 64), T64, True, True)])
+                act(TB(9), o, F.Identity, BIG - 2047.5)
+                mm([(o, P(RE0, 0, 64), T64, True, False), (o, NI16, TB(9), False, True)])
+                ts(EU, o, BIG, A.add)
             step("rows")
-            mm([(X("PC", 128, 256), P(REP, 0, 16), T16, True, True)])
-            mm([(X("PC", 256, 384), P(RSP, 0, 16), T16, True, True)])
-            step("base")
-            mm([(X("PD", 128, 144), I32, CSi, True, False), (X("PD", 128, 136), I32x, Si, False, True)])
+            mm([(X("PC", 128, 256), P(REP, 0, 64), T64, True, True), (X("PC", 256, 384), P(RSP, 0, 64), T64, True, True)])
             step("zq")
             ZQ, ZW = TF(0), TF(1, 256)
             act(ZQ, Zi, F.Identity, -0.25, 0.5)
@@ -385,7 +413,9 @@ def build(par=PAR):
                 for y in range(2):
                     p = 2 * c + y
                     step("O%d" % p)
-                    cp(X("OG", 512 * p, 512 * p + 512), IND(X("WO", 0, 4096), X("EU", e0 + 32 * p, e0 + 32 * p + 32)), OQ[p])
+                    for a, e, q in ((32 * p, 32 * p + OQ[p], "dve"), (32 * p + OQ[p], 32 * p + 32, "act")):
+                        if a < e:
+                            cp(X("OG", 16 * a, 16 * e), IND(X("WO", 0, 4096), C(EU, a, e)), q)
                     step("name%d" % c)
                     for kk in range(0, 4, 2):
                         mm([(X(bank, 32 * y + 8 * k, 32 * y + 8 * k + 8), X("OG", 512 * p + k, 512 * p + 512, 4), SELN, True, True) for k in (kk, kk + 1)])
@@ -398,13 +428,30 @@ def build(par=PAR):
                 step("eq%d" % c)
                 ts(X("EQ", 512 * c, 512 * c + 512), X(bank, 0, 512), 0.0, A.is_equal)
                 step("last%d" % c)
-                mm([(X(bank, 0, 64), WM[d], X("EQ", 512 * c + d, 512 * c + 512, 8), d == 0, d == 7) for d in range(8)])
+                o = X("PA", 64 * c, 64 * c + 64) if MERGE else X(bank, 0, 64)
+                mm([(o, WM[d], X("EQ", 512 * c + d, 512 * c + 512, 8), d == 0, d == 7) for d in range(8)])
                 h64 = lambda r: C(r, 64 * c, 64 * c + 64)
-                act(h64(TF(3)), X(bank, 0, 64), F.Ln, 2.0 ** -60, 1.0, 1.5 if t + b + c == 0 else 0.0)
+                if MERGE:
+                    if not c:
+                        continue
+                    h64, o = lambda r: r, X("PA", 0, 128)
+                i = act(h64(TF(3)), o, F.Ln, 2.0 ** -60, 1.0, 1.5 if t + b + c == MERGE else 0.0)
+                ops[i]["reads"].append(W4)
                 tt(h64(TF(4)), h64(X("PC", 256, 384)), h64(TF(3)), A.mult)
-                tt(h64(TI(0)), h64(X("PC", 128, 256)), h64(TF(4)), A.add)
-                ts(h64(TI(1)), h64(TI(0)), 4095, A.bitwise_and)
-                cp(h64(X("TU", 0, 128)), h64(TI(1)))
+                if c in PEMOD:
+                    step("mod%d" % c)
+                    x = lambda o, sp: [(o, P(REP, 0, 64), h64(T64), True, False), (o, I32, h64(TF(4)), False, sp)]
+                    mm(x(X(bank, 64, 128), True))
+                    act(h64(TB(11)), X(bank, 64, 128), F.Identity, BIG - 2047.5)
+                    step("mod2")
+                    mm(x(X("PC", 0, 64), False))
+                    step("mod%d" % c)
+                    mm([(X("PC", 0, 64), NI16, h64(TB(11)), False, True)])
+                    ts(h64(X("TU", 0, 128)), X("PC", 0, 64), BIG, A.add)
+                else:
+                    tt(h64(TI(0)), h64(X("PC", 128, 256)), h64(TF(4)), A.add)
+                    ts(h64(TI(1)), h64(TI(0)), 4095, A.bitwise_and)
+                    cp(h64(X("TU", 0, 128)), h64(TI(1)))
             step("head")
             mm([(X("PD", 0, 128), X("EQ", d, 1024, 8), PN[d], d == 0, False) for d in range(8)])
             r0, DD, AD = 0, X("DA", 0, 2048), X("DA", 2048, 4096)
@@ -414,10 +461,10 @@ def build(par=PAR):
                 tt(C(DD, a, e), IND(X("WV", 0, 4096), X("TU", r0, r0 + w)), X("OG", a, e), A.subtract)
                 step("abs%d" % c)
                 act(C(AD, a, e), C(DD, a, e), F.Abs, 0.0, 0.5)
-                for hh in range(r0 // 32, (r0 + w) // 32):
-                    mm([(X("PD", k, 128, 16, 32 * hh, 32 * hh + 32), C(AD, 512 * hh + k, 512 * hh + 512, 16), S64, False, k == 15)
-                        for k in range(16)])
                 r0 += w
+                for a, e in SP:
+                    if r0 - w < e <= r0:
+                        mm([(X("PD", k, 128, 16, a, e), C(AD, 16 * a + k, 16 * e, 16), S64, False, k == 15) for k in range(16)])
             step("pick")
             SC = TF(5)
             add("dve", ("scan", SC, D0, X("PD", 0, 128)), [D0, X("PD", 0, 128)], [SC], 0.03 + 128 * CY)
@@ -430,8 +477,12 @@ def build(par=PAR):
             ts(FO, X("PA", 0, 8), PFc(c16a), A.add)
             tt(TB(3), IND(AD, FO), ZQ, A.is_ge)
             step("mark")
-            ts(SF(0), KEY, W32, A.add, -W32, A.add)
-            act(SF(8), SF(0), F.Square, -3504.0, 1.0 / 32)
+            if SQ == "act":
+                ts(SF(0), KEY, W32, A.add, -W32, A.add)
+                act(SF(8), SF(0), F.Square, -3504.0, 1.0 / 32)
+            else:
+                ts(SI(48), KEY, 1.0 / 32, A.mult, -3504.24, A.add)
+                tt(SF(8), SI(48), SI(48), A.mult)
             tt(SI(16), SF(8), Ai, A.add)
             ts(SI(24), SI(16), 5, A.arith_shift_right, 31, A.bitwise_and)
             ts(SI(32), SI(16), 10, A.arith_shift_right, 7, A.bitwise_and)
@@ -476,48 +527,76 @@ def build(par=PAR):
             ts(SI(40), SI(0), 4, A.arith_shift_right, 1023, A.bitwise_and)
             tt(SF(64), SI(8), Si, A.mult)
             tt(SF(72), SI(40), Si, A.subtract)
-            mm([(X("PC", 0, 128, 1, 32, 48), SF(64, 16), I32, True, True)])
-            cp(X("TT", 0, 128, 1, 32, 48), X("PC", 0, 128, 1, 32, 48), "act")
-            for j, m in enumerate((REN, REA)):
-                mm([(X("PC", 128 + 128 * j, 256 + 128 * j), P(m, 0, 48), T48, True, True)])
-            act(TB(9, 256), X("PC", 128, 384), F.Identity, BIG - 2047.5)
-            tt(TF(6, 256), X("PC", 128, 384), TB(9, 256), A.subtract)
+            spec = SPEC and not last
+            if spec:
+                cp(HB(32, 16), SF(64, 16), HQ)
+                tt(HB(48, 16), SF(64, 16), HB(32, 16), A.subtract)
+                mm([(X("PC", 0, 128, 1, 64, 96), HB(32, 32), I16, True, True)])
+                cp(X("TH", 0, 128, 1, 64, 96), X("PC", 0, 128, 1, 64, 96), "act")
+                mm([(X("PC", 128 + 128 * j, 256 + 128 * j), P(m, 0, 96), X("TH", 0, 128, 1, 0, 96), True, True) for j, m in enumerate((REN, REA))])
+                act(TB(9, 256), X("PC", 128, 384), F.Identity, BIG - 2047.5)
+                if FUT:
+                    step("fmod")
+                    mm([x for j, m in enumerate((REN, REA)) for o in [X("PC", 128 + 128 * j, 256 + 128 * j)]
+                        for x in ((o, P(m, 0, 96), X("TH", 0, 128, 1, 0, 96), True, False), (o, NI16, TB(9 + j), False, True))])
+                    cp(TF(6, 256), X("PC", 128, 384), "act")
+                else:
+                    tt(TF(6, 256), X("PC", 128, 384), TB(9, 256), A.subtract)
+            step("base")
+            mm([(X("PC", 448, 464), I16, HB(16 * y, 16), y == 0, False) for y in range(2)]
+               + [(X("PC", 448, 456), I16y, HB(16 * y + 8, 8), False, y == 1) for y in range(2)])
             step("fired")
-            mm([(X("PD", 144, 152), I16 if last else I16x, C(UF, y, 64, 8), y == 0, y == 7) for y in range(8)])
+            mm([(X("PC", 464, 472), I16 if last else I16x, C(UF, y, 64, 8), y == 0, y == 7) for y in range(8)])
             step("za")
             tt(TF(2), IND(AD, FO), ZQ, A.add)
             step("acts")
             MK = X("MK", CW * t, CW * t + CW)
             cp(IND(MK, LW), ONES)
-            mm([(X("PA", 160, 176), I16, C16h, True, False)]
-               + [(X("PA", 160, 176), C(J2, 64 - k, 192 - k), C(MK, k, 256, 16), False, k == 15) for k in range(16)])
             SA = X("TU", 144, 152)
-            for h in range(2):
-                ts(P(SA, 64 * h, 64 * h + 64), X("PA", 160 + 8 * h, 168 + 8 * h, 1, 64 * h, 64 * h + 64), P(PFc(ca), 64 * h, 64 * h + 64), A.add)
-            if not last:
-                ts(X("EO", e0 + 128, e0 + 256), IND(TF(6, 256), SA), BIG, A.add)
-                send(X("EU", e0 + 128, e0 + 256), X("EO", e0 + 128, e0 + 256), "r1_%d_%d" % (b, t))
-            else:
-                ts(TF(8), IND(TF(6, 256), SA), BIG, A.add)
+
+            def choice():
+                mm([(X("PA", 160, 176), I16, C16h, True, False)]
+                   + [(X("PA", 160, 176), C(J2, 64 - k, 192 - k), C(MK, k, 256, 16), False, k == 15) for k in range(16)])
+                for h in range(2):
+                    ts(P(SA, 64 * h, 64 * h + 64), X("PA", 160 + 8 * h, 168 + 8 * h, 1, 64 * h, 64 * h + 64), P(PFc(ca), 64 * h, 64 * h + 64), A.add)
+
+            if spec:
+                choice()
+                ts(X("EO", e0, e0 + 128), IND(TF(6, 256), SA), BIG, A.add)
+                send(X("EU", e0 + 128, e0 + 256), X("EO", e0, e0 + 128), "r1_%d_%d" % (b, t))
+            if last:
                 step("end")
                 fill(SF(80), -1)
             step("state")
-            mm(([] if last else [(X("PB", 256, 280), I16, CA24, True, False)])
-               + [(X("PB", 256, 280), C(MK, 128 * h, 128 * h + 128), AR[h], last and h == 0, h == 1) for h in range(2)])
-            tt(SF(96, 24), X("PB", 256, 280), XD, A.mult)
-            tt(SF(128, 24) if last else X("SO", n0, n0 + 24), X("PD", 128, 152), SF(96, 24), A.subtract)
-            ts(X("ZB", 0, 128) if last else X("SO", n0 + 24, n0 + 152), IND(ZW, SA), ONE, A.add, -ONE, A.add)
-            if not last:
-                send(X("ST", n0, n0 + 152), X("SO", n0, n0 + 152), "r2_%d_%d" % (b, t))
+            w = 16 if last else 24
+            mm([(X("PA", 256, 256 + w), I16, C(CA24, 0, w), True, False)]
+               + [(X("PA", 256, 256 + w), C(MK, 128 * h, 128 * h + 128), C(AR[h], 0, w), False, h == 1) for h in range(2)]
+               + [(X("PA", 272, 280), C(MK, 128 * h, 128 * h + 128), C(AR[h], 16, 24), h == 0, h == 1) for h in range(2) if last])
+            tt(SF(96, 24), X("PA", 256, 280), XD, A.mult)
+            tt(X("SO", s0, s0 + 24), X("PC", 448, 472), SF(96, 24), A.subtract)
+            if spec:
+                ts(X("SO", s0 + 24, s0 + 152), IND(ZW, SA), ONE, A.add, -ONE, A.add)
+                send(X("ST", n0, n0 + 152), X("SO", s0, s0 + 152), "r2_%d_%d" % (b, t))
+            elif not last:
+                send(X("ST", n0, n0 + 24), X("SO", s0, s0 + 24), "r2_%d_%d" % (b, t))
             else:
-                mm([(X("PC", 0, 128, 1, 0, 16), SF(136, 16), I32, True, True)])
-                cp(P(TF(9), 0, 16), X("PC", 0, 128, 1, 0, 16), "act")
+                o = X("PC", 0, 128, 1, 0, 24)
+                mm([(o, X("SO", s0, s0 + 24), I32, True, True)])
+                act(P(TB(9), 0, 24), o, F.Identity, BIG - 2047.5)
+                tt(P(TF(8), 0, 24), o, P(TB(9), 0, 24), A.subtract)
+                act(P(TF(9), 0, 24), P(TF(8), 0, 24), F.Identity, BIG)
+                for j, nme in enumerate(("yc", "ys", "ya")):
+                    for h, q in enumerate(("sp", "act")):
+                        dma(q, R(nme, 128 * h, 128 * h + 128, 1, 4 * b, 4 * b + 4), P(TF(9), 8 * j + 4 * h, 8 * j + 4 * h + 4), 2, osem[q])
+            step("z")
+            if not spec:
+                choice()
+                ts(X("ZO", e0, e0 + 128), IND(ZW, SA), ONE, A.add, -ONE, A.add)
+            if not SPEC and not last:
+                send(X("ZI", e0 + 128, e0 + 256), X("ZO", e0, e0 + 128), "r1_%d_%d" % (b, t))
+            elif last:
                 for h in range(2):
-                    y = lambda nme: R(nme, 128 * h, 128 * h + 128, 1, 4 * b, 4 * b + 4)
-                    dma("act", y("yc"), P(TF(8), 64 * h, 64 * h + 64, 16), 2, osem["act"])
-                    dma("sp", y("ys"), P(TF(9), 4 * h, 4 * h + 4), 2, osem["sp"])
-                    dma("act", y("ya"), P(TF(9), 8 + 4 * h, 12 + 4 * h), 2, osem["act"])
-                    dma("sp", R("yz", 128 * h, 128 * h + 128, 1, 64 * b, 64 * b + 64), X("ZB", 0, 128, 1, 64 * h, 64 * h + 64), 16, osem["sp"])
+                    dma("sp", R("yz", 128 * h, 128 * h + 128, 1, 64 * b, 64 * b + 64), X("ZO", e0, e0 + 128, 1, 64 * h, 64 * h + 64), 16, osem["sp"])
             step("slot")
             GR, HR = X("ML", m0, m0 + 128), X("ML", m0 + 128, m0 + 136)
             o = X("PB", 288, 304)
@@ -550,7 +629,7 @@ def build(par=PAR):
                 e = blk[1]
                 for h, (w, y) in enumerate((("WO", "yo"), ("WV", "yv"))):
                     dma("g", R(y, 0, e, *rows), X(w, 0, e, 1, 0, 64), e // 8)
-                    dma("sp", X("DX", 0, 80, 1, 64 * h, 64 * h + 64), X(w, 0, e, 1, 0, 64, 16), 20)
+                    ops[dma("sp", X("DX", 0, 80, 1, 64 * h, 64 * h + 64), X(w, 0, e, 1, 0, 64, 16), 20)]["slack"] = 3.0
                 act(X("DY", 0, 80), X("DX", 0, 80), F.Identity, -127.5)
                 tt(X("DY", 80, 160), X("DX", 0, 80), X("DY", 0, 80), A.subtract)
                 ts(X("DX", 80, 160), X("DY", 0, 80), 0.0, A.is_lt, 257.0, A.mult)
@@ -567,6 +646,8 @@ def build(par=PAR):
 def overlap(a, b):
     if psum(a):
         return True
+    if a[3] == b[3] > 1 and (a[1] - b[1]) % a[3]:
+        return False
     return a[1] < b[2] and b[1] < a[2] and a[4] < b[5] and b[4] < a[5]
 
 
@@ -686,11 +767,11 @@ def flip(pre):
 
 def lay(ops, dep, cycle, hop):
     n = len(ops)
-    pre = [[(i, ops[i]["dur"] + ops[i]["lat"] + ops[i].get("kb", 0) * 0.006 + (0.0 if ops[i]["eng"] == "pe" == o["eng"] or o["recv"] else hop))
+    pre = [[(i, ops[i]["dur"] + ops[i]["lat"] + ops[i].get("slack", 0) + ops[i].get("kb", 0) * 0.006 + (0.0 if ops[i]["eng"] == "pe" == o["eng"] or o["recv"] else hop))
             for i in dep[j]] + ([(o["behind"], max(0.1, ops[o["behind"]]["kb"] * 0.006))] if "behind" in o else []) for j, o in enumerate(ops)]
     suc = flip(pre)
     rank = dict((w.split("/")[0], (int(w.split("/")[1]), a)) for x in cycle.values() for a, w in enumerate(x.split()))
-    known = set(i for i, o in enumerate(ops) if o["t"] >= 0 and o["pos"] in rank and (o["t"] < VIS - 1 or o["kind"] not in ("state", "object", "slot", "old")))
+    known = set(i for i, o in enumerate(ops) if o["t"] >= 0 and o["pos"] in rank and "behind" not in o and (o["t"] < VIS - 1 or o["kind"] not in ("state", "object", "slot", "old", "z")))
     queue = {}
     for i in known:
         o = ops[i]
@@ -705,9 +786,11 @@ def lay(ops, dep, cycle, hop):
     for j in ranked(range(n), p2, flip(p2)):
         if j in known:
             key[j] = max([key[i] + lag for i, lag in p2[j]] + [0.0])
-    for j in range(n - 1, -1, -1):
-        if key[j] is None and ops[j]["t"] < 0:
-            key[j] = min([key[i] - lag for i, lag in suc[j] if key[i] is not None] or [None])
+    for j in known:
+        key[j] += AHEAD.get((ops[j]["t"], ops[j]["b"]), 0.0)
+    for j in reversed(ranked(range(n), pre, suc)):
+        if key[j] is None and (ops[j]["t"] <= 0 or "behind" in ops[j]):
+            key[j] = min([key[i] - lag for i, lag in suc[j] if key[i] is not None] or [1e3]) + AHEAD.get(ops[j]["kind"], 0.0)
     for j in ranked(range(n), pre, suc):
         if key[j] is None:
             key[j] = max([key[i] + lag for i, lag in pre[j]] + [0.0])
@@ -718,12 +801,10 @@ def lay(ops, dep, cycle, hop):
     return ops, dep, ranked(t, pre, suc), t, [t[i] + o["dur"] + o["lat"] for i, o in enumerate(ops)]
 
 
-CYCLE = dict(
-    pe="name0.2/1 name0.3/1 rows.0/1 name1.0/1 name0.5/1 pick.4/2 rows.1/1 name1.1/1 name1.2/1 claim.0/2 name0.7/1 name1.3/1 future.3/2 claim.4/2 claim.5/2 last0.0/1 name1.5/1 df.1/2 claim.8/2 future.5/2 future.6/2 name1.7/1 acts.1/2 state.0/2 last1.0/1 fired.0/2 slot.0/2 object.0/2 base.0/1 head.0/1 abs0.1/1 object.2/2 turn.0/0 name0.0/0 abs1.1/1 name0.1/0 abs2.1/1 abs3.1/1",
-    dve="pick.0/2 pick.1/2 mark.0/2 pick.2/2 pick.3/2 mark.2/2 future.0/2 mark.4/2 mark.3/2 pick.5/2 future.2/2 mark.5/2 pick.6/2 future.1/2 mark.6/2 claim.1/2 claim.3/2 claim.2/2 eq0.0/1 claim.6/2 za.0/2 last0.2/1 claim.9/2 last0.3/1 flag.0/2 acts.0/2 last0.4/1 eq1.0/1 future.8/2 acts.2/2 acts.3/2 state.1/2 last0.5/1 acts.4/2 state.2/2 last1.2/1 state.3/2 last1.3/1 V0.0/1 last1.4/1 slot.1/2 V1.0/1 last1.5/1 object.1/2 V2.0/1 V3.0/1 O1.0/0",
-    sp="old.1/0 old.0/1",
-    act="name0.4/1 mark.1/2 O3.0/1 name0.6/1 df.0/2 name1.4/1 future.4/2 claim.7/2 last0.1/1 df.2/2 name1.6/1 dm.0/2 zq.1/1 future.7/2 object.3/3 object.4/3 last1.1/1 zq.0/1 abs0.0/1 slot.2/2 abs1.0/1 O0.0/0 abs2.0/1 abs3.0/1 turn.1/0 O2.0/0",
-    g="dm.1/2 acts.5/2 state.4/2")
+AHEAD = {(5, 1): -2.5, (5, 0): 3.0}
+CYCLE = {'sp': 'old.1/1 old.0/2', 'act': 'abs2.0/3 abs3.0/3 O1.0/2 mark.1/3 O2.0/2 name0.4/2 df.0/3 name0.6/2 O3.0/2 object.3/4 claim.7/3 last0.1/2 df.2/3 name1.4/2 dm.0/3 name1.6/2 zq.1/2 object.4/4 zq.0/2 last1.1/2 abs0.0/2 mod1.1/2 abs1.0/2 turn.1/1 slot.2/3 E.1/1', 'pe': 'object.0/4 E.2/2 abs1.1/3 abs2.1/3 rows.0/2 abs3.1/3 rows.1/2 name0.0/2 name0.1/2 name0.2/2 name0.3/2 pick.4/3 object.2/4 name1.0/2 name0.5/2 claim.0/3 name1.1/2 name0.7/2 df.1/3 claim.4/3 claim.5/3 name1.2/2 last0.0/2 claim.8/3 name1.3/2 fired.0/3 name1.5/2 state.0/3 name1.7/2 z.0/3 base.0/2 last1.0/2 head.0/2 mod1.0/2 mod2.0/2 mod1.2/2 slot.0/3 turn.0/1 abs0.1/2 E.0/1 E2.0/1', 'dve': 'E.3/2 z.3/4 O0.0/2 pick.0/3 mark.0/3 pick.1/3 object.1/4 pick.2/3 mark.2/3 pick.3/3 mark.4/3 mark.3/3 pick.5/3 mark.5/3 pick.6/3 mark.6/3 claim.1/3 claim.3/3 claim.2/3 eq0.0/2 future.0/3 claim.6/3 za.0/3 future.1/3 future.2/3 claim.9/3 last0.2/2 acts.0/3 last0.3/2 flag.0/3 last0.4/2 state.1/3 last0.5/2 state.2/3 eq1.0/2 V0.0/2 last1.2/2 z.2/3 V1.0/2 mod1.3/2 z.1/3 slot.1/3 V2.0/2 V3.0/2', 'g': 'z.4/4 dm.1/3 state.3/3'}
+CYCLE = {'dve': 'claim.9/2 flag.0/2 acts.0/2 za.0/2 last0.2/1 future.8/2 last0.3/1 last1.2/1 last0.4/1 acts.2/2 last1.3/1 acts.3/2 last0.5/1 last1.4/1 acts.4/2 V0.0/1 last1.5/1 V1.0/1 slot.1/2 V2.0/1 V3.0/1 object.1/2 state.1/2 O0.0/0 pick.0/1 state.3/2 pick.1/1 mark.0/1 state.2/2 pick.2/1 future.0/1 pick.3/1 future.1/1 future.2/1 mark.2/1 mark.4/1 mark.3/1 pick.5/1 mark.5/1 pick.6/1 mark.6/1 claim.3/1 claim.2/1 claim.1/1 eq0.0/0 claim.6/1 eq1.0/0', 'pe': 'rows.0/1 rows.1/1 last1.0/1 acts.1/2 head.0/1 slot.0/2 state.0/2 base.0/2 fired.0/2 abs0.1/1 object.0/2 abs1.1/1 object.2/2 abs2.1/1 abs3.1/1 name0.0/0 name0.1/0 name0.2/0 name0.3/0 name1.0/0 name1.1/0 pick.4/1 future.3/1 name1.2/0 name0.5/0 name1.3/0 claim.0/1 df.1/1 name0.7/0 name1.5/0 claim.4/1 claim.5/1 name1.7/0 turn.0/0 future.5/1 claim.8/1 future.6/1 last0.0/0', 'act': 'dm.0/2 future.7/2 last0.1/1 last1.1/1 zq.0/1 object.4/3 abs0.0/1 abs1.0/1 slot.2/2 abs2.0/1 abs3.0/1 O1.0/0 O2.0/0 mark.1/1 O3.0/0 name0.4/0 df.0/1 name0.6/0 name1.4/0 object.3/2 future.4/1 name1.6/0 zq.1/0 df.2/1 claim.7/1 turn.1/0', 'g': 'dm.1/2 acts.5/2 state.4/2', 'sp': 'old.0/1 old.1/0'}
+CYCLE = {'dve': 'V2.0/1 slot.1/2 V3.0/1 state.1/2 state.3/2 state.2/2 object.1/2 O0.0/0 pick.0/1 pick.1/1 mark.0/1 pick.2/1 future.0/1 pick.3/1 mark.2/1 future.2/1 mark.3/1 mark.4/1 future.1/1 pick.5/1 mark.5/1 pick.6/1 mark.6/1 future.4/1 claim.1/1 claim.2/1 claim.3/1 za.0/1 turn.1/0 eq0.0/0 claim.6/1 eq1.0/0 claim.9/1 flag.0/1 acts.0/1 last0.2/0 last1.2/0 last0.3/0 last1.3/0 last0.4/0 last1.4/0 last0.5/0 last1.5/0 acts.3/1 acts.2/1 V0.0/0 acts.4/1 V1.0/0', 'act': 'abs1.0/1 abs2.0/1 slot.2/2 abs3.0/1 O1.0/0 O2.0/0 mark.1/1 O3.0/0 name0.4/0 turn.0/0 future.3/1 name0.6/0 name1.4/0 zq.1/0 object.3/2 name1.6/0 df.0/1 claim.7/1 turn.3/0 future.6/1 df.2/1 zq.0/0 last0.1/0 last1.1/0 dm.0/1 future.8/1 object.4/2 fmod.1/1 abs0.0/0', 'pe': 'slot.0/2 head.0/1 base.0/2 fired.0/2 object.0/2 abs2.1/1 abs3.1/1 object.2/2 name0.0/0 name0.1/0 name0.2/0 name0.3/0 name1.0/0 pick.4/1 name1.1/0 name1.2/0 name0.5/0 name1.3/0 claim.0/1 name0.7/0 name1.5/0 claim.4/1 claim.5/1 name1.7/0 future.5/1 turn.2/0 df.1/1 claim.8/1 last0.0/0 last1.0/0 rows.0/0 future.7/1 acts.1/1 fmod.0/1 state.0/1', 'g': 'state.4/2 dm.1/1 acts.5/1', 'sp': 'old.1/0 old.0/0'}
 GRAPH = plan()
 PLAN = lay(GRAPH[0], GRAPH[1], CYCLE, PAR["HOP"])
 
@@ -797,7 +878,10 @@ def rank_program(g, core, T, topo):
             else:
                 ins = q.iota(ap(c[1]), c[2], c[3], c[4], allow_small_or_imprecise_dtypes=True)
         elif k == "as":
-            ins = q.affine_select(ap(c[1]), ap(c[1]), c[2], c[3], c[4], c[5], c[6])
+            ins = q.affine_select(ap(c[1]), ap(c[7]), c[2], c[3], c[4], c[5], c[6])
+        elif k == "acc":
+            ins = q.dma_start(ap(c[1]), ap(c[2]), accum_op=A.add, max_dma_last_dim=8192)
+            sem, inc = o["sem"], 16
         elif k == "scan":
             ins = q.tensor_tensor_scan(ap(c[1]), ap(c[2]), ap(c[3]), 0.0, A.add, A.max)
         elif k == "dma":

@@ -2,7 +2,7 @@ import math
 from concourse.mybir import AluOpType as A, ActivationFunctionType as F
 
 VIS, NB = 6, 2
-SW, MW, CW = 160, 144, 384
+SW, MW, CW = 32, 144, 384
 BF, FP, I3, U2 = "bfloat16", "float32", "int32", "uint16"
 SCRATCH = {}
 for _b in range(NB):
@@ -10,21 +10,22 @@ for _b in range(NB):
                        ("EQ", 1024, BF), ("ST", VIS * SW, FP), ("SO", VIS * SW, FP),
                        ("ZI", VIS * 128, BF), ("ZO", VIS * 128, BF), ("EU", VIS * 128, U2), ("EO", VIS * 128, U2), ("ML", VIS * MW, BF), ("MO", VIS * MW, BF),
                        ("CA", 512, FP), ("CB", 512, FP), ("W5", 768, BF), ("N5", 512, I3), ("YN", 256, FP),
-                       ("DF", CW, BF), ("MK", VIS * CW, BF), ("XP", 256, BF), ("XS", 256, BF), ("TT", 128, FP), ("TH", 128, BF), ("HB", 64, BF),
-                       ("TF", 10 * 128, FP), ("TI", 2 * 128, I3), ("TB", 12 * 128, BF), ("TU", 384, U2),
-                       ("SF", 192, FP), ("SI", 64, I3), ("SB", 64, BF), ("CS", 128, I3),
+                       ("DF", CW, BF), ("MK", VIS * CW, BF), ("XP", 256, BF), ("XS", 256, BF), ("TH", 128, BF), ("HB", 64, BF),
+                       ("TF", 10 * 128, FP), ("TI", 3 * 128, I3), ("ZB", 768, FP), ("UU", 144, BF), ("TB", 12 * 128, BF), ("TU", 384, U2),
+                       ("SF", 192, FP), ("SI", 64, I3), ("SB", 64, BF), ("SN", 128, I3),
                        ("DX", 320, FP), ("DY", 160, BF)):
         SCRATCH["%s%d" % (_n, _b)] = ("sbuf", [128, _w], _d)
     for _n in "ABCD":
         SCRATCH["P%s%d" % (_n, _b)] = ("psum", [128, 512], FP)
 for _n, _w, _d in (("NI", 512, I3), ("NW", 1024, FP), ("NH", 512, BF), ("PI", 64, I3), ("PF", 128, FP), ("KB", 59 * 128, BF),
-                   ("KF", 2 * 128, FP), ("KS", 256, BF), ("OI", 80, FP), ("OU", 80, U2)):
+                   ("KF", 3 * 128, FP), ("KS", 256, BF), ("OI", 80, FP), ("OU", 80, U2), ("CS", 128, I3), ("TT", 128, FP),
+                   ("V0", 128, BF), ("NV", 128, FP)):
     SCRATCH[_n] = ("sbuf", [128, _w], _d)
 OUTS = ("yn", "yo", "yv", "yx", "yc", "ys", "ya", "yz")
 ENG = ("g", "pe", "dve", "act", "sp")
-NDS = 90
+NDS = 60
 SEMAPHORES = ["c_" + e for e in ENG] + ["d%d" % i for i in range(NDS)] + ["sent"] + \
-    ["r%d_%d_%d" % (m, b, t) for m in range(3) for b in range(NB) for t in range(VIS)]
+    ["r%d_%d_%d" % (m, b, t) for m in range(5) for b in range(NB) for t in range(VIS)]
 LN2 = math.log(2.0)
 TOP = 41.5
 WB = 2 * TOP / 64
@@ -36,12 +37,19 @@ LOOK = 0.05
 LEAD = 4.0
 OQ = (32, 0, 0, 0)
 VP = (32, 32, 32, 32)
-LOGQ = dict(WO0=("dve", "act") * 4, WV0=("dve", "act") * 4, WO1=("dve", "act") * 4, WV1=("dve", "act") * 4)
+LOGQ = dict(WO0=("dve", "act") * 4, WV0=("dve", "dve", "dve", "act") * 2, WO1=("dve", "act") * 4)
 LOGB = dict(WO0=("PA0", "PD0", "PA1", "PB1", "PD1"), WV0=("PA1", "PB1", "PD1"), WO1=("PA1", "PD1", "PB1"), WV1=("PD1",))
-PEMOD, SQ, SPEC = (), "act", True
+PEMOD, SQ, SPEC = (), "dve", True
 HQ, SP = "act", ((0, 96), (96, 128))
 FUT, MERGE = True, 0
 BYG = ("WV1",)
+SLB = "PD"
+ZSEND = True
+NM, EQP = 2, 1
+HQ0 = "act"
+FSEND = True
+PASSES = 2
+GVE = 2
 NUDGE = {}
 
 
@@ -136,6 +144,9 @@ def build(par=PAR):
             wr.append(o)
         return add("pe", ("mm", lst), rd, wr, 0.03 + d)
 
+    def scan(out, d0, d1, o0, o1):
+        return add("dve", ("scan", out, d0, d1, o0, o1), [d0, d1], [out], 0.03 + n_of(out) * CY)
+
     def mset(out, v):
         return add("dve", ("ms", out, v), [], [out], cost(out, [out]))
 
@@ -166,29 +177,36 @@ def build(par=PAR):
     KS = lambda a, n: R("KS", a, a + n)
     osem = {q: newsem() for q in ("sp", "act")}
 
-    seq = [dma("sp", R("NI", 0, 256), R("nm", 0, 4096, 1, 0, 8), 128)]
-    for b in range(NB):
-        for h in range(2):
-            for j, nme in enumerate(("c0", "s0")):
-                dma("act", R("CS%d" % b, 0, 128, 1, 8 * j + 4 * h, 8 * j + 4 * h + 4),
-                    R(nme, 128 * h, 128 * h + 128, 1, 4 * b, 4 * b + 4), 2)
+    seq = [dma("sp", R("NI", 0, 128), R("nm", 0, 4096, 1, 0, 4), 64)]
+    for j, nme in enumerate(("c0", "s0")):
+        dma("act", R("CS", 0, 128, 1, 16 * j, 16 * j + 16), R(nme, 0, 256, 1, 0, 8), 8)
     iota(PIc(0), [[0, 1]], 0, 1)
     iota(R("NI", 256, 512), [[1, 256]])
-    for a in (0, 256):
-        ts(R("NW", a, a + 256), R("NI", a, a + 256), 128.0, A.is_lt, -257.0, A.mult)
-        tt(R("NW", 512 + a, 768 + a), R("NW", a, a + 256), R("NI", a, a + 256), A.add)
-    act(R("NH", 0, 256), R("NW", 512, 768), F.Identity, 256.0, 256.0)
+    def code(a, e):
+        ts(R("NW", a, e), R("NI", a, e), 128.0, A.is_lt, -257.0, A.mult)
+        tt(R("NW", 512 + a, 512 + e), R("NW", a, e), R("NI", a, e), A.add)
+
+    code(256, 512)
     for b in range(NB):
+        step("nm%d" % b)
+        code(128 * b, 128 * b + 128)
+        act(R("NH", 128 * b, 128 * b + 128), R("NW", 512 + 128 * b, 640 + 128 * b), F.Identity, 256.0, 256.0)
+        step("start")
         for w, nme in (("DA", "vo"), ("GV", "vn")):
             if w == "GV" and "WV%d" % b in BYG:
-                for c in range(2):
+                for c in range(4):
+                    if c == 2:
+                        seq.append(dma("sp", R("V0", 0, 128), R(nme, 0, 4096, 1, 64 * b, 64 * b + 64, 16), 32))
                     for h in range(2):
-                        seq.append(dma("sp", R("GV%d" % b, 2048 * c, 2048 * c + 2048, 1, 64 * h, 64 * h + 64),
-                                       R(nme, 2048 * c, 2048 * c + 2048, 1, 64 * b, 64 * b + 64), 256))
+                        seq.insert(len(seq) - (3 if c < GVE else 0),
+                                   dma("sp", R("GV%d" % b, 1024 * c, 1024 * c + 1024, 1, 64 * h, 64 * h + 64),
+                                                                         R(nme, 1024 * c, 1024 * c + 1024, 1, 64 * b, 64 * b + 64), 128))
                 continue
             for c in range(2):
                 seq.append(dma("sp", R("%s%d" % (w, b), 2048 * c, 2048 * c + 2048, 1, 0, 64), R(nme, 2048 * c, 2048 * c + 2048, 1, 64 * b, 64 * b + 64), 256))
-            seq.append(dma("sp", R("%s%d" % (w, b), 0, 4096, 1, 64, 68), R("NH", 0, 256, 1, 64 * b, 64 * b + 64), 32))
+            seq.insert(len(seq) - (0 if (b, w) == (0, "DA") else 2), dma("sp", R("%s%d" % (w, b), 0, 4096, 1, 64, 68), R("NH", 128 * b, 128 * b + 128), 32))
+            if (b, w) == (0, "DA"):
+                seq.append(dma("sp", R("NI", 128, 256), R("nm", 0, 4096, 1, 4, 8), 64))
         for h in range(2):
             seq.append(dma("sp", R("ZI%d" % b, 0, 128, 1, 64 * h, 64 * h + 64), R("z0", 128 * h, 128 * h + 128, 1, 64 * b, 64 * b + 64), 16))
         seq.append(dma("sp", R("XS%d" % b, 0, 256, 1, 0, 64), R("xo", 0, 256, 1, 64 * b, 64 * b + 64), 32))
@@ -229,7 +247,8 @@ def build(par=PAR):
         tt(m, m, MSK, A.mult)
     lin(RSP, MSK, aS)
     ts(I16, IC, PFc(cP), A.is_equal)
-    lin(I32, I16, 1.0)
+    I32 = C(I32, 0, 32)
+    lin(I32, C(I16, 0, 32), 1.0)
     lin(I16y, I16, 16.0)
     lin(I16x, I16, 32.0)
     NI16 = K(51)
@@ -248,10 +267,12 @@ def build(par=PAR):
         mm([(o, I16, CODE, True, False)] + [(C(o, y, 256, 2), SEL[y], src, False, y == 1) for y in range(2)])
         cp(out, o, "act")
 
+    TT = R("TT", 0, 128, 1, 0, 32)
+    cp(TT, R("CS", 0, 128, 1, 0, 32))
     for b in range(NB):
         X = lambda nme, a, e, *k: R("%s%d" % (nme, b), a, e, *k)
-        cp(X("TT", 0, 128, 1, 0, 16), X("CS", 0, 128, 1, 0, 16))
-        mm([(X("PC", 128, 144), X("TT", 0, 128, 1, 0, 16), P(C(I32, 0, 16), 0, 16), True, True)])
+        mm([(X("PC", 128 + 8 * j + 4 * h, 132 + 8 * j + 4 * h), TT, P(C(I32, 16 * j + 8 * b + h, 16 * j + 8 * b + 8, 2), 0, 32), True, True)
+            for j in range(2) for h in range(2)])
         cp(X("ST", 0, 16), X("PC", 128, 144), "act")
         fill(X("ST", 16, 24), 1792)
         fill(X("SF", 80, 88), -32)
@@ -261,9 +282,9 @@ def build(par=PAR):
             if w + str(b) in BYG:
                 for c in range(4):
                     asel(X(w, 1024 * c, 1024 * c + 1024), [[0, 1024]], A.is_ge, 0.0, 0, 0, X(s, 1024 * c, 1024 * c + 1024))
+                tt(R("NV", 0, 128), R("V0", 0, 128), R("NH", 128 * b, 128 * b + 128), A.add)
                 for h in range(2):
-                    i = dma("g", X(w, 0, 4096, 1, 64 * h, 64 * h + 64, 16), R("NH", 0, 256, 1, 64 * b, 64 * b + 64), 128)
-                    ops[i]["call"] = ("acc",) + ops[i]["call"][1:]
+                    dma("sp", X(w, 0, 4096, 1, 64 * h, 64 * h + 64, 16), R("NV", 0, 128), 64)
                 continue
             banks = LOGB[w + str(b)]
             for c in range(8):
@@ -308,7 +329,6 @@ def build(par=PAR):
         lin(r, PS1, v)
     iota(C256, [[256, 8]])
     iota(C16, [[16, 16]])
-    iota(C16h, [[0, 2], [16, 8]])
     for j, v in enumerate((1, 0, 56)):
         fill(C(CA24, 8 * j, 8 * j + 8), v)
     iota(KS(192, 24), [[0, 3], [1, 8]])
@@ -319,9 +339,15 @@ def build(par=PAR):
     fill(D0, 1)
     asel(D0, [[0, 8], [1, 16]], A.not_equal, -4000000.0, 0, 0)
     ts(MA, M16, PFc(ca), A.is_equal)
-    J2, IOH, IU, SF64, ONES = K(38, 192), K(40, 256), K(42, 64), K(43, 64), K(44)
-    lin(PFc(cz128), PFc(cz), 128.0)
-    ts(J2, K(4, 192), PFc(c64), A.is_equal, PFc(cz128), A.mult)
+    J2, RED, IOH, IU, SF72, ONES = K(38, 64), K(39), K(40, 256), K(42, 64), K(43, 72), K(44)
+    SF64 = C(SF72, 0, 64)
+    ts(J2, K(4, 64), PFc(c64), A.is_equal)
+    tt(RED, REA, REN, A.subtract)
+    cp(C(SF72, 64, 72), PS1)
+    for b in range(NB):
+        fill(R("UU%d" % b, 64, 72), 1)
+        fill(R("ZB%d" % b, 0, 256, 2), 0)
+        fill(R("ZB%d" % b, 256, 768, 2), 0)
     lin(PFc(c16a), PFc(ca), 16.0, 15.0)
     fill(ONES, 1)
     O = lambda a, n: R("OI", a, a + n)
@@ -356,6 +382,8 @@ def build(par=PAR):
             c = cf00 + 2 * h + y
             lin(PFc(c), PFc(fl), PFc(fy))
             lin(LY[h][y], G4, PFc(c))
+    I128 = KF(2)
+    lin(I128, I16, 1.0)
     step("zero")
     for b in range(NB):
         for t in range(VIS):
@@ -374,7 +402,7 @@ def build(par=PAR):
             SF = lambda a, n=8: X("SF", a, a + n)
             s0, e0, m0, n0 = SW * t, 128 * t, MW * t, SW * (t + 1)
             CSi, Si, Ai, Zi = X("ST", s0, s0 + 16), X("ST", s0 + 8, s0 + 16), X("ST", s0 + 16, s0 + 24), X("ZI", e0, e0 + 128)
-            if SPEC and t:
+            if t and not ZSEND:
                 Zi = X("ST", s0 + 24, s0 + 152)
             now.update(bias=LEAD if b == 0 else 0.0, t=t, b=b, step="", seen={})
             CO, CV = ("CA", "CB") if t % 2 == 0 else ("CB", "CA")
@@ -391,7 +419,7 @@ def build(par=PAR):
                 dma("sp", X("N5", 0, 256, 1, 0, 64, 16), R("nm", blk[0], blk[1], 1, 4 * b, 4 * b + 4), 4)
             step("turn")
             T64, HB = X("TH", 0, 128, 1, 0, 64), lambda a, n: X("HB", a, a + n)
-            cp(HB(0, 16), CSi, HQ)
+            cp(HB(0, 16), CSi, HQ0)
             tt(HB(16, 16), CSi, HB(0, 16), A.subtract)
             mm([(X("PC", 0, 128, 1, 32 * y, 32 * y + 32), HB(0, 32), I16, True, True) for y in range(2)])
             cp(T64, X("PC", 0, 128, 1, 0, 64), "act")
@@ -404,11 +432,11 @@ def build(par=PAR):
                 mm([(o, P(RE0, 0, 64), T64, True, False), (o, NI16, TB(9), False, True)])
                 ts(EU, o, BIG, A.add)
             step("rows")
-            mm([(X("PC", 128, 256), P(REP, 0, 64), T64, True, True), (X("PC", 256, 384), P(RSP, 0, 64), T64, True, True)])
+            mm([(X("PC", 129, 384, 2), P(REP, 0, 64), T64, True, True), (X("PC", 128, 384, 2), P(RSP, 0, 64), T64, True, True)])
             step("zq")
-            ZQ, ZW = TF(0), TF(1, 256)
+            ZQ, ZY = TF(0), TF(1)
             act(ZQ, Zi, F.Identity, -0.25, 0.5)
-            act(TF(1), Zi, F.Relu, -1.0, 1.0)
+            act(ZY, Zi, F.Abs, -0.4, 0.5)
             for c, bank in enumerate(("PA", "PB")):
                 for y in range(2):
                     p = 2 * c + y
@@ -417,8 +445,8 @@ def build(par=PAR):
                         if a < e:
                             cp(X("OG", 16 * a, 16 * e), IND(X("WO", 0, 4096), C(EU, a, e)), q)
                     step("name%d" % c)
-                    for kk in range(0, 4, 2):
-                        mm([(X(bank, 32 * y + 8 * k, 32 * y + 8 * k + 8), X("OG", 512 * p + k, 512 * p + 512, 4), SELN, True, True) for k in (kk, kk + 1)])
+                    for kk in range(0, 4, NM):
+                        mm([(X(bank, 32 * y + 8 * k, 32 * y + 8 * k + 8), X("OG", 512 * p + k, 512 * p + 512, 4), SELN, True, True) for k in range(kk, kk + NM)])
                 N1, N2 = C(TB(0), 64 * c, 64 * c + 64), C(TB(1), 64 * c, 64 * c + 64)
                 act(N1, X(bank, 0, 64), F.Identity, -127.5)
                 mm([(X(bank, 64 + 32 * y, 96 + 32 * y, 1, 32 * q, 32 * q + 32), C(N1, 32 * y, 32 * y + 32), C(I16, q, 128, 4), True, True)
@@ -428,30 +456,15 @@ def build(par=PAR):
                 step("eq%d" % c)
                 ts(X("EQ", 512 * c, 512 * c + 512), X(bank, 0, 512), 0.0, A.is_equal)
                 step("last%d" % c)
-                o = X("PA", 64 * c, 64 * c + 64) if MERGE else X(bank, 0, 64)
+                o = X(bank, 0, 64)
                 mm([(o, WM[d], X("EQ", 512 * c + d, 512 * c + 512, 8), d == 0, d == 7) for d in range(8)])
                 h64 = lambda r: C(r, 64 * c, 64 * c + 64)
-                if MERGE:
-                    if not c:
-                        continue
-                    h64, o = lambda r: r, X("PA", 0, 128)
-                i = act(h64(TF(3)), o, F.Ln, 2.0 ** -60, 1.0, 1.5 if t + b + c == MERGE else 0.0)
+                a, e = 128 * c, 128 * c + 128
+                i = act(X("ZB", a + 1, e, 2), o, F.Ln, 2.0 ** -60, 1.0, 1.5 if t + b + c == 0 else 0.0)
                 ops[i]["reads"].append(W4)
-                tt(h64(TF(4)), h64(X("PC", 256, 384)), h64(TF(3)), A.mult)
-                if c in PEMOD:
-                    step("mod%d" % c)
-                    x = lambda o, sp: [(o, P(REP, 0, 64), h64(T64), True, False), (o, I32, h64(TF(4)), False, sp)]
-                    mm(x(X(bank, 64, 128), True))
-                    act(h64(TB(11)), X(bank, 64, 128), F.Identity, BIG - 2047.5)
-                    step("mod2")
-                    mm(x(X("PC", 0, 64), False))
-                    step("mod%d" % c)
-                    mm([(X("PC", 0, 64), NI16, h64(TB(11)), False, True)])
-                    ts(h64(X("TU", 0, 128)), X("PC", 0, 64), BIG, A.add)
-                else:
-                    tt(h64(TI(0)), h64(X("PC", 128, 256)), h64(TF(4)), A.add)
-                    ts(h64(TI(1)), h64(TI(0)), 4095, A.bitwise_and)
-                    cp(h64(X("TU", 0, 128)), h64(TI(1)))
+                scan(X("TI", a, e), X("ZB", a, e), X("PC", 128 + a, 128 + e), A.mult, A.add)
+                ts(h64(TI(2)), X("TI", a + 1, e, 2), 4095, A.bitwise_and)
+                cp(h64(X("TU", 0, 128)), h64(TI(2)))
             step("head")
             mm([(X("PD", 0, 128), X("EQ", d, 1024, 8), PN[d], d == 0, False) for d in range(8)])
             r0, DD, AD = 0, X("DA", 0, 2048), X("DA", 2048, 4096)
@@ -466,11 +479,10 @@ def build(par=PAR):
                     if r0 - w < e <= r0:
                         mm([(X("PD", k, 128, 16, a, e), C(AD, 16 * a + k, 16 * e, 16), S64, False, k == 15) for k in range(16)])
             step("pick")
-            SC = TF(5)
-            add("dve", ("scan", SC, D0, X("PD", 0, 128)), [D0, X("PD", 0, 128)], [SC], 0.03 + 128 * CY)
+            SC = X("SN", 0, 128)
+            scan(SC, D0, X("PD", 0, 128), A.add, A.max)
             KEY = C(SC, 15, 128, 16)
-            ts(SI(0), KEY, 16.0, A.add)
-            ts(SI(8), SI(0), 15, A.bitwise_and)
+            ts(SI(8), KEY, 15, A.bitwise_and)
             tt(TB(2), IND(SI(8), LB), MA, A.mult)
             mm([(X("PA", 0, 8), I16, C256, True, False), (X("PA", 0, 8), TB(2), NS1, False, True)])
             FO = X("TU", 128, 136)
@@ -486,14 +498,14 @@ def build(par=PAR):
             tt(SI(16), SF(8), Ai, A.add)
             ts(SI(24), SI(16), 5, A.arith_shift_right, 31, A.bitwise_and)
             ts(SI(32), SI(16), 10, A.arith_shift_right, 7, A.bitwise_and)
-            OH, UU, UF, UW = TB(4, 256), TB(6, 64), C(TB(6), 64, 128), TB(7)
+            OH, UU, UF, UW = TB(4, 256), X("UU", 0, 64), X("UU", 72, 144), TB(7)
             tt(UU, IND(SI(24, 16), LU), IU, A.is_equal)
             tt(OH, IND(SI(24), LOH), IOH, A.is_equal)
             step("claim")
-            mm([(X("PA", 16, 80), I16x, UU, True, False), (X("PA", 16, 80), TB(3), SF64, False, True)])
+            mm([(X("PA", 16, 88), I16x, X("UU", 0, 72), True, False), (X("PA", 16, 88), TB(3), SF72, False, True)])
             for y in range(2):
                 ts(C(UW, y, 128, 2), X("PA", 16, 80), 40.5, A.is_ge, PFc(66 + y), A.mult)
-            ts(UF, X("PA", 16, 80), 40.5, A.is_ge)
+            ts(UF, X("PA", 16, 88), 40.5, A.is_ge)
             o = lambda a, e, q, st=1: X("PA", 96 + a, 96 + e, st, 32 * q, 32 * q + 32)
             l = lambda h, q: C(OH, 128 * h + 32 * q, 128 * h + 32 * q + 32)
             uw = lambda h, q: C(UW, 64 * h + 16 * q, 64 * h + 16 * q + 16)
@@ -515,15 +527,19 @@ def build(par=PAR):
             step("flag")
             HL, GG = X("MO", m0 + 128, m0 + 136), X("MO", m0, m0 + 128)
             ts(HL, X("PA", 144, 152), -64.5 * WB, A.is_gt)
+            if FSEND:
+                send(X("ML", m0 + 128, m0 + 136), HL, "r4_%d_%d" % (b, t))
             step("df")
             cp(TB(8), IND(DD, FO), "act")
             mm([(X("PB", 128 * h, 128 + 128 * h), SEL[h], TB(8), True, True) for h in range(2)])
             cp(X("DF", 0, 256), X("PB", 0, 256), "act")
             step("dm")
             cp(GG, IND(X("DF", 0, CW), LW), "act")
-            send(X("ML", m0, m0 + 136), X("MO", m0, m0 + 136), "r0_%d_%d" % (b, t))
+            w = 128 if FSEND else 136
+            send(X("ML", m0, m0 + w), X("MO", m0, m0 + w), "r0_%d_%d" % (b, t))
             step("future")
             XD = SF(64, 24)
+            ts(SI(0), KEY, 16.0, A.add)
             ts(SI(40), SI(0), 4, A.arith_shift_right, 1023, A.bitwise_and)
             tt(SF(64), SI(8), Si, A.mult)
             tt(SF(72), SI(40), Si, A.subtract)
@@ -535,35 +551,36 @@ def build(par=PAR):
                 cp(X("TH", 0, 128, 1, 64, 96), X("PC", 0, 128, 1, 64, 96), "act")
                 mm([(X("PC", 128 + 128 * j, 256 + 128 * j), P(m, 0, 96), X("TH", 0, 128, 1, 0, 96), True, True) for j, m in enumerate((REN, REA))])
                 act(TB(9, 256), X("PC", 128, 384), F.Identity, BIG - 2047.5)
-                if FUT:
-                    step("fmod")
-                    mm([x for j, m in enumerate((REN, REA)) for o in [X("PC", 128 + 128 * j, 256 + 128 * j)]
-                        for x in ((o, P(m, 0, 96), X("TH", 0, 128, 1, 0, 96), True, False), (o, NI16, TB(9 + j), False, True))])
-                    cp(TF(6, 256), X("PC", 128, 384), "act")
-                else:
-                    tt(TF(6, 256), X("PC", 128, 384), TB(9, 256), A.subtract)
+                step("fmod")
+                T96, o, o2 = X("TH", 0, 128, 1, 0, 96), X("PC", 0, 128), X("PC", 129, 384, 2)
+                mm([(o, P(RED, 0, 96), T96, True, False), (o, NI16, TB(10), False, False), (o, I16, TB(9), False, True),
+                    (o2, P(REN, 0, 96), T96, True, False), (o2, NI16, TB(9), False, True)])
+                cp(X("ZB", 257, 512, 2), o, "act")
             step("base")
-            mm([(X("PC", 448, 464), I16, HB(16 * y, 16), y == 0, False) for y in range(2)]
-               + [(X("PC", 448, 456), I16y, HB(16 * y + 8, 8), False, y == 1) for y in range(2)])
-            step("fired")
-            mm([(X("PC", 464, 472), I16 if last else I16x, C(UF, y, 64, 8), y == 0, y == 7) for y in range(8)])
+            mm([(X("PA", 288, 304), I16, HB(16 * y, 16), y == 0, False) for y in range(2)]
+               + [(X("PA", 288, 296), I16y, HB(16 * y + 8, 8), False, y == 1) for y in range(2)]
+               + [(X("PA", 304, 312), I16 if last else I16x, C(UF, 64, 72), True, True)])
             step("za")
-            tt(TF(2), IND(AD, FO), ZQ, A.add)
+            tt(X("ZB", 513, 768, 2), IND(AD, FO), ZY, A.subtract)
+            act(X("PB", 257, 512, 2), Zi, F.Relu, -0.75)
             step("acts")
             MK = X("MK", CW * t, CW * t + CW)
             cp(IND(MK, LW), ONES)
-            SA = X("TU", 144, 152)
-
-            def choice():
-                mm([(X("PA", 160, 176), I16, C16h, True, False)]
-                   + [(X("PA", 160, 176), C(J2, 64 - k, 192 - k), C(MK, k, 256, 16), False, k == 15) for k in range(16)])
-                for h in range(2):
-                    ts(P(SA, 64 * h, 64 * h + 64), X("PA", 160 + 8 * h, 168 + 8 * h, 1, 64 * h, 64 * h + 64), P(PFc(ca), 64 * h, 64 * h + 64), A.add)
-
+            marks = lambda bank, a: mm([(X(bank, a, a + 256, 2, 64 * h, 64 * h + 64), J2, C(MK, 128 * h, 128 * h + 128), True, True) for h in range(2)])
             if spec:
-                choice()
-                ts(X("EO", e0, e0 + 128), IND(TF(6, 256), SA), BIG, A.add)
+                marks("PC", 128)
+                scan(TF(6, 256), X("ZB", 256, 512), X("PC", 128, 384), A.mult, A.add)
+                ts(X("EO", e0, e0 + 128), C(TF(6), 1, 256, 2), BIG, A.add)
                 send(X("EU", e0 + 128, e0 + 256), X("EO", e0, e0 + 128), "r1_%d_%d" % (b, t))
+            step("z")
+            marks("PB", 256)
+            scan(TF(2, 256), X("ZB", 512, 768), X("PB", 256, 512), A.mult, A.add)
+            ts(X("SO", s0 + 24, s0 + 152) if spec and not ZSEND else X("ZO", e0, e0 + 128), C(TF(2), 1, 256, 2), ONE, A.add, -ONE, A.add)
+            if ZSEND and not last:
+                send(X("ZI", e0 + 128, e0 + 256), X("ZO", e0, e0 + 128), "r3_%d_%d" % (b, t))
+            if last:
+                for h in range(2):
+                    dma("sp", R("yz", 128 * h, 128 * h + 128, 1, 64 * b, 64 * b + 64), X("ZO", e0, e0 + 128, 1, 64 * h, 64 * h + 64), 16, osem["sp"])
             if last:
                 step("end")
                 fill(SF(80), -1)
@@ -573,33 +590,22 @@ def build(par=PAR):
                + [(X("PA", 256, 256 + w), C(MK, 128 * h, 128 * h + 128), C(AR[h], 0, w), False, h == 1) for h in range(2)]
                + [(X("PA", 272, 280), C(MK, 128 * h, 128 * h + 128), C(AR[h], 16, 24), h == 0, h == 1) for h in range(2) if last])
             tt(SF(96, 24), X("PA", 256, 280), XD, A.mult)
-            tt(X("SO", s0, s0 + 24), X("PC", 448, 472), SF(96, 24), A.subtract)
+            tt(X("SO", s0, s0 + 24), X("PA", 288, 312), SF(96, 24), A.subtract)
             if spec:
-                ts(X("SO", s0 + 24, s0 + 152), IND(ZW, SA), ONE, A.add, -ONE, A.add)
-                send(X("ST", n0, n0 + 152), X("SO", s0, s0 + 152), "r2_%d_%d" % (b, t))
-            elif not last:
-                send(X("ST", n0, n0 + 24), X("SO", s0, s0 + 24), "r2_%d_%d" % (b, t))
+                w = 24 if ZSEND else 152
+                send(X("ST", n0, n0 + w), X("SO", s0, s0 + w), "r2_%d_%d" % (b, t))
             else:
                 o = X("PC", 0, 128, 1, 0, 24)
-                mm([(o, X("SO", s0, s0 + 24), I32, True, True)])
+                mm([(o, X("SO", s0, s0 + 24), I128, True, True)])
                 act(P(TB(9), 0, 24), o, F.Identity, BIG - 2047.5)
                 tt(P(TF(8), 0, 24), o, P(TB(9), 0, 24), A.subtract)
                 act(P(TF(9), 0, 24), P(TF(8), 0, 24), F.Identity, BIG)
                 for j, nme in enumerate(("yc", "ys", "ya")):
                     for h, q in enumerate(("sp", "act")):
                         dma(q, R(nme, 128 * h, 128 * h + 128, 1, 4 * b, 4 * b + 4), P(TF(9), 8 * j + 4 * h, 8 * j + 4 * h + 4), 2, osem[q])
-            step("z")
-            if not spec:
-                choice()
-                ts(X("ZO", e0, e0 + 128), IND(ZW, SA), ONE, A.add, -ONE, A.add)
-            if not SPEC and not last:
-                send(X("ZI", e0 + 128, e0 + 256), X("ZO", e0, e0 + 128), "r1_%d_%d" % (b, t))
-            elif last:
-                for h in range(2):
-                    dma("sp", R("yz", 128 * h, 128 * h + 128, 1, 64 * b, 64 * b + 64), X("ZO", e0, e0 + 128, 1, 64 * h, 64 * h + 64), 16, osem["sp"])
             step("slot")
             GR, HR = X("ML", m0, m0 + 128), X("ML", m0 + 128, m0 + 136)
-            o = X("PB", 288, 304)
+            o = X("PA" if last else SLB, 160, 176)
             mm([(o, I16, C16, True, False)] + [(C(o, y, 16, 2), LY[0][y], HL, False, False) for y in range(2)]
                + [(C(o, y, 16, 2), LY[1][y], HR, False, y == 1) for y in range(2)])
             SL = X("TU", 152, 168)
@@ -607,17 +613,23 @@ def build(par=PAR):
             if not last:
                 cp(X("WO", *blk), IND(X(CO, 0, 512), SL), "act")
             step("object")
-            o = X("PD", 256, 384)
-            mm([(o, I16, Xo, True, False), (o, IH[0], GG, False, False), (o, IH[1], GR, False, True)])
-            ts(Xn, o, 0.0, A.max, 255.0, A.min)
             rows = (1, 64 * b, 64 * b + 64)
             if not last:
+                o = X("PD", 256, 384)
+                mm([(o, I16, Xo, True, False), (o, IH[0], GG, False, False), (o, IH[1], GR, False, True)])
+                ts(Xn, o, 0.0, A.max, 255.0, A.min)
                 spread(b, Xn, X(CV, 256, 512))
                 cp(X("WV", *blk), IND(X(CV, 0, 512), SL), "act")
             else:
                 o = X("PD", 256, 512)
-                mm([(P(C(o, y, 256, 2), 64 * h, 64 * h + 64), C(SEL[y], 0, 64), src, True, True) for h, src in enumerate((Xo, Xn)) for y in range(2)])
-                cp(X("W5", 256, 512), o, "act")
+                oy = lambda y, h: P(C(o, y, 256, 2), 64 * h, 64 * h + 64)
+                step("own")
+                mm([(oy(y, 0), C(SEL[y], 0, 64), Xo, True, True) for y in range(2)]
+                   + [(oy(0, 1), C(SEL[0], 0, 64), Xo, True, False), (oy(0, 1), C(SEL[0], 0, 64), GG, False, True),
+                      (oy(1, 1), C(SEL[1], 0, 64), Xo, True, False)])
+                step("object")
+                mm([(oy(1, 1), C(SEL[1], 0, 64), GR, False, True)])
+                ts(X("W5", 256, 512), o, 0.0, A.max, 255.0, A.min)
                 cp(X("W5", 512, 768), IND(X("W5", 0, 512), SL), "act")
                 cp(X("YN", 0, 256), IND(X("N5", 0, 512), SL))
                 dma("sp", R("yx", 0, 256, *rows), X("W5", 256, 512, 1, 64, 128), 32, osem["sp"])
@@ -793,18 +805,29 @@ def lay(ops, dep, cycle, hop):
             key[j] = min([key[i] - lag for i, lag in suc[j] if key[i] is not None] or [1e3]) + AHEAD.get(ops[j]["kind"], 0.0)
     for j in ranked(range(n), pre, suc):
         if key[j] is None:
-            key[j] = max([key[i] + lag for i, lag in pre[j]] + [0.0])
+            key[j] = max([key[i] + lag for i, lag in pre[j]] + [0.0]) + AHEAD.get(ops[j]["kind"], 0.0)
     t = place(ops, ranked(key, pre, suc), pre, False)
-    for _ in range(2):
+    for _ in range(PASSES):
         t = place(ops, ranked([-t[i] - o["dur"] for i, o in enumerate(ops)], suc, pre), suc, True)
         t = place(ops, ranked([-t[i] - o["dur"] for i, o in enumerate(ops)], pre, suc), pre, False)
     return ops, dep, ranked(t, pre, suc), t, [t[i] + o["dur"] + o["lat"] for i, o in enumerate(ops)]
 
 
-AHEAD = {(5, 1): -2.5, (5, 0): 3.0}
-CYCLE = {'sp': 'old.1/1 old.0/2', 'act': 'abs2.0/3 abs3.0/3 O1.0/2 mark.1/3 O2.0/2 name0.4/2 df.0/3 name0.6/2 O3.0/2 object.3/4 claim.7/3 last0.1/2 df.2/3 name1.4/2 dm.0/3 name1.6/2 zq.1/2 object.4/4 zq.0/2 last1.1/2 abs0.0/2 mod1.1/2 abs1.0/2 turn.1/1 slot.2/3 E.1/1', 'pe': 'object.0/4 E.2/2 abs1.1/3 abs2.1/3 rows.0/2 abs3.1/3 rows.1/2 name0.0/2 name0.1/2 name0.2/2 name0.3/2 pick.4/3 object.2/4 name1.0/2 name0.5/2 claim.0/3 name1.1/2 name0.7/2 df.1/3 claim.4/3 claim.5/3 name1.2/2 last0.0/2 claim.8/3 name1.3/2 fired.0/3 name1.5/2 state.0/3 name1.7/2 z.0/3 base.0/2 last1.0/2 head.0/2 mod1.0/2 mod2.0/2 mod1.2/2 slot.0/3 turn.0/1 abs0.1/2 E.0/1 E2.0/1', 'dve': 'E.3/2 z.3/4 O0.0/2 pick.0/3 mark.0/3 pick.1/3 object.1/4 pick.2/3 mark.2/3 pick.3/3 mark.4/3 mark.3/3 pick.5/3 mark.5/3 pick.6/3 mark.6/3 claim.1/3 claim.3/3 claim.2/3 eq0.0/2 future.0/3 claim.6/3 za.0/3 future.1/3 future.2/3 claim.9/3 last0.2/2 acts.0/3 last0.3/2 flag.0/3 last0.4/2 state.1/3 last0.5/2 state.2/3 eq1.0/2 V0.0/2 last1.2/2 z.2/3 V1.0/2 mod1.3/2 z.1/3 slot.1/3 V2.0/2 V3.0/2', 'g': 'z.4/4 dm.1/3 state.3/3'}
-CYCLE = {'dve': 'claim.9/2 flag.0/2 acts.0/2 za.0/2 last0.2/1 future.8/2 last0.3/1 last1.2/1 last0.4/1 acts.2/2 last1.3/1 acts.3/2 last0.5/1 last1.4/1 acts.4/2 V0.0/1 last1.5/1 V1.0/1 slot.1/2 V2.0/1 V3.0/1 object.1/2 state.1/2 O0.0/0 pick.0/1 state.3/2 pick.1/1 mark.0/1 state.2/2 pick.2/1 future.0/1 pick.3/1 future.1/1 future.2/1 mark.2/1 mark.4/1 mark.3/1 pick.5/1 mark.5/1 pick.6/1 mark.6/1 claim.3/1 claim.2/1 claim.1/1 eq0.0/0 claim.6/1 eq1.0/0', 'pe': 'rows.0/1 rows.1/1 last1.0/1 acts.1/2 head.0/1 slot.0/2 state.0/2 base.0/2 fired.0/2 abs0.1/1 object.0/2 abs1.1/1 object.2/2 abs2.1/1 abs3.1/1 name0.0/0 name0.1/0 name0.2/0 name0.3/0 name1.0/0 name1.1/0 pick.4/1 future.3/1 name1.2/0 name0.5/0 name1.3/0 claim.0/1 df.1/1 name0.7/0 name1.5/0 claim.4/1 claim.5/1 name1.7/0 turn.0/0 future.5/1 claim.8/1 future.6/1 last0.0/0', 'act': 'dm.0/2 future.7/2 last0.1/1 last1.1/1 zq.0/1 object.4/3 abs0.0/1 abs1.0/1 slot.2/2 abs2.0/1 abs3.0/1 O1.0/0 O2.0/0 mark.1/1 O3.0/0 name0.4/0 df.0/1 name0.6/0 name1.4/0 object.3/2 future.4/1 name1.6/0 zq.1/0 df.2/1 claim.7/1 turn.1/0', 'g': 'dm.1/2 acts.5/2 state.4/2', 'sp': 'old.0/1 old.1/0'}
-CYCLE = {'dve': 'V2.0/1 slot.1/2 V3.0/1 state.1/2 state.3/2 state.2/2 object.1/2 O0.0/0 pick.0/1 pick.1/1 mark.0/1 pick.2/1 future.0/1 pick.3/1 mark.2/1 future.2/1 mark.3/1 mark.4/1 future.1/1 pick.5/1 mark.5/1 pick.6/1 mark.6/1 future.4/1 claim.1/1 claim.2/1 claim.3/1 za.0/1 turn.1/0 eq0.0/0 claim.6/1 eq1.0/0 claim.9/1 flag.0/1 acts.0/1 last0.2/0 last1.2/0 last0.3/0 last1.3/0 last0.4/0 last1.4/0 last0.5/0 last1.5/0 acts.3/1 acts.2/1 V0.0/0 acts.4/1 V1.0/0', 'act': 'abs1.0/1 abs2.0/1 slot.2/2 abs3.0/1 O1.0/0 O2.0/0 mark.1/1 O3.0/0 name0.4/0 turn.0/0 future.3/1 name0.6/0 name1.4/0 zq.1/0 object.3/2 name1.6/0 df.0/1 claim.7/1 turn.3/0 future.6/1 df.2/1 zq.0/0 last0.1/0 last1.1/0 dm.0/1 future.8/1 object.4/2 fmod.1/1 abs0.0/0', 'pe': 'slot.0/2 head.0/1 base.0/2 fired.0/2 object.0/2 abs2.1/1 abs3.1/1 object.2/2 name0.0/0 name0.1/0 name0.2/0 name0.3/0 name1.0/0 pick.4/1 name1.1/0 name1.2/0 name0.5/0 name1.3/0 claim.0/1 name0.7/0 name1.5/0 claim.4/1 claim.5/1 name1.7/0 future.5/1 turn.2/0 df.1/1 claim.8/1 last0.0/0 last1.0/0 rows.0/0 future.7/1 acts.1/1 fmod.0/1 state.0/1', 'g': 'state.4/2 dm.1/1 acts.5/1', 'sp': 'old.1/0 old.0/0'}
+AHEAD = {(5, 1): -5.5, (5, 0): 2.5, "nm0": -18.5, "nm1": -2.5, "logWO0": -5.0, "logWV0": -2.5, "logWV1": -11.0, "zero": -6.0, "E": -4.0,
+         "old": -7.5, "out": -19.0, "own": -1.5, "object": -7.5, "slot": 8.0, "z": 20.0, "state": 30.5}
+CYCLE = {
+    "sp": "old.1/0 old.0/0",
+    "act": "O1.0/0 O2.0/0 O3.0/0 name0.4/0 turn.0/0 future.4/1 object.3/2 name0.6/0 name1.4/0 df.0/1 turn.3/0 name1.6/0 future.7/1 "
+           "object.4/2 claim.7/1 last0.1/0 future.9/1 zq.0/0 zq.1/1 df.2/1 last1.1/0 fmod.1/1 dm.0/1 za.1/1 abs1.0/0 abs0.0/0 abs2.0/0 "
+           "slot.2/1 abs3.0/0",
+    "dve": "O0.0/0 z.2/2 pick.0/1 mark.0/1 pick.1/1 future.0/1 mark.1/1 pick.2/1 future.1/1 future.2/1 mark.2/1 mark.3/1 mark.4/1 "
+           "future.3/1 pick.4/1 mark.5/1 pick.5/1 turn.1/0 mark.6/1 future.5/1 claim.2/1 claim.3/1 claim.1/1 eq0.0/0 claim.6/1 eq1.0/0 "
+           "last0.2/0 claim.9/1 flag.0/1 last0.3/0 acts.0/1 last0.4/0 last1.2/0 V1.0/0 acts.2/1 last1.3/0 state.1/1 acts.3/1 last1.4/0 "
+           "V0.0/0 V2.0/0 slot.1/1 V3.0/0 za.0/1 state.2/1 object.1/1 z.1/1",
+    "pe": "object.2/2 abs3.1/1 name0.0/0 name0.1/0 name0.2/0 name0.3/0 name1.0/0 pick.3/1 name1.1/0 name1.2/0 name0.5/0 name1.3/0 "
+          "claim.0/1 turn.2/0 name0.7/0 name1.5/0 future.6/1 claim.4/1 claim.5/1 name1.7/0 last0.0/0 future.8/1 rows.0/0 claim.8/1 "
+          "df.1/1 last1.0/0 fmod.0/1 base.0/1 state.0/1 acts.1/1 head.0/0 z.0/1 slot.0/1 object.0/1 abs2.1/0",
+    "g": "z.3/2 flag.1/1 dm.1/1 acts.4/1 state.3/1"}
 GRAPH = plan()
 PLAN = lay(GRAPH[0], GRAPH[1], CYCLE, PAR["HOP"])
 
@@ -883,7 +906,7 @@ def rank_program(g, core, T, topo):
             ins = q.dma_start(ap(c[1]), ap(c[2]), accum_op=A.add, max_dma_last_dim=8192)
             sem, inc = o["sem"], 16
         elif k == "scan":
-            ins = q.tensor_tensor_scan(ap(c[1]), ap(c[2]), ap(c[3]), 0.0, A.add, A.max)
+            ins = q.tensor_tensor_scan(ap(c[1]), ap(c[2]), ap(c[3]), 0.0, c[4], c[5])
         elif k == "dma":
             ins = q.dma_start(ap(c[1]), ap(c[2]))
             sem, inc = o["sem"], 16

import math
from concourse.mybir import AluOpType as A, ActivationFunctionType as F

VIS, NB = 6, 2
SW, MW, CW = 32, 144, 384
BF, FP, I3, U2 = "bfloat16", "float32", "int32", "uint16"
SCRATCH = {}
for _b in range(NB):
    for _n, _w, _d in (("DA", 4096, BF), ("GV", 4096, BF), ("WO", 4096, FP), ("WV", 4096, FP), ("OG", 2048, FP),
                       ("EQ", 1024, BF), ("ST", VIS * SW, FP), ("SO", VIS * SW, FP),
                       ("ZI", VIS * 128, BF), ("ZO", VIS * 128, BF), ("EU", VIS * 128, U2), ("EO", VIS * 128, U2), ("ML", VIS * MW, BF), ("MO", VIS * MW, BF),
                       ("CA", 512, FP), ("CB", 512, FP), ("W5", 768, BF), ("N5", 512, I3), ("YN", 256, FP),
                       ("DF", CW, BF), ("MK", VIS * CW, BF), ("XP", 256, BF), ("XS", 256, BF), ("TH", 128, BF), ("HB", 64, BF),
                       ("TF", 10 * 128, FP), ("TI", 3 * 128, I3), ("ZB", 768, FP), ("UU", 144, BF), ("TB", 12 * 128, BF), ("TU", 384, U2),
                       ("SF", 192, FP), ("SI", 64, I3), ("SB", 64, BF), ("SN", 128, I3),
                       ("DX", 320, FP), ("DY", 160, BF)):
        SCRATCH["%s%d" % (_n, _b)] = ("sbuf", [128, _w], _d)
    for _n in "ABCD":
        SCRATCH["P%s%d" % (_n, _b)] = ("psum", [128, 512], FP)
for _n, _w, _d in (("NI", 512, I3), ("NW", 1024, FP), ("NH", 512, BF), ("PI", 64, I3), ("PF", 128, FP), ("KB", 59 * 128, BF),
                   ("KF", 3 * 128, FP), ("KS", 256, BF), ("OI", 80, FP), ("OU", 80, U2), ("CS", 128, I3), ("TT", 128, FP),
                   ("V0", 128, BF), ("NV", 128, FP)):
    SCRATCH[_n] = ("sbuf", [128, _w], _d)
OUTS = ("yn", "yo", "yv", "yx", "yc", "ys", "ya", "yz")
ENG = ("g", "pe", "dve", "act", "sp")
NDS = 60
SEMAPHORES = ["c_" + e for e in ENG] + ["d%d" % i for i in range(NDS)] + ["sent"] + \
    ["r%d_%d_%d" % (m, b, t) for m in range(5) for b in range(NB) for t in range(VIS)]
LN2 = math.log(2.0)
TOP = 41.5
WB = 2 * TOP / 64
W1 = 185.0 / 1024
BIG = 786432.0
ONE, W32 = 1.5 * 2 ** 23, 1.5 * 2 ** 28
PAR = dict(HOP=0.2, GC=1.3, SC=3.8, CY=0.00083, PC=0.00042, RI=0.4, RL=1.7, FX=0.015, PX=0.0)
LOOK = 0.05
LEAD = 4.0
OQ = (32, 0, 0, 0)
VP = (32, 32, 32, 32)
LOGQ = dict(WO0=("dve", "act") * 4, WV0=("dve", "dve", "dve", "act") * 2, WO1=("dve", "act") * 4)
LOGB = dict(WO0=("PA0", "PD0", "PA1", "PB1", "PD1"), WV0=("PA1", "PB1", "PD1"), WO1=("PA1", "PD1", "PB1"), WV1=("PD1",))
PEMOD, SQ, SPEC = (), "dve", True
HQ, SP = "act", ((0, 96), (96, 128))
FUT, MERGE = True, 0
BYG = ("WV1",)
SLB = "PD"
ZSEND = True
NM, EQP = 2, 1
HQ0 = "act"
FSEND = True
PASSES = 2
GVE = 2
NUDGE = {}


def R(buf, c0, c1, step=1, p0=0, p1=128, pstep=1):
    return (buf, c0, c1, step, p0, p1, pstep)


def P(r, p0, p1, pstep=1):
    return (r[0], r[1], r[2], r[3], p0, p1, pstep)


def C(r, a, e, step=1):
    return (r[0], r[1] + a, r[1] + e, step, r[4], r[5], r[6])


def IND(win, off):
    return ("ind", win, off)


def n_of(r):
    if r[0] == "ind":
        return 16 * n_of(r[2])
    return (r[2] - r[1] + r[3] - 1) // r[3]


def two(r):
    return SCRATCH[r[0]][2] in (BF, U2)


def psum(r):
    return r[0] in SCRATCH and SCRATCH[r[0]][0] == "psum"


def build(par=PAR):
    GC, SC_, CY, PC = par["GC"], par["SC"], par["CY"], par["PC"]
    ops = []
    now = dict(bias=0.0, step="start", t=-1, b=0, n=0, seen={})

    def step(name):
        now["seen"][now["step"]] = now["n"]
        now["step"], now["n"] = name, now["seen"].get(name, 0)

    def add(eng, call, reads, writes, dur, **kw):
        rd, wr = [], []
        for r in reads:
            if isinstance(r, tuple):
                rd += [r[1], r[2]] if r[0] == "ind" else [r]
        for w in writes:
            if w[0] == "ind":
                wr.append(w[1])
                rd.append(w[2])
            else:
                wr.append(w)
        o = dict(eng=eng, call=call, reads=rd, writes=wr, dur=dur, lat=0.0, sem=None, after=None, recv=None)
        o["bias"], o["kind"], o["t"], o["b"] = now["bias"], now["step"], now["t"], now["b"]
        o["pos"] = "%s.%d" % (now["step"], now["n"]) if now["t"] >= 0 else now["step"]
        now["n"] += 1
        o.update(kw)
        ops.append(o)
        return len(ops) - 1

    def cost(out, ins, mul=1.0):
        n = n_of(out)
        if out[0] == "ind":
            return 0.06 + n * SC_ * CY
        if ins[0][0] == "ind":
            return 0.06 + n * GC * CY
        if mul == 1.0 and two(out) and all(two(i) for i in ins):
            mul = 0.5
        return par["FX"] + max(64, n * mul) * CY

    def ts(out, a, s1, o0, s2=None, o1=None):
        return add("dve", ("ts", out, a, s1, s2, o0, o1), [a, s1, s2], [out], cost(out, [a]))

    def tt(out, a, b, op):
        m = 1.0 if (a[0] == "ind" or psum(a) or psum(b)) else 2.0
        return add("dve", ("tt", out, a, b, op), [a, b], [out], cost(out, [a, b], m + 1e-9))

    def cp(out, a, eng="dve"):
        if eng == "act":
            return act(out, a, F.Identity)
        return add("dve", ("cp", out, a), [a], [out], cost(out, [a]))

    def act(out, a, f, bias=0.0, scale=1.0, extra=0.0):
        return add("act", ("act", out, a, f, bias, scale), [a, bias, scale], [out], 0.04 + extra + cost(out, [a], 1.0 + 1e-9))

    def mm(lst):
        d, rd, wr = 0.0, [], []
        for (o, l, r, st, sp) in lst:
            d += max(min(64, n_of(l)), n_of(r)) * (1 if two(l) else 4) * PC + par["PX"]
            rd += [l, r]
            wr.append(o)
        return add("pe", ("mm", lst), rd, wr, 0.03 + d)

    def scan(out, d0, d1, o0, o1):
        return add("dve", ("scan", out, d0, d1, o0, o1), [d0, d1], [out], 0.03 + n_of(out) * CY)

    def mset(out, v):
        return add("dve", ("ms", out, v), [], [out], cost(out, [out]))

    def iota(out, pat, base=0, cm=0):
        return add("g", ("io", out, pat, base, cm), [], [out], 0.13 + 2 * n_of(out) * CY)

    def asel(out, pat, op, fill, base, cm, a=None):
        return add("g", ("as", out, pat, op, fill, base, cm, a or out), [a or out], [out], 0.17 + 2 * n_of(out) * CY)

    nds = [0]

    def newsem():
        nds[0] += 1
        return "d%d" % (nds[0] - 1)

    def dma(q, out, a, kb, sem=None):
        rd = [a] if a[0] in SCRATCH else []
        return add(q, ("dma", out, a), rd, [out], 0.1 if q != "g" else 1.0, lat=1.8, sem=sem or newsem(), kb=kb)

    def send(dst, src, sem):
        i = add("g", ("rd", dst, src, sem), [src], [], par["RI"], lat=par["RL"] + n_of(src) * (2 if two(src) else 4) * 0.0006, sem="sent")
        add("none", None, [], [dst], 0.0, after=i, recv=sem)

    PIc = lambda j, n=1: R("PI", j, j + n)
    PFc = lambda j, n=1: R("PF", j, j + n)
    K = lambda j, n=128: R("KB", 128 * j, 128 * j + n)
    KF = lambda j, n=128: R("KF", 128 * j, 128 * j + n)
    KS = lambda a, n: R("KS", a, a + n)
    osem = {q: newsem() for q in ("sp", "act")}

    seq = [dma("sp", R("NI", 0, 128), R("nm", 0, 4096, 1, 0, 4), 64)]
    for j, nme in enumerate(("c0", "s0")):
        dma("act", R("CS", 0, 128, 1, 16 * j, 16 * j + 16), R(nme, 0, 256, 1, 0, 8), 8)
    iota(PIc(0), [[0, 1]], 0, 1)
    iota(R("NI", 256, 512), [[1, 256]])
    def code(a, e):
        ts(R("NW", a, e), R("NI", a, e), 128.0, A.is_lt, -257.0, A.mult)
        tt(R("NW", 512 + a, 512 + e), R("NW", a, e), R("NI", a, e), A.add)

    code(256, 512)
    for b in range(NB):
        step("nm%d" % b)
        code(128 * b, 128 * b + 128)
        act(R("NH", 128 * b, 128 * b + 128), R("NW", 512 + 128 * b, 640 + 128 * b), F.Identity, 256.0, 256.0)
        step("start")
        for w, nme in (("DA", "vo"), ("GV", "vn")):
            if w == "GV" and "WV%d" % b in BYG:
                for c in range(4):
                    if c == 2:
                        seq.append(dma("sp", R("V0", 0, 128), R(nme, 0, 4096, 1, 64 * b, 64 * b + 64, 16), 32))
                    for h in range(2):
                        seq.insert(len(seq) - (3 if c < GVE else 0),
                                   dma("sp", R("GV%d" % b, 1024 * c, 1024 * c + 1024, 1, 64 * h, 64 * h + 64),
                                                                         R(nme, 1024 * c, 1024 * c + 1024, 1, 64 * b, 64 * b + 64), 128))
                continue
            for c in range(2):
                seq.append(dma("sp", R("%s%d" % (w, b), 2048 * c, 2048 * c + 2048, 1, 0, 64), R(nme, 2048 * c, 2048 * c + 2048, 1, 64 * b, 64 * b + 64), 256))
            seq.insert(len(seq) - (0 if (b, w) == (0, "DA") else 2), dma("sp", R("%s%d" % (w, b), 0, 4096, 1, 64, 68), R("NH", 128 * b, 128 * b + 128), 32))
            if (b, w) == (0, "DA"):
                seq.append(dma("sp", R("NI", 128, 256), R("nm", 0, 4096, 1, 4, 8), 64))
        for h in range(2):
            seq.append(dma("sp", R("ZI%d" % b, 0, 128, 1, 64 * h, 64 * h + 64), R("z0", 128 * h, 128 * h + 128, 1, 64 * b, 64 * b + 64), 16))
        seq.append(dma("sp", R("XS%d" % b, 0, 256, 1, 0, 64), R("xo", 0, 256, 1, 64 * b, 64 * b + 64), 32))

    cP, ca, cg8, ch, cg, c64, ca8, ca7, cq, cr, ck = range(11)
    for j, (sh, mk) in enumerate(((0, 15), (4, 7), (6, 1), (4, 3), (0, 63), (3, 1), (0, 7), (5, 3), (4, 1), (3, 15))):
        ts(PIc(1 + j), PIc(0), sh, A.arith_shift_right, mk, A.bitwise_and)
    cp(PFc(0, 11), PIc(0, 11))
    (cbase, cdup, cz, c16a, cz128, cnh, ctp, cty, cf00, cf01, cf10, cf11, cna8, ct1, ct2, ct3, cw, cnb, cnz, cg4) = range(11, 31)
    IC, M16, G8, G4, M64 = K(0), K(1), K(2), K(3), K(4, 192)
    iota(C(M64, 0, 192), [[0, 3], [1, 64]])
    iota(IC, [[1, 128]])
    iota(M16, [[0, 8], [1, 16]])
    iota(G8, [[1, 8], [0, 16]])
    M64 = C(M64, 0, 128)
    DUP, I16, MA, I16x, PM, PM2 = K(6), K(7), K(8), K(9), K(10), K(11)
    I32, D0, MSK = KF(0), KF(1), K(58)
    ts(PFc(ct1), PFc(cP), -64.0, A.add, 0.0, A.max)
    ts(PFc(ct1), PFc(ct1), 15.0, A.mult, PFc(c64), A.add)
    ts(DUP, M64, PFc(ct1), A.is_equal)
    ts(PFc(cz), PFc(ca), 0.0, A.is_equal)
    ts(MSK, G8, PFc(ca7), A.is_equal)
    lin = lambda out, a, scale, bias=0.0: act(out, a, F.Identity, bias, scale)
    lin(PFc(cna8), PFc(ca8), -1.0, 1.0)
    c0, s0, s1, f2, d2, aP, aS, a16, aN, bA = (PFc(80 + j) for j in range(10))
    for f, v, fl in ((c0, 0.0, cna8), (s0, 0.0, ca8), (s1, 1.0, ca8), (f2, 2.0, cna8), (d2, 2.0, ca8)):
        ts(f, PFc(cq), v, A.is_equal, PFc(fl), A.mult)
    lin(aP, s0, 7.5, c0)
    lin(aP, s1, -0.000354, aP)
    lin(aS, s0, W1)
    lin(aS, s1, 1.0 / (8 * LN2) - W1, aS)
    lin(a16, s0, 16.0, c0)
    lin(aN, f2, -1.0, a16)
    lin(bA, d2, 1.0, s0)
    RE0, REP, RSP, REN, REA, I16y = (K(52 + j) for j in range(6))
    for m, al, be in ((RE0, c0, s0), (REP, aP, s0), (REN, aN, s0), (REA, a16, bA)):
        lin(m, M16, be, al)
        tt(m, m, MSK, A.mult)
    lin(RSP, MSK, aS)
    ts(I16, IC, PFc(cP), A.is_equal)
    I32 = C(I32, 0, 32)
    lin(I32, C(I16, 0, 32), 1.0)
    lin(I16y, I16, 16.0)
    lin(I16x, I16, 32.0)
    NI16 = K(51)
    lin(NI16, I16, -1.0)
    CODE = R("NH", 256, 512)
    lin(PFc(105), PFc(cz), 256.0)
    lin(CODE, R("NW", 768, 1024), PFc(105), PFc(105))
    lin(PFc(cnh), PFc(ch), -1.0, 1.0)
    SEL = [K(12), K(13)]
    for h, fl in ((0, cnh), (1, ch)):
        ts(SEL[h], M64, PFc(c64), A.is_equal, PFc(fl), A.mult)
    fill = lambda out, v: iota(out, [[0, n_of(out)]], v)

    def spread(b, src, out):
        o = R("PD%d" % b, 256, 512)
        mm([(o, I16, CODE, True, False)] + [(C(o, y, 256, 2), SEL[y], src, False, y == 1) for y in range(2)])
        cp(out, o, "act")

    TT = R("TT", 0, 128, 1, 0, 32)
    cp(TT, R("CS", 0, 128, 1, 0, 32))
    for b in range(NB):
        X = lambda nme, a, e, *k: R("%s%d" % (nme, b), a, e, *k)
        mm([(X("PC", 128 + 8 * j + 4 * h, 132 + 8 * j + 4 * h), TT, P(C(I32, 16 * j + 8 * b + h, 16 * j + 8 * b + 8, 2), 0, 32), True, True)
            for j in range(2) for h in range(2)])
        cp(X("ST", 0, 16), X("PC", 128, 144), "act")
        fill(X("ST", 16, 24), 1792)
        fill(X("SF", 80, 88), -32)
        fill(X("DF", 256, CW), 0)
        for w, s in (("WO", "DA"), ("WV", "GV")):
            step("log%s%d" % (w, b))
            if w + str(b) in BYG:
                for c in range(4):
                    asel(X(w, 1024 * c, 1024 * c + 1024), [[0, 1024]], A.is_ge, 0.0, 0, 0, X(s, 1024 * c, 1024 * c + 1024))
                tt(R("NV", 0, 128), R("V0", 0, 128), R("NH", 128 * b, 128 * b + 128), A.add)
                for h in range(2):
                    dma("sp", X(w, 0, 4096, 1, 64 * h, 64 * h + 64, 16), R("NV", 0, 128), 64)
                continue
            banks = LOGB[w + str(b)]
            for c in range(8):
                bank = R(banks[c % len(banks)], 0, 512)
                mm([(bank, P(DUP, 0, 68), X(s, 512 * c, 512 * c + 512, 1, 0, 68), True, True)])
                cp(X(w, 512 * c, 512 * c + 512), bank, LOGQ[w + str(b)][c])
        step("start")
        mm([(X("PD", 0, 128, 1, 64 * y, 64 * y + 64), P(C(I16, 0, 64), 0, 64), X("XS", y, 256, 2, 0, 64), True, True) for y in range(2)])
        cp(X("XP", 0, 128), X("PD", 0, 128), "act")
        spread(b, X("XP", 0, 128), X("CA", 256, 512))
    tE, tL, inv, dl, wE = PFc(32, 8), PFc(40, 8), PFc(48, 8), PFc(56, 8), KS(0, 8)
    lin(PFc(cbase), PFc(cg8), 16.0)
    iota(PIc(16, 8), [[1, 8]], 1, 1)
    iota(R("OI", 64, 72), [[-1, 8]], 15)
    ts(PIc(24, 8), R("OI", 64, 72), PFc(ck), A.add)
    ts(PIc(32, 16), PIc(16, 16), 15, A.bitwise_and)
    lin(PFc(cnb), PFc(ca7), 16.0)
    ts(inv, PIc(40, 8), PFc(cnb), A.add)
    ts(tE, PIc(32, 8), PFc(ca), A.min, PFc(cbase), A.add)
    ts(tL, PIc(32, 8), PFc(ca), A.max, PFc(cbase), A.add)
    tt(dl, tL, tE, A.subtract)
    act(PFc(cw), PFc(c64), F.Exp, -WB, -WB, 1.3)
    ops[act(wE, dl, F.Exp, -60 * LN2, 8 * LN2)]["reads"].append(PFc(cw))
    lin(PFc(72, 7), C(wE, 0, 7), 1.0)
    lin(PFc(79), C(wE, 7, 8), PFc(cna8))
    DM = [K(14 + d) for d in range(8)]
    WM = [K(22 + d) for d in range(8)]
    PN = [K(30 + d) for d in range(8)]
    for d in range(8):
        ts(DM[d], IC, PFc(48 + d), A.is_equal)
    for c in range(2):
        asel(K(14 + 4 * c, 512), [[0, 4], [1, 8], [8, 16]], A.not_equal, -1.0, 0, -1)
    for d in range(8):
        ts(WM[d], IC, PFc(32 + d), A.is_equal, PFc(72 + d), A.mult)
    for d in range(8):
        ts(PN[d], IC, PFc(40 + d), A.is_equal, -262144.0, A.mult)
    S64, NS1, PS1, C256, W4, C16, C16h, CA24, AR = (KS(16, 8), KS(24, 8), KS(32, 8), KS(40, 8), KS(48, 8), KS(64, 16), KS(80, 16),
                                                    KS(96, 24), [KS(128, 24), KS(160, 24)])
    SELN = PFc(112, 8)
    ts(PS1, K(0, 8), PFc(cg8), A.is_equal)
    for r, v in ((SELN, PFc(cz)), (S64, 64.0), (NS1, -1.0)):
        lin(r, PS1, v)
    iota(C256, [[256, 8]])
    iota(C16, [[16, 16]])
    for j, v in enumerate((1, 0, 56)):
        fill(C(CA24, 8 * j, 8 * j + 8), v)
    iota(KS(192, 24), [[0, 3], [1, 8]])
    lin(PFc(cnz), PFc(cz), -1.0)
    lin(PFc(cg4), PFc(cg), 1.0, 4.0)
    for h, c in ((0, cg), (1, cg4)):
        ts(AR[h], KS(192, 24), PFc(c), A.is_equal, PFc(cnz), A.mult)
    fill(D0, 1)
    asel(D0, [[0, 8], [1, 16]], A.not_equal, -4000000.0, 0, 0)
    ts(MA, M16, PFc(ca), A.is_equal)
    J2, RED, IOH, IU, SF72, ONES = K(38, 64), K(39), K(40, 256), K(42, 64), K(43, 72), K(44)
    SF64 = C(SF72, 0, 64)
    ts(J2, K(4, 64), PFc(c64), A.is_equal)
    tt(RED, REA, REN, A.subtract)
    cp(C(SF72, 64, 72), PS1)
    for b in range(NB):
        fill(R("UU%d" % b, 64, 72), 1)
        fill(R("ZB%d" % b, 0, 256, 2), 0)
        fill(R("ZB%d" % b, 256, 768, 2), 0)
    lin(PFc(c16a), PFc(ca), 16.0, 15.0)
    fill(ONES, 1)
    O = lambda a, n: R("OI", a, a + n)
    iota(O(0, 8), [[1, 8]])
    iota(O(8, 8), [[16, 8]], 1)
    iota(O(16, 16), [[1, 8], [0, 2]])
    iota(O(32, 4), [[2, 4]], 8)
    ts(O(32, 4), O(32, 4), PFc(ca8), A.add)
    cp(R("OU", 0, 36), O(0, 36))
    LB, LOH, LU = (R("OU", a, a + n) for a, n in ((0, 8), (16, 16), (32, 4)))
    iota(IOH, [[0, 8], [1, 2], [2, 16]])
    iota(IU, [[0, 8], [1, 8]])
    iota(SF64, [[1, 8], [0, 8]])
    ts(SF64, SF64, PFc(cg8), A.is_equal)
    lin(PFc(66), PFc(cw), PFc(cnh))
    lin(PFc(67), PFc(cw), PFc(ch), PFc(cnh))
    IH = [K(49), K(50)]
    for h, fl in ((0, cnh), (1, ch)):
        lin(IH[h], I16, PFc(fl))
    lin(PFc(106), PFc(ca), -WB / 2)
    ops[act(W4, O(8, 8), F.Exp, PFc(106), -WB / 2)]["reads"].append(PFc(cw))
    LY = [[K(45), K(46)], [K(47), K(48)]]
    lin(PFc(ct2), PFc(cr), 64.0, PFc(ca))
    lin(PFc(ctp), PFc(cq), 16.0, PFc(ct2))
    ts(PM, IC, PFc(ctp), A.is_equal)
    lin(PM2, PM, 2.0)
    lin(PFc(ct3), PFc(ca7), 2.0, PFc(ch))
    lin(PFc(cty), PFc(cg), 16.0, PFc(ct3))
    ts(G4, M64, PFc(cty), A.is_equal, 256.0, A.mult)
    for h, fl in ((0, cnh), (1, ch)):
        for y, fy in ((0, cna8), (1, ca8)):
            c = cf00 + 2 * h + y
            lin(PFc(c), PFc(fl), PFc(fy))
            lin(LY[h][y], G4, PFc(c))
    I128 = KF(2)
    lin(I128, I16, 1.0)
    step("zero")
    for b in range(NB):
        for t in range(VIS):
            iota(R("MK%d" % b, CW * t, CW * t + CW), [[0, CW]])
        iota(R("N5%d" % b, 0, 512), [[0, 2], [1, 256]])
    csem = [[newsem() for _ in range(2)] for _ in range(NB)]

    for t in range(VIS):
        for b in range(NB):
            last = t == VIS - 1
            X = lambda nme, a, e, *k: R("%s%d" % (nme, b), a, e, *k)
            TF = lambda j, n=128: X("TF", 128 * j, 128 * j + n)
            TI = lambda j, n=128: X("TI", 128 * j, 128 * j + n)
            TB = lambda j, n=128: X("TB", 128 * j, 128 * j + n)
            SI = lambda a, n=8: X("SI", a, a + n)
            SF = lambda a, n=8: X("SF", a, a + n)
            s0, e0, m0, n0 = SW * t, 128 * t, MW * t, SW * (t + 1)
            CSi, Si, Ai, Zi = X("ST", s0, s0 + 16), X("ST", s0 + 8, s0 + 16), X("ST", s0 + 16, s0 + 24), X("ZI", e0, e0 + 128)
            if t and not ZSEND:
                Zi = X("ST", s0 + 24, s0 + 152)
            now.update(bias=LEAD if b == 0 else 0.0, t=t, b=b, step="", seen={})
            CO, CV = ("CA", "CB") if t % 2 == 0 else ("CB", "CA")
            Xo, Xn = X("XP", 128 * (t % 2), 128 * (t % 2) + 128), X("XP", 128 - 128 * (t % 2), 256 - 128 * (t % 2))
            blk = (256 * t, 256 * t + 256)
            step("old")
            if not last:
                for c, w in ((CO, "WO"), (CV, "WV")):
                    i = dma("sp", X(c, 0, 256), X(w, *blk), 128, csem[b]["AB".index(c[1])])
                    seq += [] if t else [i]
            else:
                for h, nme in enumerate(("vo", "vn")):
                    seq.append(dma("sp", X("W5", 0, 256, 1, 64 * h, 64 * h + 64), R(nme, blk[0], blk[1], 1, 64 * b, 64 * b + 64), 32))
                dma("sp", X("N5", 0, 256, 1, 0, 64, 16), R("nm", blk[0], blk[1], 1, 4 * b, 4 * b + 4), 4)
            step("turn")
            T64, HB = X("TH", 0, 128, 1, 0, 64), lambda a, n: X("HB", a, a + n)
            cp(HB(0, 16), CSi, HQ0)
            tt(HB(16, 16), CSi, HB(0, 16), A.subtract)
            mm([(X("PC", 0, 128, 1, 32 * y, 32 * y + 32), HB(0, 32), I16, True, True) for y in range(2)])
            cp(T64, X("PC", 0, 128, 1, 0, 64), "act")
            EU = X("EU", e0, e0 + 128)
            if not (SPEC and t):
                step("E")
                o = X("PC", 384, 512)
                mm([(o, P(RE0, 0, 64), T64, True, True)])
                act(TB(9), o, F.Identity, BIG - 2047.5)
                mm([(o, P(RE0, 0, 64), T64, True, False), (o, NI16, TB(9), False, True)])
                ts(EU, o, BIG, A.add)
            step("rows")
            mm([(X("PC", 129, 384, 2), P(REP, 0, 64), T64, True, True), (X("PC", 128, 384, 2), P(RSP, 0, 64), T64, True, True)])
            step("zq")
            ZQ, ZY = TF(0), TF(1)
            act(ZQ, Zi, F.Identity, -0.25, 0.5)
            act(ZY, Zi, F.Abs, -0.4, 0.5)
            for c, bank in enumerate(("PA", "PB")):
                for y in range(2):
                    p = 2 * c + y
                    step("O%d" % p)
                    for a, e, q in ((32 * p, 32 * p + OQ[p], "dve"), (32 * p + OQ[p], 32 * p + 32, "act")):
                        if a < e:
                            cp(X("OG", 16 * a, 16 * e), IND(X("WO", 0, 4096), C(EU, a, e)), q)
                    step("name%d" % c)
                    for kk in range(0, 4, NM):
                        mm([(X(bank, 32 * y + 8 * k, 32 * y + 8 * k + 8), X("OG", 512 * p + k, 512 * p + 512, 4), SELN, True, True) for k in range(kk, kk + NM)])
                N1, N2 = C(TB(0), 64 * c, 64 * c + 64), C(TB(1), 64 * c, 64 * c + 64)
                act(N1, X(bank, 0, 64), F.Identity, -127.5)
                mm([(X(bank, 64 + 32 * y, 96 + 32 * y, 1, 32 * q, 32 * q + 32), C(N1, 32 * y, 32 * y + 32), C(I16, q, 128, 4), True, True)
                    for y in range(2) for q in range(4)])
                cp(N2, X(bank, 64, 128), "act")
                mm([(X(bank, d, 512, 8), DM[d], N2, True, True) for d in range(8)])
                step("eq%d" % c)
                ts(X("EQ", 512 * c, 512 * c + 512), X(bank, 0, 512), 0.0, A.is_equal)
                step("last%d" % c)
                o = X(bank, 0, 64)
                mm([(o, WM[d], X("EQ", 512 * c + d, 512 * c + 512, 8), d == 0, d == 7) for d in range(8)])
                h64 = lambda r: C(r, 64 * c, 64 * c + 64)
                a, e = 128 * c, 128 * c + 128
                i = act(X("ZB", a + 1, e, 2), o, F.Ln, 2.0 ** -60, 1.0, 1.5 if t + b + c == 0 else 0.0)
                ops[i]["reads"].append(W4)
                scan(X("TI", a, e), X("ZB", a, e), X("PC", 128 + a, 128 + e), A.mult, A.add)
                ts(h64(TI(2)), X("TI", a + 1, e, 2), 4095, A.bitwise_and)
                cp(h64(X("TU", 0, 128)), h64(TI(2)))
            step("head")
            mm([(X("PD", 0, 128), X("EQ", d, 1024, 8), PN[d], d == 0, False) for d in range(8)])
            r0, DD, AD = 0, X("DA", 0, 2048), X("DA", 2048, 4096)
            for c, w in enumerate(VP):
                a, e = 16 * r0, 16 * (r0 + w)
                step("V%d" % c)
                tt(C(DD, a, e), IND(X("WV", 0, 4096), X("TU", r0, r0 + w)), X("OG", a, e), A.subtract)
                step("abs%d" % c)
                act(C(AD, a, e), C(DD, a, e), F.Abs, 0.0, 0.5)
                r0 += w
                for a, e in SP:
                    if r0 - w < e <= r0:
                        mm([(X("PD", k, 128, 16, a, e), C(AD, 16 * a + k, 16 * e, 16), S64, False, k == 15) for k in range(16)])
            step("pick")
            SC = X("SN", 0, 128)
            scan(SC, D0, X("PD", 0, 128), A.add, A.max)
            KEY = C(SC, 15, 128, 16)
            ts(SI(8), KEY, 15, A.bitwise_and)
            tt(TB(2), IND(SI(8), LB), MA, A.mult)
            mm([(X("PA", 0, 8), I16, C256, True, False), (X("PA", 0, 8), TB(2), NS1, False, True)])
            FO = X("TU", 128, 136)
            ts(FO, X("PA", 0, 8), PFc(c16a), A.add)
            tt(TB(3), IND(AD, FO), ZQ, A.is_ge)
            step("mark")
            if SQ == "act":
                ts(SF(0), KEY, W32, A.add, -W32, A.add)
                act(SF(8), SF(0), F.Square, -3504.0, 1.0 / 32)
            else:
                ts(SI(48), KEY, 1.0 / 32, A.mult, -3504.24, A.add)
                tt(SF(8), SI(48), SI(48), A.mult)
            tt(SI(16), SF(8), Ai, A.add)
            ts(SI(24), SI(16), 5, A.arith_shift_right, 31, A.bitwise_and)
            ts(SI(32), SI(16), 10, A.arith_shift_right, 7, A.bitwise_and)
            OH, UU, UF, UW = TB(4, 256), X("UU", 0, 64), X("UU", 72, 144), TB(7)
            tt(UU, IND(SI(24, 16), LU), IU, A.is_equal)
            tt(OH, IND(SI(24), LOH), IOH, A.is_equal)
            step("claim")
            mm([(X("PA", 16, 88), I16x, X("UU", 0, 72), True, False), (X("PA", 16, 88), TB(3), SF72, False, True)])
            for y in range(2):
                ts(C(UW, y, 128, 2), X("PA", 16, 80), 40.5, A.is_ge, PFc(66 + y), A.mult)
            ts(UF, X("PA", 16, 88), 40.5, A.is_ge)
            o = lambda a, e, q, st=1: X("PA", 96 + a, 96 + e, st, 32 * q, 32 * q + 32)
            l = lambda h, q: C(OH, 128 * h + 32 * q, 128 * h + 32 * q + 32)
            uw = lambda h, q: C(UW, 64 * h + 16 * q, 64 * h + 16 * q + 16)
            uf = lambda h, q: C(UF, 32 * h + 8 * q, 32 * h + 8 * q + 8)
            mm([(o(0, 16, q), l(0, q), uw(0, q), True, True) for q in range(4)])
            lst = []
            for q in range(4):
                lst += [(o(16, 32, q), l(1, q), uw(1, q), True, False)] + [(o(16 + y, 32, q, 2), l(0, q), uf(0, q), False, y == 1) for y in range(2)]
            lst.append((X("PA", 128, 136), I16, W4, True, False))
            for q in range(4):
                lst += [(o(32, 40, q), l(h, q), uf(h, q), False, h == 1) for h in range(2)]
            mm(lst)
            ts(SF(16, 40), X("PA", 96, 136), math.exp(-2 * TOP), A.max, 1.0, A.min)
            act(X("SB", 0, 40), SF(16, 40), F.Ln, 0.0, math.exp(TOP))
            mm([(X("PA", 144, 152), PM, X("SB", 16 * j + y, 16 * j + 16, 2), j + y == 0, False) for j in range(2) for y in range(2)]
               + [(X("PA", 144, 152), PM2, X("SB", 32, 40), False, True)])
            LW = X("TU", 136, 144)
            ts(LW, X("PA", 144, 152), -1.0 / WB, A.mult, 191.125, A.add)
            step("flag")
            HL, GG = X("MO", m0 + 128, m0 + 136), X("MO", m0, m0 + 128)
            ts(HL, X("PA", 144, 152), -64.5 * WB, A.is_gt)
            if FSEND:
                send(X("ML", m0 + 128, m0 + 136), HL, "r4_%d_%d" % (b, t))
            step("df")
            cp(TB(8), IND(DD, FO), "act")
            mm([(X("PB", 128 * h, 128 + 128 * h), SEL[h], TB(8), True, True) for h in range(2)])
            cp(X("DF", 0, 256), X("PB", 0, 256), "act")
            step("dm")
            cp(GG, IND(X("DF", 0, CW), LW), "act")
            w = 128 if FSEND else 136
            send(X("ML", m0, m0 + w), X("MO", m0, m0 + w), "r0_%d_%d" % (b, t))
            step("future")
            XD = SF(64, 24)
            ts(SI(0), KEY, 16.0, A.add)
            ts(SI(40), SI(0), 4, A.arith_shift_right, 1023, A.bitwise_and)
            tt(SF(64), SI(8), Si, A.mult)
            tt(SF(72), SI(40), Si, A.subtract)
            spec = SPEC and not last
            if spec:
                cp(HB(32, 16), SF(64, 16), HQ)
                tt(HB(48, 16), SF(64, 16), HB(32, 16), A.subtract)
                mm([(X("PC", 0, 128, 1, 64, 96), HB(32, 32), I16, True, True)])
                cp(X("TH", 0, 128, 1, 64, 96), X("PC", 0, 128, 1, 64, 96), "act")
                mm([(X("PC", 128 + 128 * j, 256 + 128 * j), P(m, 0, 96), X("TH", 0, 128, 1, 0, 96), True, True) for j, m in enumerate((REN, REA))])
                act(TB(9, 256), X("PC", 128, 384), F.Identity, BIG - 2047.5)
                step("fmod")
                T96, o, o2 = X("TH", 0, 128, 1, 0, 96), X("PC", 0, 128), X("PC", 129, 384, 2)
                mm([(o, P(RED, 0, 96), T96, True, False), (o, NI16, TB(10), False, False), (o, I16, TB(9), False, True),
                    (o2, P(REN, 0, 96), T96, True, False), (o2, NI16, TB(9), False, True)])
                cp(X("ZB", 257, 512, 2), o, "act")
            step("base")
            mm([(X("PA", 288, 304), I16, HB(16 * y, 16), y == 0, False) for y in range(2)]
               + [(X("PA", 288, 296), I16y, HB(16 * y + 8, 8), False, y == 1) for y in range(2)]
               + [(X("PA", 304, 312), I16 if last else I16x, C(UF, 64, 72), True, True)])
            step("za")
            tt(X("ZB", 513, 768, 2), IND(AD, FO), ZY, A.subtract)
            act(X("PB", 257, 512, 2), Zi, F.Relu, -0.75)
            step("acts")
            MK = X("MK", CW * t, CW * t + CW)
            cp(IND(MK, LW), ONES)
            marks = lambda bank, a: mm([(X(bank, a, a + 256, 2, 64 * h, 64 * h + 64), J2, C(MK, 128 * h, 128 * h + 128), True, True) for h in range(2)])
            if spec:
                marks("PC", 128)
                scan(TF(6, 256), X("ZB", 256, 512), X("PC", 128, 384), A.mult, A.add)
                ts(X("EO", e0, e0 + 128), C(TF(6), 1, 256, 2), BIG, A.add)
                send(X("EU", e0 + 128, e0 + 256), X("EO", e0, e0 + 128), "r1_%d_%d" % (b, t))
            step("z")
            marks("PB", 256)
            scan(TF(2, 256), X("ZB", 512, 768), X("PB", 256, 512), A.mult, A.add)
            ts(X("SO", s0 + 24, s0 + 152) if spec and not ZSEND else X("ZO", e0, e0 + 128), C(TF(2), 1, 256, 2), ONE, A.add, -ONE, A.add)
            if ZSEND and not last:
                send(X("ZI", e0 + 128, e0 + 256), X("ZO", e0, e0 + 128), "r3_%d_%d" % (b, t))
            if last:
                for h in range(2):
                    dma("sp", R("yz", 128 * h, 128 * h + 128, 1, 64 * b, 64 * b + 64), X("ZO", e0, e0 + 128, 1, 64 * h, 64 * h + 64), 16, osem["sp"])
            if last:
                step("end")
                fill(SF(80), -1)
            step("state")
            w = 16 if last else 24
            mm([(X("PA", 256, 256 + w), I16, C(CA24, 0, w), True, False)]
               + [(X("PA", 256, 256 + w), C(MK, 128 * h, 128 * h + 128), C(AR[h], 0, w), False, h == 1) for h in range(2)]
               + [(X("PA", 272, 280), C(MK, 128 * h, 128 * h + 128), C(AR[h], 16, 24), h == 0, h == 1) for h in range(2) if last])
            tt(SF(96, 24), X("PA", 256, 280), XD, A.mult)
            tt(X("SO", s0, s0 + 24), X("PA", 288, 312), SF(96, 24), A.subtract)
            if spec:
                w = 24 if ZSEND else 152
                send(X("ST", n0, n0 + w), X("SO", s0, s0 + w), "r2_%d_%d" % (b, t))
            else:
                o = X("PC", 0, 128, 1, 0, 24)
                mm([(o, X("SO", s0, s0 + 24), I128, True, True)])
                act(P(TB(9), 0, 24), o, F.Identity, BIG - 2047.5)
                tt(P(TF(8), 0, 24), o, P(TB(9), 0, 24), A.subtract)
                act(P(TF(9), 0, 24), P(TF(8), 0, 24), F.Identity, BIG)
                for j, nme in enumerate(("yc", "ys", "ya")):
                    for h, q in enumerate(("sp", "act")):
                        dma(q, R(nme, 128 * h, 128 * h + 128, 1, 4 * b, 4 * b + 4), P(TF(9), 8 * j + 4 * h, 8 * j + 4 * h + 4), 2, osem[q])
            step("slot")
            GR, HR = X("ML", m0, m0 + 128), X("ML", m0 + 128, m0 + 136)
            o = X("PA" if last else SLB, 160, 176)
            mm([(o, I16, C16, True, False)] + [(C(o, y, 16, 2), LY[0][y], HL, False, False) for y in range(2)]
               + [(C(o, y, 16, 2), LY[1][y], HR, False, y == 1) for y in range(2)])
            SL = X("TU", 152, 168)
            ts(SL, o, PFc(ca), A.add)
            if not last:
                cp(X("WO", *blk), IND(X(CO, 0, 512), SL), "act")
            step("object")
            rows = (1, 64 * b, 64 * b + 64)
            if not last:
                o = X("PD", 256, 384)
                mm([(o, I16, Xo, True, False), (o, IH[0], GG, False, False), (o, IH[1], GR, False, True)])
                ts(Xn, o, 0.0, A.max, 255.0, A.min)
                spread(b, Xn, X(CV, 256, 512))
                cp(X("WV", *blk), IND(X(CV, 0, 512), SL), "act")
            else:
                o = X("PD", 256, 512)
                oy = lambda y, h: P(C(o, y, 256, 2), 64 * h, 64 * h + 64)
                step("own")
                mm([(oy(y, 0), C(SEL[y], 0, 64), Xo, True, True) for y in range(2)]
                   + [(oy(0, 1), C(SEL[0], 0, 64), Xo, True, False), (oy(0, 1), C(SEL[0], 0, 64), GG, False, True),
                      (oy(1, 1), C(SEL[1], 0, 64), Xo, True, False)])
                step("object")
                mm([(oy(1, 1), C(SEL[1], 0, 64), GR, False, True)])
                ts(X("W5", 256, 512), o, 0.0, A.max, 255.0, A.min)
                cp(X("W5", 512, 768), IND(X("W5", 0, 512), SL), "act")
                cp(X("YN", 0, 256), IND(X("N5", 0, 512), SL))
                dma("sp", R("yx", 0, 256, *rows), X("W5", 256, 512, 1, 64, 128), 32, osem["sp"])
                dma("act", R("yo", blk[0], blk[1], *rows), X("W5", 512, 768, 1, 0, 64), 32, osem["act"])
                dma("sp", R("yv", blk[0], blk[1], *rows), X("W5", 512, 768, 1, 64, 128), 32, osem["sp"])
                dma("sp", R("yn", blk[0], blk[1], 1, 4 * b, 4 * b + 4), X("YN", 0, 256, 1, 0, 64, 16), 4, osem["sp"])
            if t == VIS - 2:
                step("out")
                e = blk[1]
                for h, (w, y) in enumerate((("WO", "yo"), ("WV", "yv"))):
                    dma("g", R(y, 0, e, *rows), X(w, 0, e, 1, 0, 64), e // 8)
                    ops[dma("sp", X("DX", 0, 80, 1, 64 * h, 64 * h + 64), X(w, 0, e, 1, 0, 64, 16), 20)]["slack"] = 3.0
                act(X("DY", 0, 80), X("DX", 0, 80), F.Identity, -127.5)
                tt(X("DY", 80, 160), X("DX", 0, 80), X("DY", 0, 80), A.subtract)
                ts(X("DX", 80, 160), X("DY", 0, 80), 0.0, A.is_lt, 257.0, A.mult)
                act(X("DX", 160, 240), X("DY", 0, 80), F.Identity, -1.0, 1.0 / 256)
                tt(X("DX", 240, 320), X("DX", 80, 160), X("DX", 160, 240), A.add)
                for h, y in enumerate(("yo", "yv")):
                    dma("sp", R(y, 0, e, 1, 64 * b, 64 * b + 64, 16), X("DY", 80, 160, 1, 64 * h, 64 * h + 64), 10, osem["sp"])
                dma("sp", R("yn", 0, e, 1, 4 * b, 4 * b + 4), X("DX", 240, 320, 1, 0, 64), 20, osem["sp"])
    for a, e in zip(seq, seq[1:]):
        ops[e]["behind"] = a
    return ops


def overlap(a, b):
    if psum(a):
        return True
    if a[3] == b[3] > 1 and (a[1] - b[1]) % a[3]:
        return False
    return a[1] < b[2] and b[1] < a[2] and a[4] < b[5] and b[4] < a[5]


def plan(par=PAR):
    ops = build(par)
    n = len(ops)
    hist = {}
    dep = [set() for _ in ops]
    for i, o in enumerate(ops):
        acc = [(r, False) for r in o["reads"]] + [(r, True) for r in o["writes"]]
        for r, wr in acc:
            for (j, r2, w2) in hist.get(r[0], ()):
                if j != i and (wr or w2 or (psum(r) and ops[j]["eng"] != o["eng"])) and overlap(r, r2):
                    dep[i].add(j)
        for r, wr in acc:
            h = hist.setdefault(r[0], [])
            if wr and (psum(r) or (r[3] == 1 and r[6] == 1)):
                h[:] = [x for x in h if not (psum(r) or (r[1] <= x[1][1] and x[1][2] <= r[2] and r[4] <= x[1][4] and x[1][5] <= r[5]))]
            h.append((i, r, wr))
        if o["recv"]:
            dep[i] = set([o["after"]])
    succ = [[] for _ in ops]
    for i in range(n):
        for j in dep[i]:
            succ[j].append(i)
    behind = dict((o["behind"], i) for i, o in enumerate(ops) if "behind" in o)
    tail = [0.0] * n
    for i in range(n - 1, -1, -1):
        o = ops[i]
        tail[i] = o["dur"] + o["lat"] + o.get("kb", 0) * 0.006 + max([tail[j] + par["HOP"] for j in succ[i]] or [0.0])
    return ops, dep, succ, behind, tail


def arrange(ops, dep, succ, behind, tail, nudge, hop=PAR["HOP"]):
    n = len(ops)
    tail = [tail[i] + nudge.get(ops[i]["kind"], 0.0) + ops[i]["bias"] for i in range(n)]
    free = dict((e, 0.0) for e in ENG + ("none",))
    bus = [0.0]
    left = [len(d) + ("behind" in o) for d, o in zip(dep, ops)]
    ready = dict((e, {}) for e in free)
    for i in range(n):
        if not left[i]:
            ready[ops[i]["eng"]][i] = 0.0
    order, fin, start = [], [0.0] * n, [0.0] * n
    while len(order) < n:
        best = None
        for e in free:
            c = ready[e]
            if not c:
                continue
            t0 = max(free[e], min(c.values()))
            if best is None or t0 < best[0]:
                best = (t0, e)
        c = ready[best[1]]
        i = max((i for i in c if c[i] <= best[0] + LOOK), key=lambda i: (tail[i], -i))
        o = ops[i]
        t0 = max(free[o["eng"]], c.pop(i))
        start[i] = t0
        free[o["eng"]] = t0 + o["dur"]
        f = t0 + o["dur"] + o["lat"]
        if "kb" in o:
            bus[0] = max(bus[0], f) + o["kb"] * 0.006
            f = bus[0]
        fin[i] = f
        order.append(i)
        for j in succ[i] + ([behind[i]] if i in behind else []):
            left[j] -= 1
            if not left[j]:
                ready[ops[j]["eng"]][j] = max([fin[k] + (0.0 if ops[k]["eng"] == "pe" == ops[j]["eng"] or ops[j]["recv"] else hop) for k in dep[j]] + [t0])
    return ops, dep, order, start, fin


def ranked(key, pre, suc):
    left = [len(p) for p in pre]
    ready = sorted(((key[i], i) for i in range(len(pre)) if not left[i]), reverse=True)
    out = []
    while ready:
        i = ready.pop()[1]
        out.append(i)
        for j, _ in suc[i]:
            left[j] -= 1
            if not left[j]:
                ready.append((key[j], j))
        ready.sort(reverse=True)
    return out


def place(ops, seq, pre, back):
    busy, t = {}, [0.0] * len(ops)
    for j in seq:
        o = ops[j]
        d = o["dur"]
        if back:
            r = max([t[i] + ops[i]["dur"] + lag - d for i, lag in pre[j]] + [o["lat"] + o.get("kb", 0) * 0.006])
        else:
            r = max([t[i] + lag for i, lag in pre[j]] + [0.0])
        if d:
            q = busy.setdefault(o["eng"], [])
            k = len(q)
            while k and q[k - 1][1] > r:
                k -= 1
            while k < len(q) and q[k][0] < r + d - 1e-9:
                r = max(r, q[k][1])
                k += 1
            q.insert(k, (r, r + d))
        t[j] = r
    return t


def flip(pre):
    suc = [[] for _ in pre]
    for j, p in enumerate(pre):
        for i, lag in p:
            suc[i].append((j, lag))
    return suc


def lay(ops, dep, cycle, hop):
    n = len(ops)
    pre = [[(i, ops[i]["dur"] + ops[i]["lat"] + ops[i].get("slack", 0) + ops[i].get("kb", 0) * 0.006 + (0.0 if ops[i]["eng"] == "pe" == o["eng"] or o["recv"] else hop))
            for i in dep[j]] + ([(o["behind"], max(0.1, ops[o["behind"]]["kb"] * 0.006))] if "behind" in o else []) for j, o in enumerate(ops)]
    suc = flip(pre)
    rank = dict((w.split("/")[0], (int(w.split("/")[1]), a)) for x in cycle.values() for a, w in enumerate(x.split()))
    known = set(i for i, o in enumerate(ops) if o["t"] >= 0 and o["pos"] in rank and "behind" not in o and (o["t"] < VIS - 1 or o["kind"] not in ("state", "object", "slot", "old", "z")))
    queue = {}
    for i in known:
        o = ops[i]
        queue.setdefault(o["eng"], []).append((2 * o["t"] + o["b"] + rank[o["pos"]][0], rank[o["pos"]][1], i))
    known |= set(i for i, o in enumerate(ops) if o["recv"] and o["after"] in known)
    p2 = [[(j, lag) for j, lag in pre[i] if j in known] if i in known else [] for i in range(n)]
    for q in queue.values():
        q.sort()
        for a, b in zip(q, q[1:]):
            p2[b[2]].append((a[2], ops[a[2]]["dur"]))
    key = [None] * n
    for j in ranked(range(n), p2, flip(p2)):
        if j in known:
            key[j] = max([key[i] + lag for i, lag in p2[j]] + [0.0])
    for j in known:
        key[j] += AHEAD.get((ops[j]["t"], ops[j]["b"]), 0.0)
    for j in reversed(ranked(range(n), pre, suc)):
        if key[j] is None and (ops[j]["t"] <= 0 or "behind" in ops[j]):
            key[j] = min([key[i] - lag for i, lag in suc[j] if key[i] is not None] or [1e3]) + AHEAD.get(ops[j]["kind"], 0.0)
    for j in ranked(range(n), pre, suc):
        if key[j] is None:
            key[j] = max([key[i] + lag for i, lag in pre[j]] + [0.0]) + AHEAD.get(ops[j]["kind"], 0.0)
    t = place(ops, ranked(key, pre, suc), pre, False)
    for _ in range(PASSES):
        t = place(ops, ranked([-t[i] - o["dur"] for i, o in enumerate(ops)], suc, pre), suc, True)
        t = place(ops, ranked([-t[i] - o["dur"] for i, o in enumerate(ops)], pre, suc), pre, False)
    return ops, dep, ranked(t, pre, suc), t, [t[i] + o["dur"] + o["lat"] for i, o in enumerate(ops)]


AHEAD = {(5, 1): -5.5, (5, 0): 2.5, "nm0": -18.5, "nm1": -2.5, "logWO0": -5.0, "logWV0": -2.5, "logWV1": -11.0, "zero": -6.0, "E": -4.0,
         "old": -7.5, "out": -19.0, "own": -1.5, "object": -7.5, "slot": 8.0, "z": 20.0, "state": 30.5}
CYCLE = {
    "sp": "old.1/0 old.0/0",
    "act": "O1.0/0 O2.0/0 O3.0/0 name0.4/0 turn.0/0 future.4/1 object.3/2 name0.6/0 name1.4/0 df.0/1 turn.3/0 name1.6/0 future.7/1 "
           "object.4/2 claim.7/1 last0.1/0 future.9/1 zq.0/0 zq.1/1 df.2/1 last1.1/0 fmod.1/1 dm.0/1 za.1/1 abs1.0/0 abs0.0/0 abs2.0/0 "
           "slot.2/1 abs3.0/0",
    "dve": "O0.0/0 z.2/2 pick.0/1 mark.0/1 pick.1/1 future.0/1 mark.1/1 pick.2/1 future.1/1 future.2/1 mark.2/1 mark.3/1 mark.4/1 "
           "future.3/1 pick.4/1 mark.5/1 pick.5/1 turn.1/0 mark.6/1 future.5/1 claim.2/1 claim.3/1 claim.1/1 eq0.0/0 claim.6/1 eq1.0/0 "
           "last0.2/0 claim.9/1 flag.0/1 last0.3/0 acts.0/1 last0.4/0 last1.2/0 V1.0/0 acts.2/1 last1.3/0 state.1/1 acts.3/1 last1.4/0 "
           "V0.0/0 V2.0/0 slot.1/1 V3.0/0 za.0/1 state.2/1 object.1/1 z.1/1",
    "pe": "object.2/2 abs3.1/1 name0.0/0 name0.1/0 name0.2/0 name0.3/0 name1.0/0 pick.3/1 name1.1/0 name1.2/0 name0.5/0 name1.3/0 "
          "claim.0/1 turn.2/0 name0.7/0 name1.5/0 future.6/1 claim.4/1 claim.5/1 name1.7/0 last0.0/0 future.8/1 rows.0/0 claim.8/1 "
          "df.1/1 last1.0/0 fmod.0/1 base.0/1 state.0/1 acts.1/1 head.0/0 z.0/1 slot.0/1 object.0/1 abs2.1/0",
    "g": "z.3/2 flag.1/1 dm.1/1 acts.4/1 state.3/1"}
GRAPH = plan()
PLAN = lay(GRAPH[0], GRAPH[1], CYCLE, PAR["HOP"])


def rank_program(g, core, T, topo):
    rank = T.rank_of(core)
    if rank is None:
        return
    ops, dep, order = PLAN[:3]
    nxt = T.cores[(rank + 1) % len(T.cores)]
    prv = T.cores[(rank - 1) % len(T.cores)]
    rid, pid = topo.addr(nxt)[:2]
    mask = topo.mask(core, nxt)
    n_out, n_in = len(topo.engines(core, nxt)), len(topo.engines(prv, core))
    Q = {"g": g, "pe": g.tensor, "dve": g.vector, "act": g.scalar, "sp": g.sync}

    def ap(r):
        if not isinstance(r, tuple):
            return r
        if r[0] == "ind":
            return ap(r[1]).indirect(ap(r[2]))
        ps = slice(r[4], r[5], r[6]) if r[6] > 1 else slice(r[4], r[5])
        cs = slice(r[1], r[2], r[3]) if r[3] > 1 else slice(r[1], r[2])
        return T[r[0]][ps, cs]

    count, mark, know = {}, {}, {}
    seen = dict((e, {}) for e in ENG)
    for i in order:
        o = ops[i]
        if o["recv"]:
            mark[i], know[i] = (o["recv"], n_in), {o["recv"]: n_in}
            count[o["recv"]] = n_in
            continue
        e = o["eng"]
        q, kn = Q[e], seen[e]
        need = {}
        for j in dep[i]:
            if e == "pe" == ops[j]["eng"]:
                continue
            s, v = mark[j]
            if kn.get(s, 0) < v and need.get(s, (0, 0))[0] < v:
                need[s] = (v, j)
        for s, (v, j) in sorted(need.items(), key=lambda x: -x[1][1]):
            if kn.get(s, 0) < v:
                q.wait_ge(T.sem[s], v)
                for s2, v2 in know[j].items():
                    if kn.get(s2, 0) < v2:
                        kn[s2] = v2
        c = o["call"]
        k = c[0]
        sem, inc = "c_" + e, 1
        if k == "ts":
            if c[4] is None:
                ins = q.tensor_scalar(ap(c[1]), ap(c[2]), ap(c[3]), None, c[5])
            else:
                ins = q.tensor_scalar(ap(c[1]), ap(c[2]), ap(c[3]), ap(c[4]), c[5], c[6])
        elif k == "tt":
            ins = q.tensor_tensor(ap(c[1]), ap(c[2]), ap(c[3]), c[4])
        elif k == "cp":
            ins = q.tensor_copy(ap(c[1]), ap(c[2]))
        elif k == "act":
            ins = q.activation(ap(c[1]), ap(c[2]), c[3], bias=ap(c[4]), scale=ap(c[5]))
        elif k == "mm":
            for (x, l, r, st, sp) in c[1]:
                ins = q.matmul(ap(x), ap(l), ap(r), st, sp)
        elif k == "ms":
            ins = q.memset(ap(c[1]), c[2])
        elif k == "io":
            if SCRATCH[c[1][0]][2] == I3:
                ins = q.iota(ap(c[1]), c[2], c[3], c[4])
            else:
                ins = q.iota(ap(c[1]), c[2], c[3], c[4], allow_small_or_imprecise_dtypes=True)
        elif k == "as":
            ins = q.affine_select(ap(c[1]), ap(c[7]), c[2], c[3], c[4], c[5], c[6])
        elif k == "acc":
            ins = q.dma_start(ap(c[1]), ap(c[2]), accum_op=A.add, max_dma_last_dim=8192)
            sem, inc = o["sem"], 16
        elif k == "scan":
            ins = q.tensor_tensor_scan(ap(c[1]), ap(c[2]), ap(c[3]), 0.0, c[4], c[5])
        elif k == "dma":
            ins = q.dma_start(ap(c[1]), ap(c[2]))
            sem, inc = o["sem"], 16
        else:
            q.remote_dma(ap(c[1]), ap(c[2]), T.sem[c[3]], T.sem.sent, pid, rid, mask)
            ins, sem, inc = None, "sent", n_out
        if ins is not None:
            ins.then_inc(T.sem[sem], inc)
        count[sem] = count.get(sem, 0) + inc
        mark[i] = (sem, count[sem])
        know[i] = dict(kn)
        know[i][sem] = count[sem]
    for s in sorted(count):
        if seen["g"].get(s, 0) < count[s]:
            g.wait_ge(T.sem[s], count[s])
